import numpy as np
import ml_dtypes


def mxq(x, axis, fmt="e4m3"):
    dtype, down = {"e4m3": (ml_dtypes.float8_e4m3fn, 7), "e5m2": (ml_dtypes.float8_e5m2, 14)}[fmt]
    v = np.moveaxis(np.asarray(x, np.float32).astype(ml_dtypes.bfloat16).astype(np.float64), axis, -1)
    blocks = v.reshape(v.shape[:-1] + (-1, 32))
    amax = np.abs(blocks).max(-1, keepdims=True)
    byte = np.maximum(np.where(amax > 0, np.frexp(amax)[1] - 1 + 127, 0) - down, 1)
    scale = np.exp2(byte - 127.0)
    codes = (blocks / scale).astype(np.float32).astype(dtype).astype(np.float64)
    return np.moveaxis((codes * scale).reshape(v.shape), -1, axis)


WIDE = False


def mx_kscale(k):
    if not WIDE:
        return np.ones(k)
    levels = np.array([10, -10, 5, -5, 0])
    if k % 512:
        return np.exp2(np.random.permutation(np.resize(levels, k // 32))).repeat(32)
    a = np.empty((k // 512, 16))
    for p in range(k // 512):
        a[p, :8] = np.random.permutation(np.resize(levels, 8))
        for g in range(8):
            far = levels[np.abs(levels - a[p, g]) >= 10]
            a[p, g + 8] = far[np.random.randint(len(far))]
    return np.exp2(a.ravel()).repeat(32)


def f64(x):
    return np.asarray(x).astype(np.float64)


def striped(idx):
    return np.tile(idx.reshape(-1, 16).T, (8, 1)).astype(np.uint16)


def unstriped(offs):
    return offs[:16].T.reshape(-1).astype(np.int64)


def pack_weight(w):
    k, n = w.shape
    w = f64(np.asarray(w, np.float32).astype(ml_dtypes.bfloat16)).reshape(k // 32, 32, n)
    amax = np.abs(w).max(1)
    byte = np.clip(np.where(amax > 0, np.frexp(amax)[1] - 1 + 127 - 7, 1), 1, 254)
    scaled = (w * np.exp2(127.0 - byte)[:, None, :]).reshape(k, n).astype(np.float32)
    words = np.ascontiguousarray(scaled.reshape(k // 512, 128, 4, n).transpose(0, 1, 3, 2)).astype(ml_dtypes.float8_e4m3fn).view(np.uint8)
    return words, np.ascontiguousarray(byte.astype(np.uint8).reshape(k // 512, 16, n))


def unpack_weight(words, scales):
    g, p, n, _ = words.shape
    vals = np.ascontiguousarray(words).view(ml_dtypes.float8_e4m3fn).astype(np.float64) * np.repeat(np.exp2(scales.astype(np.float64) - 127.0), 8, axis=1)[..., None]
    return vals.transpose(0, 1, 3, 2).reshape(g * 512, n)


def sigmoid(v):
    return 1.0 / (1.0 + np.exp(-np.maximum(v, -700.0)))


K, T, S, V, H, N = 1024, 1024, 512, 256, 512, 128


def setup_inputs():
    n = np.random.standard_normal
    s = mx_kscale(K)[:, None]
    u = mx_kscale(H)
    near = np.random.permutation(S)
    packed_xT = pack_weight(n((K, T)) * s)
    return {
        "x_words": packed_xT[0],
        "x_scales": packed_xT[1],
        "w1": (n((K, H)) / np.sqrt(K) / s).astype(np.float32),
        "w2": (n((K, H)) / np.sqrt(K) / s * u).astype(np.float32),
        "w3": (n((K, H)) / np.sqrt(K) / s).astype(np.float32),
        "w4": (n((H, N)) / np.sqrt(H) / u[:, None]).astype(np.float32),
        "w5": (n((K, N)) / np.sqrt(K) / s).astype(np.float32),
        "offs": striped(np.random.permutation(T)[:S]),
        "pos1": striped(near[:V]),
        "pos2": striped(near[V:]),
        "nxt1": striped(np.random.permutation(S)[:V]),
        "nxt2": striped(np.random.permutation(S)[:V]),
        "own": striped(np.random.permutation(S)[:V]),
    }


def reference(x_words, x_scales, w1, w2, w3, w4, w5, offs, pos1, pos2, nxt1, nxt2, own):
    xq = unpack_weight(x_words, x_scales)[:, unstriped(offs)]
    gg = sigmoid(mxq(f64(w5), 0, "e4m3").T @ xq)
    y = mxq(f64(w2), 0, "e4m3").T @ xq
    a = (sigmoid(mxq(f64(w1), 0, "e4m3").T @ xq)) * y
    ap0 = a[:, unstriped(pos1)]
    ee = mxq(f64(w3), 0, "e4m3").T @ xq
    ap1 = a[:, unstriped(pos2)]
    z = ap0 * ee[:, unstriped(nxt1)] + ap1 * ee[:, unstriped(nxt2)]
    rr = mxq(f64(w4), 0, "e4m3").T @ mxq(z, 0, "e4m3")
    return gg[:, unstriped(own)] * rr

@@ -1,0 +1,221 @@
+from contextlib import ExitStack
+
+import concourse.mybir as mybir
+
+K, T, S, V, H, N = 1024, 1024, 512, 256, 512, 128
+FLOPS = 2 * K * S * (3 * H + N) + 2 * H * N * V
+
+F32 = mybir.dt.float32
+BF16 = mybir.dt.bfloat16
+I32 = mybir.dt.int32
+U32 = mybir.dt.uint32
+U16 = mybir.dt.uint16
+U8 = mybir.dt.uint8
+FP8X4 = mybir.dt.float8_e4m3fn_x4
+MULT = mybir.AluOpType.mult
+ADD = mybir.AluOpType.add
+SIGMOID = mybir.ActivationFunctionType.Sigmoid
+
+P = 128
+PACK = 4
+K_PASS = P * PACK
+PASSES = K // K_PASS
+TILES = H // P
+
+
+def tile_picked_ytri_gated_p_kernel(
+    tc, x_words, x_scales, w1, w2, w3, w4, w5, offs, pos1, pos2, nxt1, nxt2, own, out
+):
+    nc = tc.nc
+    with ExitStack() as ctx:
+        keep = ctx.enter_context(tc.tile_pool(name="keep", bufs=1))
+        banks = ctx.enter_context(tc.psum_pool(name="banks", bufs=8))
+
+        def load_list(dram, name):
+            tile = keep.tile(list(dram.shape), U16, name=name)
+            nc.sync.dma_start(out=tile[:], in_=dram)
+            return tile
+
+        def load_weight(w, g, c0, c1, name):
+            raw = keep.tile([P, PACK, c1 - c0], F32, name=name)
+            rows = w[g * K_PASS : (g + 1) * K_PASS, :].rearrange("(p j) c -> p j c", j=PACK)
+            nc.sync.dma_start(out=raw[:], in_=rows[:, :, c0:c1])
+            return raw
+
+        def load_words(g):
+            tile = keep.tile([P, T], U32, name="x_all_words%d" % g)
+            nc.sync.dma_start(out=tile[:].bitcast(I32), in_=x_words[g].rearrange("p n t -> p (n t)").bitcast(I32))
+            return tile
+
+        def copy_on(engine, dst, src):
+            if engine == "vector":
+                nc.vector.tensor_copy(out=dst, in_=src)
+            else:
+                nc.scalar.copy(out=dst, in_=src)
+
+        def quantize(values, width, name):
+            codes = keep.tile([P, width], U32, name=name + "_codes", align_bytes=64)
+            scales = keep.tile([P, width], U8, name=name + "_scales", align_bytes=64)
+            nc.vector.quantize_mx(out=codes[:].bitcast(FP8X4), scales=scales[:], in_=values)
+            return codes, scales
+
+        x_all_scales = keep.tile([P, T], U8, name="x_all_scales")
+        nc.gpsimd.memset(x_all_scales[:].bitcast(I32), 0)
+        for q in range(4):
+            nc.sync.dma_start(
+                out=x_all_scales[32 * q : 32 * q + 4 * PASSES, :].bitcast(I32),
+                in_=x_scales[:, 4 * q : 4 * q + 4, :].bitcast(I32),
+            )
+        warm = keep.tile([P, 1], F32, name="warm")
+        nc.vector.memset(warm[:], 0.0)
+        warm_out = keep.tile([P, 1], F32, name="warm_out")
+        nc.scalar.activation(out=warm_out[:], in_=warm[:], func=SIGMOID)
+
+        offs_t = load_list(offs, "offs_t")
+        x_all = [load_words(0)]
+        w1_raw = [load_weight(w1, 0, 0, H, "w1_raw0")]
+        x_all.append(load_words(1))
+        w1_raw.append(load_weight(w1, 1, 0, H, "w1_raw1"))
+        w2_raw0 = load_weight(w2, 0, 0, H, "w2_raw0")
+        w2_raw1 = [load_weight(w2, 1, c0, c0 + H // 2, "w2_raw1_%d" % c0) for c0 in (0, H // 2)]
+        pos_t = [load_list(pos1, "pos1_t"), load_list(pos2, "pos2_t")]
+        w3_raw = [load_weight(w3, g, 0, H, "w3_raw%d" % g) for g in range(PASSES)]
+        nxt_t = [load_list(nxt1, "nxt1_t"), load_list(nxt2, "nxt2_t")]
+        w5_raw = keep.tile([P, PASSES, PACK, N], F32, name="w5_raw")
+        nc.sync.dma_start(
+            out=w5_raw[:].rearrange("p g j c -> p g (j c)"), in_=w5.rearrange("(g p j) c -> p g (j c)", g=PASSES, j=PACK)
+        )
+        w4_raw = load_weight(w4, 0, 0, N, "w4_raw")
+        own_t = load_list(own, "own_t")
+
+        x_scale = keep.tile([P, S], U8, name="x_scale", align_bytes=64)
+        x_codes = [keep.tile([P, S], U32, name="x_codes%d" % g, align_bytes=64) for g in range(PASSES)]
+
+        def gather_words(g):
+            nc.vector.tensor_copy(out=x_codes[g][:], in_=x_all[g][:].indirect(offs_t[:]))
+
+        def pair_tile(name):
+            return keep.tile([P, 2, P, PACK], BF16, name=name, align_bytes=64)
+
+        def round_pair(engine, grouped, raw, pair, m0=0):
+            count = raw.shape[2] // TILES
+            src = raw[:].rearrange("p j (m t) -> p m j t", t=TILES)[:, :, :, 2 * pair : 2 * pair + 2]
+            dst = grouped[:].rearrange("p e m j -> p m j e")[:, m0 : m0 + count, :, :]
+            copy_on(engine, dst, src)
+
+        def quantize_pair(grouped, name):
+            return quantize(grouped[:].rearrange("p e m j -> p (e m j)"), 2 * P, name)
+
+        def prepare(engine, raw, pair, name):
+            grouped = pair_tile(name + "_bf16")
+            round_pair(engine, grouped, raw, pair)
+            return quantize_pair(grouped, name)
+
+        def one_pass(acc, quantized, column, g):
+            codes, scales = quantized
+            nc.tensor.matmul_mx(
+                out=acc[:],
+                lhsT=codes[:, column : column + P].bitcast(FP8X4),
+                lhsT_scale=scales[:, column : column + P],
+                rhs=x_codes[g][:].bitcast(FP8X4),
+                rhs_scale=x_scale[4 * g :, :],
+                start=(g == 0),
+                stop=(g == PASSES - 1),
+            )
+
+        def passes(accs, pairs, g):
+            for t in range(TILES):
+                one_pass(accs[t], pairs[t // 2], (t % 2) * P, g)
+
+        def new_banks(name):
+            return [banks.tile([P, S], F32, name="%s%d" % (name, t), tag="acc") for t in range(TILES)]
+
+        nc.vector.tensor_copy(out=x_scale[:], in_=x_all_scales[:].indirect(offs_t[:]))
+        gather_words(0)
+        w1_q0 = [prepare("scalar", w1_raw[0], 0, "w1_00"), prepare("vector", w1_raw[0], 1, "w1_01")]
+        gather_words(1)
+        gate_acc = new_banks("gate_acc")
+        passes(gate_acc, w1_q0, 0)
+        w1_q1 = [prepare("vector", w1_raw[1], 0, "w1_10"), prepare("scalar", w1_raw[1], 1, "w1_11")]
+        passes(gate_acc, w1_q1, 1)
+        w2_q0 = [prepare("vector", w2_raw0, 0, "w2_00"), prepare("scalar", w2_raw0, 1, "w2_01")]
+        y_acc = new_banks("y_acc")
+        passes(y_acc, w2_q0, 0)
+        gate = [keep.tile([P, S], F32, name="gate%d" % t) for t in range(TILES)]
+        for t in (0, 1):
+            nc.scalar.activation(out=gate[t][:], in_=gate_acc[t][:], func=SIGMOID)
+        grouped = [pair_tile("w2_1%d_bf16" % pair) for pair in range(2)]
+        w2_q1 = []
+        for half in range(2):
+            for pair, engine in enumerate(("vector", "scalar")):
+                round_pair(engine, grouped[pair], w2_raw1[half], pair, half * P // 2)
+                if half == 1:
+                    w2_q1.append(quantize_pair(grouped[pair], "w2_1%d" % pair))
+        passes(y_acc, w2_q1, 1)
+        for t in (2, 3):
+            nc.scalar.activation(out=gate[t][:], in_=gate_acc[t][:], func=SIGMOID)
+        a = [keep.tile([P, S], F32, name="a%d" % t) for t in range(TILES)]
+        for t in range(TILES):
+            nc.vector.tensor_tensor(out=a[t][:], in0=y_acc[t][:], in1=gate[t][:], op=MULT)
+
+        e_acc = new_banks("e_acc")
+        for g in range(PASSES):
+            passes(e_acc, [prepare("scalar", w3_raw[g], pair, "w3_%d%d" % (g, pair)) for pair in range(2)], g)
+        ee = [keep.tile([P, S], F32, name="ee%d" % t) for t in range(TILES)]
+        for t in range(TILES):
+            nc.scalar.copy(out=ee[t][:], in_=e_acc[t][:])
+
+        w5_bf16 = keep.tile([P, PASSES, N, PACK], BF16, name="w5_bf16", align_bytes=64)
+        nc.scalar.copy(
+            out=w5_bf16[:].rearrange("p g (c i) j -> p g c j i", i=4),
+            in_=w5_raw[:].rearrange("p g j (c i) -> p g c j i", i=4),
+        )
+        w5_q = quantize(w5_bf16[:].rearrange("p g c j -> p (g c j)"), PASSES * N, "w5")
+        g_acc = banks.tile([P, S], F32, name="g_acc", tag="acc")
+        for g in range(PASSES):
+            one_pass(g_acc, w5_q, g * N, g)
+        gg = keep.tile([P, S], F32, name="gg")
+        nc.scalar.activation(out=gg[:], in_=g_acc[:], func=SIGMOID)
+        w4_bf16 = keep.tile([P, N, PACK], BF16, name="w4_bf16", align_bytes=64)
+        nc.scalar.copy(
+            out=w4_bf16[:].rearrange("p (c i) j -> p c j i", i=4), in_=w4_raw[:].rearrange("p j (c i) -> p c j i", i=4)
+        )
+        w4_codes, w4_scales = quantize(w4_bf16[:].rearrange("p c j -> p (c j)"), N, "w4")
+
+        picked_a = {}
+        for t in range(TILES):
+            for d in range(2):
+                picked_a[t, d] = keep.tile([P, V], F32, name="picked_a%d%d" % (t, d))
+                nc.vector.tensor_copy(out=picked_a[t, d][:], in_=a[t][:].indirect(pos_t[d][:]))
+        terms = [keep.tile([P, TILES, V], F32, name="term%d" % d) for d in range(2)]
+        for t in range(TILES):
+            for d in range(2):
+                nc.vector.tensor_tensor(
+                    out=terms[d][:, t, :], in0=ee[t][:].indirect(nxt_t[d][:]), in1=picked_a[t, d][:], op=MULT
+                )
+
+        halves = [slice(0, V // 2), slice(V // 2, V)]
+        z = []
+        for h, cols in enumerate(halves):
+            z.append(keep.tile([P, V // 2, PACK], BF16, name="z%d" % h, align_bytes=64))
+            in0, in1 = (term[:, :, cols].rearrange("p t (c i) -> p c t i", i=4) for term in terms)
+            nc.vector.tensor_tensor(out=z[h][:].rearrange("p (c i) t -> p c t i", i=4), in0=in0, in1=in1, op=ADD)
+        rr = []
+        for h in range(2):
+            z_codes, z_scales = quantize(z[h][:].rearrange("p v t -> p (v t)"), V // 2, "z%d" % h)
+            rr.append(banks.tile([P, V // 2], F32, name="rr%d" % h, tag="acc"))
+            nc.tensor.matmul_mx(
+                out=rr[h][:],
+                lhsT=w4_codes[:].bitcast(FP8X4),
+                lhsT_scale=w4_scales[:],
+                rhs=z_codes[:].bitcast(FP8X4),
+                rhs_scale=z_scales[:],
+                start=True,
+                stop=True,
+            )
+        picked_g = keep.tile([P, V], F32, name="picked_g")
+        nc.vector.tensor_copy(out=picked_g[:], in_=gg[:].indirect(own_t[:]))
+        for h, cols in enumerate(halves):
+            result = keep.tile([P, V // 2], F32, name="result%d" % h)
+            nc.vector.tensor_tensor(out=result[:], in0=rr[h][:], in1=picked_g[:, cols], op=MULT)
+            nc.sync.dma_start(out=out[:, cols], in_=result[:])

@@ -61,6 +61,8 @@ def tile_picked_ytri_gated_p_kernel(
 
         x_all_scales = keep.tile([P, T], U8, name="x_all_scales")
         nc.gpsimd.memset(x_all_scales[:].bitcast(I32), 0)
+        x_all = [load_words(0)]
+        offs_t = load_list(offs, "offs_t")
         for q in range(4):
             nc.sync.dma_start(
                 out=x_all_scales[32 * q : 32 * q + 4 * PASSES, :].bitcast(I32),
@@ -71,21 +73,21 @@ def tile_picked_ytri_gated_p_kernel(
         warm_out = keep.tile([P, 1], F32, name="warm_out")
         nc.scalar.activation(out=warm_out[:], in_=warm[:], func=SIGMOID)
 
-        offs_t = load_list(offs, "offs_t")
-        x_all = [load_words(0)]
-        w1_raw = [load_weight(w1, 0, 0, H, "w1_raw0")]
         x_all.append(load_words(1))
-        w1_raw.append(load_weight(w1, 1, 0, H, "w1_raw1"))
+        w1_raw = [load_weight(w1, 0, 0, H, "w1_raw0")]
         w2_raw0 = load_weight(w2, 0, 0, H, "w2_raw0")
+        w1_raw.append(load_weight(w1, 1, 0, H, "w1_raw1"))
         w2_raw1 = [load_weight(w2, 1, c0, c0 + H // 2, "w2_raw1_%d" % c0) for c0 in (0, H // 2)]
-        pos_t = [load_list(pos1, "pos1_t"), load_list(pos2, "pos2_t")]
-        w3_raw = [load_weight(w3, g, 0, H, "w3_raw%d" % g) for g in range(PASSES)]
-        nxt_t = [load_list(nxt1, "nxt1_t"), load_list(nxt2, "nxt2_t")]
+        w3_raw = [load_weight(w3, 0, 0, H, "w3_raw0")]
+        pos_t = [load_list(pos1, "pos1_t")]
+        w3_raw.append(load_weight(w3, 1, 0, H, "w3_raw1"))
         w5_raw = keep.tile([P, PASSES, PACK, N], F32, name="w5_raw")
         nc.sync.dma_start(
             out=w5_raw[:].rearrange("p g j c -> p g (j c)"), in_=w5.rearrange("(g p j) c -> p g (j c)", g=PASSES, j=PACK)
         )
+        pos_t.append(load_list(pos2, "pos2_t"))
         w4_raw = load_weight(w4, 0, 0, N, "w4_raw")
+        nxt_t = [load_list(nxt1, "nxt1_t"), load_list(nxt2, "nxt2_t")]
         own_t = load_list(own, "own_t")
 
         x_scale = keep.tile([P, S], U8, name="x_scale", align_bytes=64)
@@ -130,57 +132,56 @@ def tile_picked_ytri_gated_p_kernel(
         def new_banks(name):
             return [banks.tile([P, S], F32, name="%s%d" % (name, t), tag="acc") for t in range(TILES)]
 
-        nc.vector.tensor_copy(out=x_scale[:], in_=x_all_scales[:].indirect(offs_t[:]))
         gather_words(0)
-        w1_q0 = [prepare("scalar", w1_raw[0], 0, "w1_00"), prepare("vector", w1_raw[0], 1, "w1_01")]
+        nc.vector.tensor_copy(out=x_scale[:], in_=x_all_scales[:].indirect(offs_t[:]))
         gather_words(1)
+
+        def prepare_pass(raw, name):
+            return [prepare(engine, raw, pair, "%s%d" % (name, pair)) for pair, engine in enumerate(("vector", "scalar"))]
+
         gate_acc = new_banks("gate_acc")
-        passes(gate_acc, w1_q0, 0)
-        w1_q1 = [prepare("vector", w1_raw[1], 0, "w1_10"), prepare("scalar", w1_raw[1], 1, "w1_11")]
-        passes(gate_acc, w1_q1, 1)
-        w2_q0 = [prepare("vector", w2_raw0, 0, "w2_00"), prepare("scalar", w2_raw0, 1, "w2_01")]
         y_acc = new_banks("y_acc")
-        passes(y_acc, w2_q0, 0)
-        gate = [keep.tile([P, S], F32, name="gate%d" % t) for t in range(TILES)]
-        for t in (0, 1):
-            nc.scalar.activation(out=gate[t][:], in_=gate_acc[t][:], func=SIGMOID)
+        passes(gate_acc, prepare_pass(w1_raw[0], "w1_0"), 0)
+        passes(y_acc, prepare_pass(w2_raw0, "w2_0"), 0)
+        passes(gate_acc, prepare_pass(w1_raw[1], "w1_1"), 1)
         grouped = [pair_tile("w2_1%d_bf16" % pair) for pair in range(2)]
-        w2_q1 = []
         for half in range(2):
-            for pair, engine in enumerate(("vector", "scalar")):
-                round_pair(engine, grouped[pair], w2_raw1[half], pair, half * P // 2)
-                if half == 1:
-                    w2_q1.append(quantize_pair(grouped[pair], "w2_1%d" % pair))
-        passes(y_acc, w2_q1, 1)
-        for t in (2, 3):
+            for pair in range(2):
+                round_pair("vector", grouped[pair], w2_raw1[half], pair, half * P // 2)
+        passes(y_acc, [quantize_pair(grouped[pair], "w2_1%d" % pair) for pair in range(2)], 1)
+        gate = [keep.tile([P, S], F32, name="gate%d" % t) for t in range(TILES)]
+        for t in range(TILES):
             nc.scalar.activation(out=gate[t][:], in_=gate_acc[t][:], func=SIGMOID)
         a = [keep.tile([P, S], F32, name="a%d" % t) for t in range(TILES)]
         for t in range(TILES):
             nc.vector.tensor_tensor(out=a[t][:], in0=y_acc[t][:], in1=gate[t][:], op=MULT)
 
         e_acc = new_banks("e_acc")
+        w3_q = []
         for g in range(PASSES):
-            passes(e_acc, [prepare("scalar", w3_raw[g], pair, "w3_%d%d" % (g, pair)) for pair in range(2)], g)
-        ee = [keep.tile([P, S], F32, name="ee%d" % t) for t in range(TILES)]
-        for t in range(TILES):
-            nc.scalar.copy(out=ee[t][:], in_=e_acc[t][:])
-
+            w3_q.append([prepare("scalar", w3_raw[g], pair, "w3_%d%d" % (g, pair)) for pair in range(2)])
+            if g == 0:
+                passes(e_acc, w3_q[0], 0)
         w5_bf16 = keep.tile([P, PASSES, N, PACK], BF16, name="w5_bf16", align_bytes=64)
         nc.scalar.copy(
             out=w5_bf16[:].rearrange("p g (c i) j -> p g c j i", i=4),
             in_=w5_raw[:].rearrange("p g j (c i) -> p g c j i", i=4),
         )
         w5_q = quantize(w5_bf16[:].rearrange("p g c j -> p (g c j)"), PASSES * N, "w5")
-        g_acc = banks.tile([P, S], F32, name="g_acc", tag="acc")
-        for g in range(PASSES):
-            one_pass(g_acc, w5_q, g * N, g)
-        gg = keep.tile([P, S], F32, name="gg")
-        nc.scalar.activation(out=gg[:], in_=g_acc[:], func=SIGMOID)
         w4_bf16 = keep.tile([P, N, PACK], BF16, name="w4_bf16", align_bytes=64)
         nc.scalar.copy(
             out=w4_bf16[:].rearrange("p (c i) j -> p c j i", i=4), in_=w4_raw[:].rearrange("p j (c i) -> p c j i", i=4)
         )
         w4_codes, w4_scales = quantize(w4_bf16[:].rearrange("p c j -> p (c j)"), N, "w4")
+        passes(e_acc, w3_q[1], 1)
+        ee = [keep.tile([P, S], F32, name="ee%d" % t) for t in range(TILES)]
+        for t in range(TILES):
+            nc.scalar.copy(out=ee[t][:], in_=e_acc[t][:])
+        g_acc = banks.tile([P, S], F32, name="g_acc", tag="acc")
+        for g in range(PASSES):
+            one_pass(g_acc, w5_q, g * N, g)
+        gg = keep.tile([P, S], F32, name="gg")
+        nc.scalar.activation(out=gg[:], in_=g_acc[:], func=SIGMOID)
 
         picked_a = {}
         for t in range(TILES):
@@ -197,7 +198,7 @@ def tile_picked_ytri_gated_p_kernel(
         halves = [slice(0, V // 2), slice(V // 2, V)]
         z = []
         for h, cols in enumerate(halves):
-            z.append(keep.tile([P, V // 2, PACK], BF16, name="z%d" % h, align_bytes=64))
+            z.append(keep.tile([P, V // 2, PACK], BF16, name="z%d" % h, tag="z%d" % h, align_bytes=64))
             in0, in1 = (term[:, :, cols].rearrange("p t (c i) -> p c t i", i=4) for term in terms)
             nc.vector.tensor_tensor(out=z[h][:].rearrange("p (c i) t -> p c t i", i=4), in0=in0, in1=in1, op=ADD)
         rr = []
@@ -213,7 +214,7 @@ def tile_picked_ytri_gated_p_kernel(
                 start=True,
                 stop=True,
             )
-        picked_g = keep.tile([P, V], F32, name="picked_g")
+        picked_g = keep.tile([P, V], F32, name="picked_g", tag="z0", align_bytes=64)
         nc.vector.tensor_copy(out=picked_g[:], in_=gg[:].indirect(own_t[:]))
         for h, cols in enumerate(halves):
             result = keep.tile([P, V // 2], F32, name="result%d" % h)

@@ -1,6 +1,7 @@
 from contextlib import ExitStack
 
 import concourse.mybir as mybir
+from concourse.masks import make_identity
 
 K, T, S, V, H, N = 1024, 1024, 512, 256, 512, 128
 FLOPS = 2 * K * S * (3 * H + N) + 2 * H * N * V
@@ -21,6 +22,7 @@ PACK = 4
 K_PASS = P * PACK
 PASSES = K // K_PASS
 TILES = H // P
+HALF = H // 2
 
 
 def tile_picked_ytri_gated_p_kernel(
@@ -29,35 +31,52 @@ def tile_picked_ytri_gated_p_kernel(
     nc = tc.nc
     with ExitStack() as ctx:
         keep = ctx.enter_context(tc.tile_pool(name="keep", bufs=1))
-        banks = ctx.enter_context(tc.psum_pool(name="banks", bufs=8))
+        psum = ctx.enter_context(tc.psum_pool(name="psum", bufs=1))
+        banks = [psum.tile([P, S], F32, name="bank%d" % i) for i in range(8)]
 
         def load_list(dram, name):
             tile = keep.tile(list(dram.shape), U16, name=name)
             nc.sync.dma_start(out=tile[:], in_=dram)
             return tile
 
-        def load_weight(w, g, c0, c1, name):
-            raw = keep.tile([P, PACK, c1 - c0], F32, name=name)
+        raw = {}
+
+        def load_weight(w, name, g, t0, t1):
+            tile = keep.tile([P, PACK, (t1 - t0) * P], F32, name="%s_raw%d%d" % (name, t0, g))
             rows = w[g * K_PASS : (g + 1) * K_PASS, :].rearrange("(p j) c -> p j c", j=PACK)
-            nc.sync.dma_start(out=raw[:], in_=rows[:, :, c0:c1])
-            return raw
+            nc.sync.dma_start(out=tile[:], in_=rows[:, :, t0 * P : t1 * P])
+            raw[name, t0, g] = tile
 
         def load_words(g):
             tile = keep.tile([P, T], U32, name="x_all_words%d" % g)
             nc.sync.dma_start(out=tile[:].bitcast(I32), in_=x_words[g].rearrange("p n t -> p (n t)").bitcast(I32))
             return tile
 
-        def copy_on(engine, dst, src):
+        rounded, quantized = {}, {}
+
+        def round_on(engine, key):
+            tile = raw[key]
+            grouped = keep.tile([P, tile.shape[2], PACK], BF16, name="%s_%d%d_bf16" % key, align_bytes=64)
+            dst = grouped[:].rearrange("p (c i) j -> p c j i", i=4)
+            src = tile[:].rearrange("p j (c i) -> p c j i", i=4)
             if engine == "vector":
                 nc.vector.tensor_copy(out=dst, in_=src)
+            elif engine == "gpsimd":
+                nc.gpsimd.tensor_copy(out=dst, in_=src)
             else:
                 nc.scalar.copy(out=dst, in_=src)
+            rounded[key] = grouped[:].rearrange("p c j -> p (c j)")
 
-        def quantize(values, width, name):
+        def quantize(values, name):
+            width = values.shape[1] // PACK
             codes = keep.tile([P, width], U32, name=name + "_codes", align_bytes=64)
             scales = keep.tile([P, width], U8, name=name + "_scales", align_bytes=64)
             nc.vector.quantize_mx(out=codes[:].bitcast(FP8X4), scales=scales[:], in_=values)
             return codes, scales
+
+        def prepare(engine, key):
+            round_on(engine, key)
+            quantized[key] = quantize(rounded[key], "%s_%d%d" % key)
 
         x_all_scales = keep.tile([P, T], U8, name="x_all_scales")
         nc.gpsimd.memset(x_all_scales[:].bitcast(I32), 0)
@@ -68,145 +87,191 @@ def tile_picked_ytri_gated_p_kernel(
                 out=x_all_scales[32 * q : 32 * q + 4 * PASSES, :].bitcast(I32),
                 in_=x_scales[:, 4 * q : 4 * q + 4, :].bitcast(I32),
             )
+        load_weight(w3, "w3", 0, 0, 1)
+        x_all.append(load_words(1))
         warm = keep.tile([P, 1], F32, name="warm")
         nc.vector.memset(warm[:], 0.0)
         warm_out = keep.tile([P, 1], F32, name="warm_out")
         nc.scalar.activation(out=warm_out[:], in_=warm[:], func=SIGMOID)
+        identity = keep.tile([P, P], F32, name="identity")
+        make_identity(nc, identity[:])
 
-        x_all.append(load_words(1))
-        w1_raw = [load_weight(w1, 0, 0, H, "w1_raw0")]
-        w2_raw0 = load_weight(w2, 0, 0, H, "w2_raw0")
-        w1_raw.append(load_weight(w1, 1, 0, H, "w1_raw1"))
-        w2_raw1 = [load_weight(w2, 1, c0, c0 + H // 2, "w2_raw1_%d" % c0) for c0 in (0, H // 2)]
-        w3_raw = [load_weight(w3, 0, 0, H, "w3_raw0")]
-        pos_t = [load_list(pos1, "pos1_t")]
-        w3_raw.append(load_weight(w3, 1, 0, H, "w3_raw1"))
-        w5_raw = keep.tile([P, PASSES, PACK, N], F32, name="w5_raw")
-        nc.sync.dma_start(
-            out=w5_raw[:].rearrange("p g j c -> p g (j c)"), in_=w5.rearrange("(g p j) c -> p g (j c)", g=PASSES, j=PACK)
-        )
-        pos_t.append(load_list(pos2, "pos2_t"))
-        w4_raw = load_weight(w4, 0, 0, N, "w4_raw")
+        load_weight(w3, "w3", 1, 0, 1)
+        for g in range(PASSES):
+            load_weight(w3, "w3", g, 1, 2)
         nxt_t = [load_list(nxt1, "nxt1_t"), load_list(nxt2, "nxt2_t")]
+        for w, name in ((w1, "w1"), (w2, "w2")):
+            for g in range(PASSES):
+                load_weight(w, name, g, 0, 2)
+        pos_t = [load_list(pos1, "pos1_t")]
+        load_weight(w1, "w1", 0, 2, 4)
+        pos_t.append(load_list(pos2, "pos2_t"))
+        load_weight(w2, "w2", 0, 2, 4)
+        load_weight(w1, "w1", 1, 2, 4)
+        load_weight(w2, "w2", 1, 2, 4)
+        load_weight(w3, "w3", 0, 2, 4)
         own_t = load_list(own, "own_t")
+        load_weight(w3, "w3", 1, 2, 4)
+        for g in range(PASSES):
+            load_weight(w5, "w5", g, 0, 1)
+        load_weight(w4, "w4", 0, 0, 1)
 
         x_scale = keep.tile([P, S], U8, name="x_scale", align_bytes=64)
         x_codes = [keep.tile([P, S], U32, name="x_codes%d" % g, align_bytes=64) for g in range(PASSES)]
+        nc.vector.tensor_copy(out=x_codes[0][:], in_=x_all[0][:].indirect(offs_t[:]))
+        nc.vector.tensor_copy(out=x_scale[:], in_=x_all_scales[:].indirect(offs_t[:]))
 
-        def gather_words(g):
-            nc.vector.tensor_copy(out=x_codes[g][:], in_=x_all[g][:].indirect(offs_t[:]))
-
-        def pair_tile(name):
-            return keep.tile([P, 2, P, PACK], BF16, name=name, align_bytes=64)
-
-        def round_pair(engine, grouped, raw, pair, m0=0):
-            count = raw.shape[2] // TILES
-            src = raw[:].rearrange("p j (m t) -> p m j t", t=TILES)[:, :, :, 2 * pair : 2 * pair + 2]
-            dst = grouped[:].rearrange("p e m j -> p m j e")[:, m0 : m0 + count, :, :]
-            copy_on(engine, dst, src)
-
-        def quantize_pair(grouped, name):
-            return quantize(grouped[:].rearrange("p e m j -> p (e m j)"), 2 * P, name)
-
-        def prepare(engine, raw, pair, name):
-            grouped = pair_tile(name + "_bf16")
-            round_pair(engine, grouped, raw, pair)
-            return quantize_pair(grouped, name)
-
-        def one_pass(acc, quantized, column, g):
-            codes, scales = quantized
+        def one_pass(bank, key, u):
+            codes, scales = quantized[key]
+            g = key[2]
             nc.tensor.matmul_mx(
-                out=acc[:],
-                lhsT=codes[:, column : column + P].bitcast(FP8X4),
-                lhsT_scale=scales[:, column : column + P],
+                out=banks[bank][:],
+                lhsT=codes[:, u * P : (u + 1) * P].bitcast(FP8X4),
+                lhsT_scale=scales[:, u * P : (u + 1) * P],
                 rhs=x_codes[g][:].bitcast(FP8X4),
                 rhs_scale=x_scale[4 * g :, :],
                 start=(g == 0),
                 stop=(g == PASSES - 1),
             )
 
-        def passes(accs, pairs, g):
-            for t in range(TILES):
-                one_pass(accs[t], pairs[t // 2], (t % 2) * P, g)
+        def multiply(name, t0, count, first_bank):
+            for u in range(count):
+                for g in range(PASSES):
+                    one_pass(first_bank + u, (name, t0, g), u)
 
-        def new_banks(name):
-            return [banks.tile([P, S], F32, name="%s%d" % (name, t), tag="acc") for t in range(TILES)]
+        def spare(name, width, host=None, row=0):
+            if host is None:
+                return keep.tile([P, width], F32, name=name)[:]
+            return raw[host][:].rearrange("p j c -> p (j c)")[:, row * V : row * V + width]
 
-        gather_words(0)
-        nc.vector.tensor_copy(out=x_scale[:], in_=x_all_scales[:].indirect(offs_t[:]))
-        gather_words(1)
+        ee, gate, a, picked, terms = {}, {}, {}, {}, {}
 
-        def prepare_pass(raw, name):
-            return [prepare(engine, raw, pair, "%s%d" % (name, pair)) for pair, engine in enumerate(("vector", "scalar"))]
+        def copy_e(t, bank):
+            ee[t] = keep.tile([P, S], F32, name="ee%d" % t)
+            nc.scalar.copy(out=ee[t][:], in_=banks[bank][:])
 
-        gate_acc = new_banks("gate_acc")
-        y_acc = new_banks("y_acc")
-        passes(gate_acc, prepare_pass(w1_raw[0], "w1_0"), 0)
-        passes(y_acc, prepare_pass(w2_raw0, "w2_0"), 0)
-        passes(gate_acc, prepare_pass(w1_raw[1], "w1_1"), 1)
-        grouped = [pair_tile("w2_1%d_bf16" % pair) for pair in range(2)]
-        for half in range(2):
-            for pair in range(2):
-                round_pair("vector", grouped[pair], w2_raw1[half], pair, half * P // 2)
-        passes(y_acc, [quantize_pair(grouped[pair], "w2_1%d" % pair) for pair in range(2)], 1)
-        gate = [keep.tile([P, S], F32, name="gate%d" % t) for t in range(TILES)]
-        for t in range(TILES):
-            nc.scalar.activation(out=gate[t][:], in_=gate_acc[t][:], func=SIGMOID)
-        a = [keep.tile([P, S], F32, name="a%d" % t) for t in range(TILES)]
-        for t in range(TILES):
-            nc.vector.tensor_tensor(out=a[t][:], in0=y_acc[t][:], in1=gate[t][:], op=MULT)
+        def make_gate(t, bank, host=None, row=0):
+            gate[t] = spare("gate%d" % t, S, host, row)
+            nc.scalar.activation(out=gate[t], in_=banks[bank][:], func=SIGMOID)
 
-        e_acc = new_banks("e_acc")
-        w3_q = []
+        def make_a(t, bank):
+            a[t] = keep.tile([P, S], F32, name="a%d" % t)
+            nc.vector.tensor_tensor(out=a[t][:], in0=banks[bank][:], in1=gate[t], op=MULT)
+
+        def fetch(window, offsets, t, d, host=None, row=0):
+            picked[t, d] = spare("picked%d%d" % (t, d), V, host, row)
+            nc.vector.tensor_copy(out=picked[t, d], in_=window[t][:].indirect(offsets[d][:]))
+
+        def fetch_times(window, offsets, t, d, host=None, row=0):
+            terms[t, d] = spare("term%d%d" % (t, d), V, host, row)
+            nc.vector.tensor_tensor(out=terms[t, d], in0=window[t][:].indirect(offsets[d][:]), in1=picked[t, d], op=MULT)
+            for b in range(2):
+                terms[t, d, b] = terms[t, d][:, b * P : (b + 1) * P]
+
+        def fetch_times_half(window, offsets, t, d, b):
+            terms[t, d, b] = spare("term%d%d%d" % (t, d, b), P)
+            nc.vector.tensor_tensor(
+                out=terms[t, d, b],
+                in0=window[t][:].indirect(offsets[d][:, 8 * b : 8 * (b + 1)]),
+                in1=picked[t, d][:, b * P : (b + 1) * P],
+                op=MULT,
+            )
+
+        z_rows = [keep.tile([P, 2, P, 2], BF16, name="z_rows%d" % b) for b in range(2)]
+
+        def turn(tiles, b, bank):
+            for u, t in enumerate(tiles):
+                for d in range(2):
+                    nc.tensor.matmul(
+                        banks[bank][:, u * P : (u + 1) * P],
+                        terms[t, d, b],
+                        identity[:],
+                        start=(d == 0),
+                        stop=(d == 1),
+                        is_transpose=True,
+                    )
+            nc.scalar.copy(
+                out=z_rows[b][:, :, 32 * tiles[0] : 32 * (tiles[-1] + 1), :],
+                in_=banks[bank][:, : len(tiles) * P].rearrange("p (m e i) -> p e m i", e=2, i=2),
+            )
+
+        prepare("scalar", ("w3", 0, 0))
+        one_pass(0, ("w3", 0, 0), 0)
+        nc.vector.tensor_copy(out=x_codes[1][:], in_=x_all[1][:].indirect(offs_t[:]))
+        prepare("scalar", ("w3", 0, 1))
+        one_pass(0, ("w3", 0, 1), 0)
         for g in range(PASSES):
-            w3_q.append([prepare("scalar", w3_raw[g], pair, "w3_%d%d" % (g, pair)) for pair in range(2)])
-            if g == 0:
-                passes(e_acc, w3_q[0], 0)
-        w5_bf16 = keep.tile([P, PASSES, N, PACK], BF16, name="w5_bf16", align_bytes=64)
-        nc.scalar.copy(
-            out=w5_bf16[:].rearrange("p g (c i) j -> p g c j i", i=4),
-            in_=w5_raw[:].rearrange("p g j (c i) -> p g c j i", i=4),
-        )
-        w5_q = quantize(w5_bf16[:].rearrange("p g c j -> p (g c j)"), PASSES * N, "w5")
-        w4_bf16 = keep.tile([P, N, PACK], BF16, name="w4_bf16", align_bytes=64)
-        nc.scalar.copy(
-            out=w4_bf16[:].rearrange("p (c i) j -> p c j i", i=4), in_=w4_raw[:].rearrange("p j (c i) -> p c j i", i=4)
-        )
-        w4_codes, w4_scales = quantize(w4_bf16[:].rearrange("p c j -> p (c j)"), N, "w4")
-        passes(e_acc, w3_q[1], 1)
-        ee = [keep.tile([P, S], F32, name="ee%d" % t) for t in range(TILES)]
-        for t in range(TILES):
-            nc.scalar.copy(out=ee[t][:], in_=e_acc[t][:])
-        g_acc = banks.tile([P, S], F32, name="g_acc", tag="acc")
+            prepare("scalar", ("w3", 1, g))
+            one_pass(1, ("w3", 1, g), 0)
+        for t in range(2):
+            copy_e(t, t)
+        prepare("vector", ("w1", 0, 0))
+        prepare("scalar", ("w1", 0, 1))
+        multiply("w1", 0, 2, 2)
+        prepare("scalar", ("w2", 0, 0))
+        prepare("vector", ("w2", 0, 1))
+        multiply("w2", 0, 2, 4)
+        make_gate(0, 2)
+        make_gate(1, 3)
+        prepare("scalar", ("w1", 2, 0))
+        prepare("scalar", ("w2", 2, 0))
+        prepare("scalar", ("w1", 2, 1))
+        prepare("vector", ("w2", 2, 1))
+        multiply("w1", 2, 2, 0)
+        multiply("w2", 2, 2, 6)
+        prepare("scalar", ("w3", 2, 0))
+        for t in range(2, 4):
+            make_gate(t, t - 2, ("w3", 2, 0), 2 * (t - 2))
+        prepare("scalar", ("w3", 2, 1))
+        multiply("w3", 2, 2, 2)
+        for t in range(2, 4):
+            copy_e(t, t)
+        fetch(ee, nxt_t, 0, 0, ("w1", 0, 0), 0)
+        fetch(ee, nxt_t, 0, 1, ("w1", 0, 0), 1)
+        fetch(ee, nxt_t, 1, 0, ("w1", 0, 1))
+        fetch(ee, nxt_t, 1, 1, ("w2", 0, 1))
+        make_a(0, 4)
+        fetch_times(a, pos_t, 0, 0, ("w1", 2, 0), 0)
+        fetch_times(a, pos_t, 0, 1, ("w1", 2, 0), 1)
+        make_a(1, 5)
+        fetch_times(a, pos_t, 1, 0, ("w1", 2, 1))
+        fetch_times(a, pos_t, 1, 1, ("w2", 2, 1))
         for g in range(PASSES):
-            one_pass(g_acc, w5_q, g * N, g)
+            prepare("scalar", ("w5", 0, g))
+        multiply("w5", 0, 1, 4)
         gg = keep.tile([P, S], F32, name="gg")
-        nc.scalar.activation(out=gg[:], in_=g_acc[:], func=SIGMOID)
-
-        picked_a = {}
-        for t in range(TILES):
-            for d in range(2):
-                picked_a[t, d] = keep.tile([P, V], F32, name="picked_a%d%d" % (t, d))
-                nc.vector.tensor_copy(out=picked_a[t, d][:], in_=a[t][:].indirect(pos_t[d][:]))
-        terms = [keep.tile([P, TILES, V], F32, name="term%d" % d) for d in range(2)]
-        for t in range(TILES):
-            for d in range(2):
-                nc.vector.tensor_tensor(
-                    out=terms[d][:, t, :], in0=ee[t][:].indirect(nxt_t[d][:]), in1=picked_a[t, d][:], op=MULT
-                )
-
-        halves = [slice(0, V // 2), slice(V // 2, V)]
-        z = []
-        for h, cols in enumerate(halves):
-            z.append(keep.tile([P, V // 2, PACK], BF16, name="z%d" % h, tag="z%d" % h, align_bytes=64))
-            in0, in1 = (term[:, :, cols].rearrange("p t (c i) -> p c t i", i=4) for term in terms)
-            nc.vector.tensor_tensor(out=z[h][:].rearrange("p (c i) t -> p c t i", i=4), in0=in0, in1=in1, op=ADD)
-        rr = []
-        for h in range(2):
-            z_codes, z_scales = quantize(z[h][:].rearrange("p v t -> p (v t)"), V // 2, "z%d" % h)
-            rr.append(banks.tile([P, V // 2], F32, name="rr%d" % h, tag="acc"))
+        nc.scalar.activation(out=gg[:], in_=banks[4][:], func=SIGMOID)
+        make_a(2, 6)
+        make_a(3, 7)
+        fetch(a, pos_t, 2, 0)
+        fetch(a, pos_t, 2, 1, ("w3", 2, 1))
+        fetch(a, pos_t, 3, 0, ("w5", 0, 0))
+        fetch(a, pos_t, 3, 1, ("w5", 0, 1))
+        prepare("scalar", ("w4", 0, 0))
+        w4_codes, w4_scales = quantized["w4", 0, 0]
+        for b in range(2):
+            turn((0, 1), b, 6 + b)
+        for b in range(2):
+            for t in range(2, 4):
+                for d in range(2):
+                    fetch_times_half(ee, nxt_t, t, d, b)
+        picked_g = keep.tile([P, V], F32, name="picked_g")
+        nc.vector.tensor_copy(out=picked_g[:], in_=gg[:].indirect(own_t[:]))
+        for b in range(2):
+            for t in range(2, 4):
+                turn((t,), b, 2 * b + t - 2)
+            z_words = z_rows[b][:].rearrange("p e m i -> p (e m i)").bitcast(F32)
+            back = banks[6 + b][:, : 2 * P]
+            for e in range(2):
+                nc.tensor.transpose(back[:, e * P : (e + 1) * P], z_words[:, e * P : (e + 1) * P], identity[:])
+            z = keep.tile([P, P * PACK], BF16, name="z%d" % b, align_bytes=64)
+            nc.scalar.copy(
+                out=z[:].bitcast(F32).rearrange("p (v e) -> p v e", e=2), in_=back.rearrange("p (e v) -> p v e", e=2)
+            )
+            z_codes, z_scales = quantize(z[:], "z%d" % b)
+            rr = banks[(4, 5)[b]][:, :P]
             nc.tensor.matmul_mx(
-                out=rr[h][:],
+                out=rr,
                 lhsT=w4_codes[:].bitcast(FP8X4),
                 lhsT_scale=w4_scales[:],
                 rhs=z_codes[:].bitcast(FP8X4),
@@ -214,9 +279,6 @@ def tile_picked_ytri_gated_p_kernel(
                 start=True,
                 stop=True,
             )
-        picked_g = keep.tile([P, V], F32, name="picked_g", tag="z0", align_bytes=64)
-        nc.vector.tensor_copy(out=picked_g[:], in_=gg[:].indirect(own_t[:]))
-        for h, cols in enumerate(halves):
-            result = keep.tile([P, V // 2], F32, name="result%d" % h)
-            nc.vector.tensor_tensor(out=result[:], in0=rr[h][:], in1=picked_g[:, cols], op=MULT)
-            nc.sync.dma_start(out=out[:, cols], in_=result[:])
+            result = keep.tile([P, P], F32, name="result%d" % b)
+            nc.vector.tensor_tensor(out=result[:], in0=rr, in1=picked_g[:, b * P : (b + 1) * P], op=MULT)
+            nc.sync.dma_start(out=out[:, b * P : (b + 1) * P], in_=result[:])

@@ -52,17 +52,21 @@ def tile_picked_ytri_gated_p_kernel(
             nc.sync.dma_start(out=tile[:].bitcast(I32), in_=x_words[g].rearrange("p n t -> p (n t)").bitcast(I32))
             return tile
 
-        rounded, quantized = {}, {}
+        staged, rounded, quantized = {}, {}, {}
 
-        def round_on(engine, key):
+        def round_on(engine, key, reuse):
             tile = raw[key]
-            grouped = keep.tile([P, tile.shape[2], PACK], BF16, name="%s_%d%d_bf16" % key, align_bytes=64)
+            if reuse is None:
+                grouped = keep.tile([P, tile.shape[2], PACK], BF16, name="%s_%d%d_bf16" % key, align_bytes=64)
+            else:
+                grouped = staged[reuse]
+            staged[key] = grouped
             dst = grouped[:].rearrange("p (c i) j -> p c j i", i=4)
             src = tile[:].rearrange("p j (c i) -> p c j i", i=4)
             if engine == "vector":
                 nc.vector.tensor_copy(out=dst, in_=src)
             elif engine == "gpsimd":
-                nc.gpsimd.tensor_copy(out=dst, in_=src)
+                nc.gpsimd.tensor_copy(out=grouped[:], in_=tile[:].rearrange("p j c -> p c j"))
             else:
                 nc.scalar.copy(out=dst, in_=src)
             rounded[key] = grouped[:].rearrange("p c j -> p (c j)")
@@ -74,8 +78,8 @@ def tile_picked_ytri_gated_p_kernel(
             nc.vector.quantize_mx(out=codes[:].bitcast(FP8X4), scales=scales[:], in_=values)
             return codes, scales
 
-        def prepare(engine, key):
-            round_on(engine, key)
+        def prepare(engine, key, reuse=None):
+            round_on(engine, key, reuse)
             quantized[key] = quantize(rounded[key], "%s_%d%d" % key)
 
         x_all_scales = keep.tile([P, T], U8, name="x_all_scales")
@@ -109,8 +113,8 @@ def tile_picked_ytri_gated_p_kernel(
         load_weight(w2, "w2", 0, 2, 4)
         load_weight(w1, "w1", 1, 2, 4)
         load_weight(w2, "w2", 1, 2, 4)
-        load_weight(w3, "w3", 0, 2, 4)
         own_t = load_list(own, "own_t")
+        load_weight(w3, "w3", 0, 2, 4)
         load_weight(w3, "w3", 1, 2, 4)
         for g in range(PASSES):
             load_weight(w5, "w5", g, 0, 1)
@@ -206,29 +210,29 @@ def tile_picked_ytri_gated_p_kernel(
         for t in range(2):
             copy_e(t, t)
         prepare("vector", ("w1", 0, 0))
-        prepare("scalar", ("w1", 0, 1))
+        prepare("gpsimd", ("w1", 0, 1), ("w1", 0, 0))
         multiply("w1", 0, 2, 2)
         prepare("scalar", ("w2", 0, 0))
         prepare("vector", ("w2", 0, 1))
         multiply("w2", 0, 2, 4)
         make_gate(0, 2)
         make_gate(1, 3)
-        prepare("scalar", ("w1", 2, 0))
+        prepare("gpsimd", ("w1", 2, 0), ("w2", 0, 1))
         prepare("scalar", ("w2", 2, 0))
         prepare("scalar", ("w1", 2, 1))
-        prepare("vector", ("w2", 2, 1))
+        prepare("scalar", ("w2", 2, 1))
         multiply("w1", 2, 2, 0)
         multiply("w2", 2, 2, 6)
-        prepare("scalar", ("w3", 2, 0))
         for t in range(2, 4):
-            make_gate(t, t - 2, ("w3", 2, 0), 2 * (t - 2))
+            make_gate(t, t - 2)
+        prepare("gpsimd", ("w3", 2, 0), ("w2", 2, 1))
         prepare("scalar", ("w3", 2, 1))
         multiply("w3", 2, 2, 2)
         for t in range(2, 4):
             copy_e(t, t)
         fetch(ee, nxt_t, 0, 0, ("w1", 0, 0), 0)
         fetch(ee, nxt_t, 0, 1, ("w1", 0, 0), 1)
-        fetch(ee, nxt_t, 1, 0, ("w1", 0, 1))
+        fetch(ee, nxt_t, 1, 0, ("w1", 0, 0), 2)
         fetch(ee, nxt_t, 1, 1, ("w2", 0, 1))
         make_a(0, 4)
         fetch_times(a, pos_t, 0, 0, ("w1", 2, 0), 0)

@@ -71,6 +71,17 @@ def tile_picked_ytri_gated_p_kernel(
                 nc.scalar.copy(out=dst, in_=src)
             rounded[key] = grouped[:].rearrange("p c j -> p (c j)")
 
+        def prepare_tile(engine, source, u):
+            key = (source[0], source[1] + u, source[2])
+            grouped = keep.tile([P, P, PACK], BF16, name="%s_%d%d_tile" % key, align_bytes=64)
+            dst = grouped[:].rearrange("p (c i) j -> p c j i", i=4)
+            src = raw[source][:, :, u * P : (u + 1) * P].rearrange("p j (c i) -> p c j i", i=4)
+            if engine == "vector":
+                nc.vector.tensor_copy(out=dst, in_=src)
+            else:
+                nc.scalar.copy(out=dst, in_=src)
+            quantized[key] = quantize(grouped[:].rearrange("p c j -> p (c j)"), "%s_%d%d" % key)
+
         def quantize(values, name):
             width = values.shape[1] // PACK
             codes = keep.tile([P, width], U32, name=name + "_codes", align_bytes=64)
@@ -91,7 +102,7 @@ def tile_picked_ytri_gated_p_kernel(
                 out=x_all_scales[32 * q : 32 * q + 4 * PASSES, :].bitcast(I32),
                 in_=x_scales[:, 4 * q : 4 * q + 4, :].bitcast(I32),
             )
-        load_weight(w3, "w3", 0, 0, 1)
+        load_weight(w3, "w3", 0, 0, 2)
         x_all.append(load_words(1))
         warm = keep.tile([P, 1], F32, name="warm")
         nc.vector.memset(warm[:], 0.0)
@@ -100,9 +111,7 @@ def tile_picked_ytri_gated_p_kernel(
         identity = keep.tile([P, P], F32, name="identity")
         make_identity(nc, identity[:])
 
-        load_weight(w3, "w3", 1, 0, 1)
-        for g in range(PASSES):
-            load_weight(w3, "w3", g, 1, 2)
+        load_weight(w3, "w3", 1, 0, 2)
         nxt_t = [load_list(nxt1, "nxt1_t"), load_list(nxt2, "nxt2_t")]
         for w, name in ((w1, "w1"), (w2, "w2")):
             for g in range(PASSES):
@@ -113,12 +122,12 @@ def tile_picked_ytri_gated_p_kernel(
         load_weight(w2, "w2", 0, 2, 4)
         load_weight(w1, "w1", 1, 2, 4)
         load_weight(w2, "w2", 1, 2, 4)
-        own_t = load_list(own, "own_t")
         load_weight(w3, "w3", 0, 2, 4)
         load_weight(w3, "w3", 1, 2, 4)
         for g in range(PASSES):
             load_weight(w5, "w5", g, 0, 1)
         load_weight(w4, "w4", 0, 0, 1)
+        own_t = load_list(own, "own_t")
 
         x_scale = keep.tile([P, S], U8, name="x_scale", align_bytes=64)
         x_codes = [keep.tile([P, S], U32, name="x_codes%d" % g, align_bytes=64) for g in range(PASSES)]
@@ -173,7 +182,10 @@ def tile_picked_ytri_gated_p_kernel(
                 terms[t, d, b] = terms[t, d][:, b * P : (b + 1) * P]
 
         def fetch_times_half(window, offsets, t, d, b):
-            terms[t, d, b] = spare("term%d%d%d" % (t, d, b), P)
+            if (t, b) == (2, 1):
+                terms[t, d, b] = picked[3, d][:, :P]
+            else:
+                terms[t, d, b] = spare("term%d%d%d" % (t, d, b), P)
             nc.vector.tensor_tensor(
                 out=terms[t, d, b],
                 in0=window[t][:].indirect(offsets[d][:, 8 * b : 8 * (b + 1)]),
@@ -199,18 +211,17 @@ def tile_picked_ytri_gated_p_kernel(
                 in_=banks[bank][:, : len(tiles) * P].rearrange("p (m e i) -> p e m i", e=2, i=2),
             )
 
-        prepare("scalar", ("w3", 0, 0))
-        one_pass(0, ("w3", 0, 0), 0)
+        for u in range(2):
+            prepare_tile("scalar", ("w3", 0, 0), u)
+            one_pass(u, ("w3", u, 0), 0)
         nc.vector.tensor_copy(out=x_codes[1][:], in_=x_all[1][:].indirect(offs_t[:]))
-        prepare("scalar", ("w3", 0, 1))
-        one_pass(0, ("w3", 0, 1), 0)
-        for g in range(PASSES):
-            prepare("scalar", ("w3", 1, g))
-            one_pass(1, ("w3", 1, g), 0)
+        for u, engine in enumerate(("vector", "scalar")):
+            prepare_tile(engine, ("w3", 0, 1), u)
+            one_pass(u, ("w3", u, 1), 0)
         for t in range(2):
             copy_e(t, t)
         prepare("vector", ("w1", 0, 0))
-        prepare("gpsimd", ("w1", 0, 1), ("w1", 0, 0))
+        prepare("scalar", ("w1", 0, 1))
         multiply("w1", 0, 2, 2)
         prepare("scalar", ("w2", 0, 0))
         prepare("vector", ("w2", 0, 1))
@@ -225,29 +236,31 @@ def tile_picked_ytri_gated_p_kernel(
         multiply("w2", 2, 2, 6)
         for t in range(2, 4):
             make_gate(t, t - 2)
-        prepare("gpsimd", ("w3", 2, 0), ("w2", 2, 1))
-        prepare("scalar", ("w3", 2, 1))
-        multiply("w3", 2, 2, 2)
-        for t in range(2, 4):
-            copy_e(t, t)
+        round_on("gpsimd", ("w3", 2, 0), ("w2", 2, 1))
+        round_on("scalar", ("w3", 2, 1), None)
         fetch(ee, nxt_t, 0, 0, ("w1", 0, 0), 0)
         fetch(ee, nxt_t, 0, 1, ("w1", 0, 0), 1)
         fetch(ee, nxt_t, 1, 0, ("w1", 0, 0), 2)
         fetch(ee, nxt_t, 1, 1, ("w2", 0, 1))
         make_a(0, 4)
         fetch_times(a, pos_t, 0, 0, ("w1", 2, 0), 0)
-        fetch_times(a, pos_t, 0, 1, ("w1", 2, 0), 1)
+        fetch_times(a, pos_t, 0, 1, ("w2", 2, 0))
         make_a(1, 5)
         fetch_times(a, pos_t, 1, 0, ("w1", 2, 1))
         fetch_times(a, pos_t, 1, 1, ("w2", 2, 1))
+        make_a(2, 6)
+        make_a(3, 7)
+        fetch(a, pos_t, 2, 0)
+        for g in range(PASSES):
+            quantized["w3", 2, g] = quantize(rounded["w3", 2, g], "w3_2%d" % g)
+        multiply("w3", 2, 2, 2)
+        for t in range(2, 4):
+            copy_e(t, t)
         for g in range(PASSES):
             prepare("scalar", ("w5", 0, g))
         multiply("w5", 0, 1, 4)
         gg = keep.tile([P, S], F32, name="gg")
         nc.scalar.activation(out=gg[:], in_=banks[4][:], func=SIGMOID)
-        make_a(2, 6)
-        make_a(3, 7)
-        fetch(a, pos_t, 2, 0)
         fetch(a, pos_t, 2, 1, ("w3", 2, 1))
         fetch(a, pos_t, 3, 0, ("w5", 0, 0))
         fetch(a, pos_t, 3, 1, ("w5", 0, 1))
@@ -270,7 +283,8 @@ def tile_picked_ytri_gated_p_kernel(
                 nc.tensor.transpose(back[:, e * P : (e + 1) * P], z_words[:, e * P : (e + 1) * P], identity[:])
             z = keep.tile([P, P * PACK], BF16, name="z%d" % b, align_bytes=64)
             nc.scalar.copy(
-                out=z[:].bitcast(F32).rearrange("p (v e) -> p v e", e=2), in_=back.rearrange("p (e v) -> p v e", e=2)
+                out=z[:].bitcast(F32).rearrange("p (v i e) -> p v e i", i=2, e=2),
+                in_=back.rearrange("p (e v i) -> p v e i", e=2, i=2),
             )
             z_codes, z_scales = quantize(z[:], "z%d" % b)
             rr = banks[(4, 5)[b]][:, :P]

@@ -147,6 +147,18 @@ def tile_picked_ytri_gated_p_kernel(
                 stop=(g == PASSES - 1),
             )
 
+        def keep_warm(bank):
+            codes, scales = quantized["w1", 0, 0]
+            nc.tensor.matmul_mx(
+                out=banks[bank][:],
+                lhsT=codes[:, :P].bitcast(FP8X4),
+                lhsT_scale=scales[:, :P],
+                rhs=x_codes[0][:].bitcast(FP8X4),
+                rhs_scale=x_scale[:],
+                start=True,
+                stop=True,
+            )
+
         def multiply(name, t0, count, first_bank):
             for u in range(count):
                 for g in range(PASSES):
@@ -223,6 +235,7 @@ def tile_picked_ytri_gated_p_kernel(
         prepare("vector", ("w1", 0, 0))
         prepare("scalar", ("w1", 0, 1))
         multiply("w1", 0, 2, 2)
+        keep_warm(1)
         prepare("scalar", ("w2", 0, 0))
         prepare("vector", ("w2", 0, 1))
         multiply("w2", 0, 2, 4)
@@ -243,13 +256,16 @@ def tile_picked_ytri_gated_p_kernel(
         fetch(ee, nxt_t, 1, 0, ("w1", 0, 0), 2)
         fetch(ee, nxt_t, 1, 1, ("w2", 0, 1))
         make_a(0, 4)
+        keep_warm(4)
         fetch_times(a, pos_t, 0, 0, ("w1", 2, 0), 0)
         fetch_times(a, pos_t, 0, 1, ("w2", 2, 0))
         make_a(1, 5)
         fetch_times(a, pos_t, 1, 0, ("w1", 2, 1))
         fetch_times(a, pos_t, 1, 1, ("w2", 2, 1))
         make_a(2, 6)
+        keep_warm(6)
         make_a(3, 7)
+        keep_warm(7)
         fetch(a, pos_t, 2, 0)
         for g in range(PASSES):
             quantized["w3", 2, g] = quantize(rounded["w3", 2, g], "w3_2%d" % g)

@@ -42,13 +42,13 @@ def tile_picked_ytri_gated_p_kernel(
         raw = {}
 
         def load_weight(w, name, g, t0, t1):
-            tile = keep.tile([P, PACK, (t1 - t0) * P], F32, name="%s_raw%d%d" % (name, t0, g))
+            tile = keep.tile([P, PACK, (t1 - t0) * P], F32, name="%s_raw%d%d" % (name, t0, g), align_bytes=64)
             rows = w[g * K_PASS : (g + 1) * K_PASS, :].rearrange("(p j) c -> p j c", j=PACK)
             nc.sync.dma_start(out=tile[:], in_=rows[:, :, t0 * P : t1 * P])
             raw[name, t0, g] = tile
 
         def load_words(g):
-            tile = keep.tile([P, T], U32, name="x_all_words%d" % g)
+            tile = keep.tile([P, T], U32, name="x_all_words%d" % g, align_bytes=64)
             nc.sync.dma_start(out=tile[:].bitcast(I32), in_=x_words[g].rearrange("p n t -> p (n t)").bitcast(I32))
             return tile
 
@@ -117,13 +117,12 @@ def tile_picked_ytri_gated_p_kernel(
             for g in range(PASSES):
                 load_weight(w, name, g, 0, 2)
         pos_t = [load_list(pos1, "pos1_t")]
-        load_weight(w1, "w1", 0, 2, 4)
-        pos_t.append(load_list(pos2, "pos2_t"))
-        load_weight(w2, "w2", 0, 2, 4)
-        load_weight(w1, "w1", 1, 2, 4)
-        load_weight(w2, "w2", 1, 2, 4)
         load_weight(w3, "w3", 0, 2, 4)
+        pos_t.append(load_list(pos2, "pos2_t"))
         load_weight(w3, "w3", 1, 2, 4)
+        for w, name in ((w1, "w1"), (w2, "w2")):
+            for g in range(PASSES):
+                load_weight(w, name, g, 2, 4)
         for g in range(PASSES):
             load_weight(w5, "w5", g, 0, 1)
         load_weight(w4, "w4", 0, 0, 1)
@@ -241,60 +240,65 @@ def tile_picked_ytri_gated_p_kernel(
         multiply("w2", 0, 2, 4)
         make_gate(0, 2)
         make_gate(1, 3)
-        prepare("gpsimd", ("w1", 2, 0), ("w2", 0, 1))
-        prepare("scalar", ("w2", 2, 0))
-        prepare("scalar", ("w1", 2, 1))
-        prepare("scalar", ("w2", 2, 1))
-        multiply("w1", 2, 2, 0)
-        multiply("w2", 2, 2, 6)
+        prepare("gpsimd", ("w3", 2, 0), ("w2", 0, 1))
+        prepare("scalar", ("w3", 2, 1))
+        multiply("w3", 2, 2, 0)
+        prepare("scalar", ("w1", 2, 0))
         for t in range(2, 4):
-            make_gate(t, t - 2)
-        round_on("gpsimd", ("w3", 2, 0), ("w2", 2, 1))
-        round_on("scalar", ("w3", 2, 1), None)
+            copy_e(t, t - 2)
+        prepare("vector", ("w1", 2, 1))
+        multiply("w1", 2, 2, 2)
+        prepare("scalar", ("w2", 2, 0))
+        prepare("vector", ("w2", 2, 1))
+        for u in range(2):
+            one_pass(6 + u, ("w2", 2, 0), u)
+            one_pass(6 + u, ("w2", 2, 1), u)
+        for t in range(2, 4):
+            make_gate(t, t)
+        keep_warm(2)
         fetch(ee, nxt_t, 0, 0, ("w1", 0, 0), 0)
         fetch(ee, nxt_t, 0, 1, ("w1", 0, 0), 1)
         fetch(ee, nxt_t, 1, 0, ("w1", 0, 0), 2)
         fetch(ee, nxt_t, 1, 1, ("w2", 0, 1))
         make_a(0, 4)
         keep_warm(4)
-        fetch_times(a, pos_t, 0, 0, ("w1", 2, 0), 0)
-        fetch_times(a, pos_t, 0, 1, ("w2", 2, 0))
+        fetch_times(a, pos_t, 0, 0, ("w3", 2, 0), 0)
         make_a(1, 5)
-        fetch_times(a, pos_t, 1, 0, ("w1", 2, 1))
-        fetch_times(a, pos_t, 1, 1, ("w2", 2, 1))
-        make_a(2, 6)
-        keep_warm(6)
-        make_a(3, 7)
-        keep_warm(7)
-        fetch(a, pos_t, 2, 0)
-        for g in range(PASSES):
-            quantized["w3", 2, g] = quantize(rounded["w3", 2, g], "w3_2%d" % g)
-        multiply("w3", 2, 2, 2)
-        for t in range(2, 4):
-            copy_e(t, t)
+        keep_warm(5)
+        fetch_times(a, pos_t, 0, 1, ("w3", 2, 0), 1)
+        fetch_times(a, pos_t, 1, 0, ("w3", 2, 1), 0)
+        fetch_times(a, pos_t, 1, 1, ("w3", 2, 1), 1)
+        fetch(ee, nxt_t, 2, 0, ("w1", 2, 1), 0)
+        fetch(ee, nxt_t, 2, 1, ("w1", 2, 1), 1)
+        fetch(ee, nxt_t, 3, 0, ("w2", 2, 1), 0)
+        fetch(ee, nxt_t, 3, 1, ("w2", 2, 1), 1)
         for g in range(PASSES):
             prepare("scalar", ("w5", 0, g))
         multiply("w5", 0, 1, 4)
         gg = keep.tile([P, S], F32, name="gg")
         nc.scalar.activation(out=gg[:], in_=banks[4][:], func=SIGMOID)
-        fetch(a, pos_t, 2, 1, ("w3", 2, 1))
-        fetch(a, pos_t, 3, 0, ("w5", 0, 0))
-        fetch(a, pos_t, 3, 1, ("w5", 0, 1))
-        prepare("scalar", ("w4", 0, 0))
-        w4_codes, w4_scales = quantized["w4", 0, 0]
+        make_a(2, 6)
+        make_a(3, 7)
         for b in range(2):
-            turn((0, 1), b, 6 + b)
+            turn((0, 1), b, 2 + b)
         for b in range(2):
             for t in range(2, 4):
                 for d in range(2):
-                    fetch_times_half(ee, nxt_t, t, d, b)
+                    fetch_times_half(a, pos_t, t, d, b)
+        w4_bf16 = picked[2, 1].bitcast(BF16)
+        nc.vector.tensor_copy(
+            out=w4_bf16.rearrange("p (c i j) -> p c j i", i=4, j=PACK),
+            in_=raw["w4", 0, 0][:].rearrange("p j (c i) -> p c j i", i=4),
+        )
         picked_g = keep.tile([P, V], F32, name="picked_g")
         nc.vector.tensor_copy(out=picked_g[:], in_=gg[:].indirect(own_t[:]))
+        w4_codes, w4_scales = quantize(w4_bf16, "w4")
         for b in range(2):
             for t in range(2, 4):
-                turn((t,), b, 2 * b + t - 2)
+                turn((t,), b, ((0, 1), (5, 6))[b][t - 2])
+        for b in range(2):
             z_words = z_rows[b][:].rearrange("p e m i -> p (e m i)").bitcast(F32)
-            back = banks[6 + b][:, : 2 * P]
+            back = banks[(5, 3)[b]][:, : 2 * P]
             for e in range(2):
                 nc.tensor.transpose(back[:, e * P : (e + 1) * P], z_words[:, e * P : (e + 1) * P], identity[:])
             z = keep.tile([P, P * PACK], BF16, name="z%d" % b, align_bytes=64)
@@ -303,7 +307,7 @@ def tile_picked_ytri_gated_p_kernel(
                 in_=back.rearrange("p (e v i) -> p v e i", e=2, i=2),
             )
             z_codes, z_scales = quantize(z[:], "z%d" % b)
-            rr = banks[(4, 5)[b]][:, :P]
+            rr = banks[(7, 4)[b]][:, :P]
             nc.tensor.matmul_mx(
                 out=rr,
                 lhsT=w4_codes[:].bitcast(FP8X4),

@@ -146,18 +146,6 @@ def tile_picked_ytri_gated_p_kernel(
                 stop=(g == PASSES - 1),
             )
 
-        def keep_warm(bank):
-            codes, scales = quantized["w1", 0, 0]
-            nc.tensor.matmul_mx(
-                out=banks[bank][:],
-                lhsT=codes[:, :P].bitcast(FP8X4),
-                lhsT_scale=scales[:, :P],
-                rhs=x_codes[0][:].bitcast(FP8X4),
-                rhs_scale=x_scale[:],
-                start=True,
-                stop=True,
-            )
-
         def multiply(name, t0, count, first_bank):
             for u in range(count):
                 for g in range(PASSES):
@@ -234,7 +222,6 @@ def tile_picked_ytri_gated_p_kernel(
         prepare("vector", ("w1", 0, 0))
         prepare("scalar", ("w1", 0, 1))
         multiply("w1", 0, 2, 2)
-        keep_warm(1)
         prepare("scalar", ("w2", 0, 0))
         prepare("vector", ("w2", 0, 1))
         multiply("w2", 0, 2, 4)
@@ -255,16 +242,13 @@ def tile_picked_ytri_gated_p_kernel(
             one_pass(6 + u, ("w2", 2, 1), u)
         for t in range(2, 4):
             make_gate(t, t)
-        keep_warm(2)
         fetch(ee, nxt_t, 0, 0, ("w1", 0, 0), 0)
         fetch(ee, nxt_t, 0, 1, ("w1", 0, 0), 1)
         fetch(ee, nxt_t, 1, 0, ("w1", 0, 0), 2)
         fetch(ee, nxt_t, 1, 1, ("w2", 0, 1))
         make_a(0, 4)
-        keep_warm(4)
         fetch_times(a, pos_t, 0, 0, ("w3", 2, 0), 0)
         make_a(1, 5)
-        keep_warm(5)
         fetch_times(a, pos_t, 0, 1, ("w3", 2, 0), 1)
         fetch_times(a, pos_t, 1, 0, ("w3", 2, 1), 0)
         fetch_times(a, pos_t, 1, 1, ("w3", 2, 1), 1)

@@ -21,8 +21,9 @@ P = 128
 PACK = 4
 K_PASS = P * PACK
 PASSES = K // K_PASS
-TILES = H // P
-HALF = H // 2
+TILE_WORDS = P * PACK // 2
+PIECE_WORDS = 2 * TILE_WORDS
+LAP = 16
 
 
 def tile_picked_ytri_gated_p_kernel(
@@ -52,35 +53,25 @@ def tile_picked_ytri_gated_p_kernel(
             nc.sync.dma_start(out=tile[:].bitcast(I32), in_=x_words[g].rearrange("p n t -> p (n t)").bitcast(I32))
             return tile
 
-        staged, rounded, quantized = {}, {}, {}
+        def scratch(name, words):
+            return keep.tile([P, words], F32, name=name, align_bytes=64)[:]
 
-        def round_on(engine, key, reuse):
-            tile = raw[key]
-            if reuse is None:
-                grouped = keep.tile([P, tile.shape[2], PACK], BF16, name="%s_%d%d_bf16" % key, align_bytes=64)
-            else:
-                grouped = staged[reuse]
-            staged[key] = grouped
-            dst = grouped[:].rearrange("p (c i) j -> p c j i", i=4)
-            src = tile[:].rearrange("p j (c i) -> p c j i", i=4)
-            if engine == "vector":
-                nc.vector.tensor_copy(out=dst, in_=src)
-            elif engine == "gpsimd":
-                nc.gpsimd.tensor_copy(out=grouped[:], in_=tile[:].rearrange("p j c -> p c j"))
-            else:
-                nc.scalar.copy(out=dst, in_=src)
-            rounded[key] = grouped[:].rearrange("p c j -> p (c j)")
-
-        def prepare_tile(engine, source, u):
-            key = (source[0], source[1] + u, source[2])
-            grouped = keep.tile([P, P, PACK], BF16, name="%s_%d%d_tile" % key, align_bytes=64)
-            dst = grouped[:].rearrange("p (c i) j -> p c j i", i=4)
-            src = raw[source][:, :, u * P : (u + 1) * P].rearrange("p j (c i) -> p c j i", i=4)
+        def round_on(engine, src, stage):
+            grouped = stage.bitcast(BF16).rearrange("p (c j) -> p c j", j=PACK)
+            if engine == "gpsimd":
+                nc.gpsimd.tensor_scalar(
+                    out=grouped, in0=src.rearrange("p j c -> p c j"), scalar1=1.0, scalar2=0.0, op0=MULT, op1=ADD
+                )
+                return
+            dst = grouped.rearrange("p (c i) j -> p c j i", i=4)
+            src = src.rearrange("p j (c i) -> p c j i", i=4)
             if engine == "vector":
                 nc.vector.tensor_copy(out=dst, in_=src)
             else:
                 nc.scalar.copy(out=dst, in_=src)
-            quantized[key] = quantize(grouped[:].rearrange("p c j -> p (c j)"), "%s_%d%d" % key)
+
+        def round_tile(engine, key, u, stage):
+            round_on(engine, raw[key][:, :, u * P : (u + 1) * P], stage[:, u * TILE_WORDS : (u + 1) * TILE_WORDS])
 
         def quantize(values, name):
             width = values.shape[1] // PACK
@@ -89,53 +80,8 @@ def tile_picked_ytri_gated_p_kernel(
             nc.vector.quantize_mx(out=codes[:].bitcast(FP8X4), scales=scales[:], in_=values)
             return codes, scales
 
-        def prepare(engine, key, reuse=None):
-            round_on(engine, key, reuse)
-            quantized[key] = quantize(rounded[key], "%s_%d%d" % key)
-
-        x_all_scales = keep.tile([P, T], U8, name="x_all_scales")
-        nc.gpsimd.memset(x_all_scales[:].bitcast(I32), 0)
-        x_all = [load_words(0)]
-        offs_t = load_list(offs, "offs_t")
-        for q in range(4):
-            nc.sync.dma_start(
-                out=x_all_scales[32 * q : 32 * q + 4 * PASSES, :].bitcast(I32),
-                in_=x_scales[:, 4 * q : 4 * q + 4, :].bitcast(I32),
-            )
-        load_weight(w3, "w3", 0, 0, 2)
-        x_all.append(load_words(1))
-        warm = keep.tile([P, 1], F32, name="warm")
-        nc.vector.memset(warm[:], 0.0)
-        warm_out = keep.tile([P, 1], F32, name="warm_out")
-        nc.scalar.activation(out=warm_out[:], in_=warm[:], func=SIGMOID)
-        identity = keep.tile([P, P], F32, name="identity")
-        make_identity(nc, identity[:])
-
-        load_weight(w3, "w3", 1, 0, 2)
-        nxt_t = [load_list(nxt1, "nxt1_t"), load_list(nxt2, "nxt2_t")]
-        for w, name in ((w1, "w1"), (w2, "w2")):
-            for g in range(PASSES):
-                load_weight(w, name, g, 0, 2)
-        pos_t = [load_list(pos1, "pos1_t")]
-        load_weight(w3, "w3", 0, 2, 4)
-        pos_t.append(load_list(pos2, "pos2_t"))
-        load_weight(w3, "w3", 1, 2, 4)
-        for w, name in ((w1, "w1"), (w2, "w2")):
-            for g in range(PASSES):
-                load_weight(w, name, g, 2, 4)
-        for g in range(PASSES):
-            load_weight(w5, "w5", g, 0, 1)
-        load_weight(w4, "w4", 0, 0, 1)
-        own_t = load_list(own, "own_t")
-
-        x_scale = keep.tile([P, S], U8, name="x_scale", align_bytes=64)
-        x_codes = [keep.tile([P, S], U32, name="x_codes%d" % g, align_bytes=64) for g in range(PASSES)]
-        nc.vector.tensor_copy(out=x_codes[0][:], in_=x_all[0][:].indirect(offs_t[:]))
-        nc.vector.tensor_copy(out=x_scale[:], in_=x_all_scales[:].indirect(offs_t[:]))
-
-        def one_pass(bank, key, u):
-            codes, scales = quantized[key]
-            g = key[2]
+        def one_pass(bank, planes, u, g):
+            codes, scales = planes
             nc.tensor.matmul_mx(
                 out=banks[bank][:],
                 lhsT=codes[:, u * P : (u + 1) * P].bitcast(FP8X4),
@@ -146,15 +92,10 @@ def tile_picked_ytri_gated_p_kernel(
                 stop=(g == PASSES - 1),
             )
 
-        def multiply(name, t0, count, first_bank):
-            for u in range(count):
-                for g in range(PASSES):
-                    one_pass(first_bank + u, (name, t0, g), u)
-
-        def spare(name, width, host=None, row=0):
-            if host is None:
-                return keep.tile([P, width], F32, name=name)[:]
-            return raw[host][:].rearrange("p j c -> p (j c)")[:, row * V : row * V + width]
+        def multiply(key, stage, first_bank):
+            planes = quantize(stage.bitcast(BF16), "%s_%d%d" % key)
+            for u in range(stage.shape[1] // TILE_WORDS):
+                one_pass(first_bank + u, planes, u, key[2])
 
         ee, gate, a, picked, terms = {}, {}, {}, {}, {}
 
@@ -162,32 +103,28 @@ def tile_picked_ytri_gated_p_kernel(
             ee[t] = keep.tile([P, S], F32, name="ee%d" % t)
             nc.scalar.copy(out=ee[t][:], in_=banks[bank][:])
 
-        def make_gate(t, bank, host=None, row=0):
-            gate[t] = spare("gate%d" % t, S, host, row)
+        def make_gate(t, bank, place):
+            gate[t] = place
             nc.scalar.activation(out=gate[t], in_=banks[bank][:], func=SIGMOID)
 
         def make_a(t, bank):
             a[t] = keep.tile([P, S], F32, name="a%d" % t)
             nc.vector.tensor_tensor(out=a[t][:], in0=banks[bank][:], in1=gate[t], op=MULT)
 
-        def fetch(window, offsets, t, d, host=None, row=0):
-            picked[t, d] = spare("picked%d%d" % (t, d), V, host, row)
-            nc.vector.tensor_copy(out=picked[t, d], in_=window[t][:].indirect(offsets[d][:]))
+        def fetch(t, d, place):
+            picked[t, d] = place
+            nc.vector.tensor_copy(out=place, in_=ee[t][:].indirect(nxt_t[d][:]))
 
-        def fetch_times(window, offsets, t, d, host=None, row=0):
-            terms[t, d] = spare("term%d%d" % (t, d), V, host, row)
-            nc.vector.tensor_tensor(out=terms[t, d], in0=window[t][:].indirect(offsets[d][:]), in1=picked[t, d], op=MULT)
+        def fetch_times(t, d, place):
+            nc.vector.tensor_tensor(out=place, in0=a[t][:].indirect(pos_t[d][:]), in1=picked[t, d], op=MULT)
             for b in range(2):
-                terms[t, d, b] = terms[t, d][:, b * P : (b + 1) * P]
+                terms[t, d, b] = place[:, b * P : (b + 1) * P]
 
-        def fetch_times_half(window, offsets, t, d, b):
-            if (t, b) == (2, 1):
-                terms[t, d, b] = picked[3, d][:, :P]
-            else:
-                terms[t, d, b] = spare("term%d%d%d" % (t, d, b), P)
+        def fetch_times_half(t, d, b, place):
+            terms[t, d, b] = place
             nc.vector.tensor_tensor(
-                out=terms[t, d, b],
-                in0=window[t][:].indirect(offsets[d][:, 8 * b : 8 * (b + 1)]),
+                out=place,
+                in0=a[t][:].indirect(pos_t[d][:, 8 * b : 8 * (b + 1)]),
                 in1=picked[t, d][:, b * P : (b + 1) * P],
                 op=MULT,
             )
@@ -210,79 +147,9 @@ def tile_picked_ytri_gated_p_kernel(
                 in_=banks[bank][:, : len(tiles) * P].rearrange("p (m e i) -> p e m i", e=2, i=2),
             )
 
-        for u in range(2):
-            prepare_tile("scalar", ("w3", 0, 0), u)
-            one_pass(u, ("w3", u, 0), 0)
-        nc.vector.tensor_copy(out=x_codes[1][:], in_=x_all[1][:].indirect(offs_t[:]))
-        for u, engine in enumerate(("vector", "scalar")):
-            prepare_tile(engine, ("w3", 0, 1), u)
-            one_pass(u, ("w3", u, 1), 0)
-        for t in range(2):
-            copy_e(t, t)
-        prepare("vector", ("w1", 0, 0))
-        prepare("scalar", ("w1", 0, 1))
-        multiply("w1", 0, 2, 2)
-        prepare("scalar", ("w2", 0, 0))
-        prepare("vector", ("w2", 0, 1))
-        multiply("w2", 0, 2, 4)
-        make_gate(0, 2)
-        make_gate(1, 3)
-        prepare("gpsimd", ("w3", 2, 0), ("w2", 0, 1))
-        prepare("scalar", ("w3", 2, 1))
-        multiply("w3", 2, 2, 0)
-        prepare("scalar", ("w1", 2, 0))
-        for t in range(2, 4):
-            copy_e(t, t - 2)
-        prepare("vector", ("w1", 2, 1))
-        multiply("w1", 2, 2, 2)
-        prepare("scalar", ("w2", 2, 0))
-        prepare("vector", ("w2", 2, 1))
-        for u in range(2):
-            one_pass(6 + u, ("w2", 2, 0), u)
-            one_pass(6 + u, ("w2", 2, 1), u)
-        for t in range(2, 4):
-            make_gate(t, t)
-        fetch(ee, nxt_t, 0, 0, ("w1", 0, 0), 0)
-        fetch(ee, nxt_t, 0, 1, ("w1", 0, 0), 1)
-        fetch(ee, nxt_t, 1, 0, ("w1", 0, 0), 2)
-        fetch(ee, nxt_t, 1, 1, ("w2", 0, 1))
-        make_a(0, 4)
-        fetch_times(a, pos_t, 0, 0, ("w3", 2, 0), 0)
-        make_a(1, 5)
-        fetch_times(a, pos_t, 0, 1, ("w3", 2, 0), 1)
-        fetch_times(a, pos_t, 1, 0, ("w3", 2, 1), 0)
-        fetch_times(a, pos_t, 1, 1, ("w3", 2, 1), 1)
-        fetch(ee, nxt_t, 2, 0, ("w1", 2, 1), 0)
-        fetch(ee, nxt_t, 2, 1, ("w1", 2, 1), 1)
-        fetch(ee, nxt_t, 3, 0, ("w2", 2, 1), 0)
-        fetch(ee, nxt_t, 3, 1, ("w2", 2, 1), 1)
-        for g in range(PASSES):
-            prepare("scalar", ("w5", 0, g))
-        multiply("w5", 0, 1, 4)
-        gg = keep.tile([P, S], F32, name="gg")
-        nc.scalar.activation(out=gg[:], in_=banks[4][:], func=SIGMOID)
-        make_a(2, 6)
-        make_a(3, 7)
-        for b in range(2):
-            turn((0, 1), b, 2 + b)
-        for b in range(2):
-            for t in range(2, 4):
-                for d in range(2):
-                    fetch_times_half(a, pos_t, t, d, b)
-        w4_bf16 = picked[2, 1].bitcast(BF16)
-        nc.vector.tensor_copy(
-            out=w4_bf16.rearrange("p (c i j) -> p c j i", i=4, j=PACK),
-            in_=raw["w4", 0, 0][:].rearrange("p j (c i) -> p c j i", i=4),
-        )
-        picked_g = keep.tile([P, V], F32, name="picked_g")
-        nc.vector.tensor_copy(out=picked_g[:], in_=gg[:].indirect(own_t[:]))
-        w4_codes, w4_scales = quantize(w4_bf16, "w4")
-        for b in range(2):
-            for t in range(2, 4):
-                turn((t,), b, ((0, 1), (5, 6))[b][t - 2])
-        for b in range(2):
+        def finish(b, back_bank, rr_bank):
             z_words = z_rows[b][:].rearrange("p e m i -> p (e m i)").bitcast(F32)
-            back = banks[(5, 3)[b]][:, : 2 * P]
+            back = banks[back_bank][:, : 2 * P]
             for e in range(2):
                 nc.tensor.transpose(back[:, e * P : (e + 1) * P], z_words[:, e * P : (e + 1) * P], identity[:])
             z = keep.tile([P, P * PACK], BF16, name="z%d" % b, align_bytes=64)
@@ -291,11 +158,11 @@ def tile_picked_ytri_gated_p_kernel(
                 in_=back.rearrange("p (e v i) -> p v e i", e=2, i=2),
             )
             z_codes, z_scales = quantize(z[:], "z%d" % b)
-            rr = banks[(7, 4)[b]][:, :P]
+            rr = banks[rr_bank][:, :P]
             nc.tensor.matmul_mx(
                 out=rr,
-                lhsT=w4_codes[:].bitcast(FP8X4),
-                lhsT_scale=w4_scales[:],
+                lhsT=w4_planes[0][:].bitcast(FP8X4),
+                lhsT_scale=w4_planes[1][:],
                 rhs=z_codes[:].bitcast(FP8X4),
                 rhs_scale=z_scales[:],
                 start=True,
@@ -304,3 +171,131 @@ def tile_picked_ytri_gated_p_kernel(
             result = keep.tile([P, P], F32, name="result%d" % b)
             nc.vector.tensor_tensor(out=result[:], in0=rr, in1=picked_g[:, b * P : (b + 1) * P], op=MULT)
             nc.sync.dma_start(out=out[:, b * P : (b + 1) * P], in_=result[:])
+
+        x_all_scales = keep.tile([P, T], U8, name="x_all_scales")
+        nc.gpsimd.memset(x_all_scales[:].bitcast(I32), 0)
+        x_all = [load_words(0)]
+        offs_t = load_list(offs, "offs_t")
+        for q in range(4):
+            nc.sync.dma_start(
+                out=x_all_scales[32 * q : 32 * q + 4 * PASSES, :].bitcast(I32),
+                in_=x_scales[:, 4 * q : 4 * q + 4, :].bitcast(I32),
+            )
+        x_all.append(load_words(1))
+        warm = keep.tile([P, 1], F32, name="warm")
+        nc.vector.memset(warm[:], 0.0)
+        warm_out = keep.tile([P, 1], F32, name="warm_out")
+        nc.scalar.activation(out=warm_out[:], in_=warm[:], func=SIGMOID)
+        identity = keep.tile([P, P], F32, name="identity")
+        make_identity(nc, identity[:])
+
+        for g in range(PASSES):
+            load_weight(w3, "w3", g, 0, 2)
+        nxt_t = [load_list(nxt1, "nxt1_t"), load_list(nxt2, "nxt2_t")]
+        for g in range(PASSES):
+            load_weight(w3, "w3", g, 2, 4)
+        for w, name in ((w1, "w1"), (w2, "w2")):
+            for g in range(PASSES):
+                load_weight(w, name, g, 0, 2)
+        pos_t = [load_list(pos1, "pos1_t"), load_list(pos2, "pos2_t")]
+        for w, name in ((w1, "w1"), (w2, "w2")):
+            for g in range(PASSES):
+                load_weight(w, name, g, 2, 4)
+        w5_raw = keep.tile([P, PASSES, PACK * N], F32, name="w5_raw", align_bytes=64)
+        nc.sync.dma_start(out=w5_raw[:], in_=w5.rearrange("(g p j) c -> p g (j c)", g=PASSES, j=PACK))
+        load_weight(w4, "w4", 0, 0, 1)
+        own_t = load_list(own, "own_t")
+
+        x_scale = keep.tile([P, S], U8, name="x_scale", align_bytes=64)
+        x_codes = [keep.tile([P, S], U32, name="x_codes%d" % g, align_bytes=64) for g in range(PASSES)]
+        nc.vector.tensor_copy(out=x_codes[0][:], in_=x_all[0][:].indirect(offs_t[:]))
+        nc.vector.tensor_copy(out=x_scale[:], in_=x_all_scales[:].indirect(offs_t[:]))
+        nc.vector.tensor_copy(out=x_codes[1][:], in_=x_all[1][:].indirect(offs_t[:]))
+
+        arena = scratch("arena", 6 * PIECE_WORDS + 5 * LAP)
+        chain = [arena[:, 5 * LAP + n * (PIECE_WORDS - LAP) :][:, :PIECE_WORDS] for n in range(6)]
+        slot = [arena[:, n * V : (n + 1) * V] for n in range(12)]
+
+        first = {}
+        for g, u, engine in ((0, 0, "scalar"), (0, 1, "scalar"), (1, 0, "vector"), (1, 1, "scalar")):
+            first[g, u] = scratch("first%d%d" % (g, u), TILE_WORDS)
+            round_on(engine, raw["w3", 0, g][:, :, u * P : (u + 1) * P], first[g, u])
+        for g in range(PASSES):
+            for u in range(2):
+                one_pass(u, quantize(first[g, u].bitcast(BF16), "w3_first%d%d" % (g, u)), 0, g)
+        round_on("vector", raw["w3", 2, 0][:], chain[0])
+        copy_e(0, 0)
+        copy_e(1, 1)
+        multiply(("w3", 2, 0), chain[0], 2)
+        fetch(0, 0, slot[0])
+        fetch(0, 1, slot[1])
+        round_tile("gpsimd", ("w3", 2, 1), 0, chain[1])
+        round_tile("scalar", ("w3", 2, 1), 1, chain[1])
+        multiply(("w3", 2, 1), chain[1], 2)
+        fetch(1, 0, slot[2])
+        fetch(1, 1, slot[3])
+        round_tile("gpsimd", ("w1", 0, 0), 0, chain[2])
+        round_tile("scalar", ("w1", 0, 0), 1, chain[2])
+        copy_e(2, 2)
+        copy_e(3, 3)
+        multiply(("w1", 0, 0), chain[2], 4)
+        fetch(2, 0, slot[4])
+        fetch(2, 1, slot[5])
+        round_tile("gpsimd", ("w1", 0, 1), 0, chain[3])
+        round_tile("scalar", ("w1", 0, 1), 1, chain[3])
+        multiply(("w1", 0, 1), chain[3], 4)
+        fetch(3, 0, slot[6])
+        late = {key: scratch("%s_%d%d_stage" % key, PIECE_WORDS) for key in (("w2", 0, 0), ("w1", 2, 1), ("w2", 2, 0), ("w2", 2, 1))}
+        round_on("scalar", raw["w2", 0, 0][:], late["w2", 0, 0])
+        round_tile("gpsimd", ("w2", 0, 1), 0, chain[4])
+        round_tile("vector", ("w2", 0, 1), 1, chain[4])
+        multiply(("w2", 0, 0), late["w2", 0, 0], 6)
+        multiply(("w2", 0, 1), chain[4], 6)
+        for t in range(2):
+            make_gate(t, 4 + t, scratch("gate%d" % t, S))
+        fetch(3, 1, slot[8])
+        round_on("gpsimd", raw["w1", 2, 0][:], chain[5])
+        make_a(0, 6)
+        make_a(1, 7)
+        multiply(("w1", 2, 0), chain[5], 0)
+        fetch_times(0, 0, slot[11])
+        for key, bank, t, d in ((("w1", 2, 1), 0, 0, 1), (("w2", 2, 0), 2, 1, 0), (("w2", 2, 1), 2, 1, 1)):
+            round_on("scalar", raw[key][:], late[key])
+            multiply(key, late[key], bank)
+            fetch_times(t, d, late[key][:, :V])
+        last_raw = raw["w2", 2, 1][:].rearrange("p j c -> p (j c)")
+        for t in range(2, 4):
+            make_gate(t, t - 2, last_raw[:, (t - 2) * S : (t - 1) * S])
+        w5_stage = scratch("w5_stage", PIECE_WORDS)
+        for g in range(PASSES):
+            round_on(
+                "scalar",
+                w5_raw[:, g, :].rearrange("p (j c) -> p j c", j=PACK),
+                w5_stage[:, g * TILE_WORDS : (g + 1) * TILE_WORDS],
+            )
+        make_a(2, 2)
+        make_a(3, 3)
+        for b in range(2):
+            turn((0, 1), b, 5 + b)
+        fetch_times(2, 0, gate[3][:, :V])
+        w5_planes = quantize(w5_stage.bitcast(BF16), "w5")
+        for g in range(PASSES):
+            one_pass(4, w5_planes, g, g)
+        w4_stage = scratch("w4_stage", TILE_WORDS)
+        round_on("scalar", raw["w4", 0, 0][:], w4_stage)
+        fetch_times(2, 1, w5_stage[:, :V])
+        for d in range(2):
+            fetch_times_half(3, d, 0, w5_stage[:, V + d * P : V + (d + 1) * P])
+        for d in range(2):
+            fetch_times_half(3, d, 1, picked[2, 1][:, d * P : (d + 1) * P])
+        for b in range(2):
+            turn((2,), b, (7, 0)[b])
+        gg = keep.tile([P, S], F32, name="gg")
+        nc.scalar.activation(out=gg[:], in_=banks[4][:], func=SIGMOID)
+        for b in range(2):
+            turn((3,), b, (1, 2)[b])
+        w4_planes = quantize(w4_stage.bitcast(BF16), "w4")
+        picked_g = keep.tile([P, V], F32, name="picked_g")
+        nc.vector.tensor_copy(out=picked_g[:], in_=gg[:].indirect(own_t[:]))
+        finish(0, 3, 6)
+        finish(1, 5, 7)

@@ -14,7 +14,6 @@ U16 = mybir.dt.uint16
 U8 = mybir.dt.uint8
 FP8X4 = mybir.dt.float8_e4m3fn_x4
 MULT = mybir.AluOpType.mult
-ADD = mybir.AluOpType.add
 SIGMOID = mybir.ActivationFunctionType.Sigmoid
 
 P = 128
@@ -59,9 +58,7 @@ def tile_picked_ytri_gated_p_kernel(
         def round_on(engine, src, stage):
             grouped = stage.bitcast(BF16).rearrange("p (c j) -> p c j", j=PACK)
             if engine == "gpsimd":
-                nc.gpsimd.tensor_scalar(
-                    out=grouped, in0=src.rearrange("p j c -> p c j"), scalar1=1.0, scalar2=0.0, op0=MULT, op1=ADD
-                )
+                nc.gpsimd.tensor_copy(out=grouped, in_=src.rearrange("p j c -> p c j"))
                 return
             dst = grouped.rearrange("p (c i) j -> p c j i", i=4)
             src = src.rearrange("p j (c i) -> p c j i", i=4)

@@ -39,13 +39,16 @@ def tile_picked_ytri_gated_p_kernel(
             nc.sync.dma_start(out=tile[:], in_=dram)
             return tile
 
-        raw = {}
+        raw, stage = {}, {}
 
-        def load_weight(w, name, g, t0, t1):
+        def load_weight(w, name, g, t0, t1, place=None):
             tile = keep.tile([P, PACK, (t1 - t0) * P], F32, name="%s_raw%d%d" % (name, t0, g), align_bytes=64)
             rows = w[g * K_PASS : (g + 1) * K_PASS, :].rearrange("(p j) c -> p j c", j=PACK)
             nc.sync.dma_start(out=tile[:], in_=rows[:, :, t0 * P : t1 * P])
             raw[name, t0, g] = tile
+            if place is None:
+                place = scratch("%s_stage%d%d" % (name, t0, g), (t1 - t0) * TILE_WORDS)
+            stage[name, t0, g] = place
 
         def load_words(g):
             tile = keep.tile([P, T], U32, name="x_all_words%d" % g, align_bytes=64)
@@ -57,9 +60,6 @@ def tile_picked_ytri_gated_p_kernel(
 
         def round_on(engine, src, stage):
             grouped = stage.bitcast(BF16).rearrange("p (c j) -> p c j", j=PACK)
-            if engine == "gpsimd":
-                nc.gpsimd.tensor_copy(out=grouped, in_=src.rearrange("p j c -> p c j"))
-                return
             dst = grouped.rearrange("p (c i) j -> p c j i", i=4)
             src = src.rearrange("p j (c i) -> p c j i", i=4)
             if engine == "vector":
@@ -67,8 +67,13 @@ def tile_picked_ytri_gated_p_kernel(
             else:
                 nc.scalar.copy(out=dst, in_=src)
 
-        def round_tile(engine, key, u, stage):
-            round_on(engine, raw[key][:, :, u * P : (u + 1) * P], stage[:, u * TILE_WORDS : (u + 1) * TILE_WORDS])
+        def round_columns(engine, key, c0, c1):
+            round_on(engine, raw[key][:, :, c0:c1], stage[key][:, 2 * c0 : 2 * c1])
+
+        def round_shared(key):
+            round_columns("vector", key, 0, P // 2)
+            round_columns("vector", key, 3 * P // 2, 2 * P)
+            round_columns("scalar", key, P // 2, 3 * P // 2)
 
         def quantize(values, name):
             width = values.shape[1] // PACK
@@ -89,10 +94,21 @@ def tile_picked_ytri_gated_p_kernel(
                 stop=(g == PASSES - 1),
             )
 
-        def multiply(key, stage, first_bank):
-            planes = quantize(stage.bitcast(BF16), "%s_%d%d" % key)
-            for u in range(stage.shape[1] // TILE_WORDS):
+        def multiply(key, first_bank):
+            for u in range(2):
+                multiply_tile(key, u, first_bank + u)
+
+        def multiply_whole(key, first_bank):
+            planes = quantize(stage[key].bitcast(BF16), "%s_%d%d" % key)
+            for u in range(2):
                 one_pass(first_bank + u, planes, u, key[2])
+
+        def multiply_tile(key, u, bank):
+            values = stage[key][:, u * TILE_WORDS : (u + 1) * TILE_WORDS].bitcast(BF16)
+            one_pass(bank, quantize(values, "%s_%d%d" % key + "_%d" % u), 0, key[2])
+
+        def behind(key, u):
+            return stage[key][:, u * V : (u + 1) * V]
 
         ee, gate, a, picked, terms = {}, {}, {}, {}, {}
 
@@ -178,6 +194,7 @@ def tile_picked_ytri_gated_p_kernel(
                 out=x_all_scales[32 * q : 32 * q + 4 * PASSES, :].bitcast(I32),
                 in_=x_scales[:, 4 * q : 4 * q + 4, :].bitcast(I32),
             )
+        load_weight(w3, "w3", 0, 0, 2)
         x_all.append(load_words(1))
         warm = keep.tile([P, 1], F32, name="warm")
         nc.vector.memset(warm[:], 0.0)
@@ -186,18 +203,20 @@ def tile_picked_ytri_gated_p_kernel(
         identity = keep.tile([P, P], F32, name="identity")
         make_identity(nc, identity[:])
 
-        for g in range(PASSES):
-            load_weight(w3, "w3", g, 0, 2)
-        nxt_t = [load_list(nxt1, "nxt1_t"), load_list(nxt2, "nxt2_t")]
-        for g in range(PASSES):
-            load_weight(w3, "w3", g, 2, 4)
+        for t in range(2):
+            load_weight(w3, "w3", 1, t, t + 1)
+        load_weight(w3, "w3", 0, 2, 4)
+        nxt_t = [load_list(nxt2, "nxt2_t"), load_list(nxt1, "nxt1_t")][::-1]
+        load_weight(w3, "w3", 1, 2, 4)
         for w, name in ((w1, "w1"), (w2, "w2")):
             for g in range(PASSES):
                 load_weight(w, name, g, 0, 2)
         pos_t = [load_list(pos1, "pos1_t"), load_list(pos2, "pos2_t")]
-        for w, name in ((w1, "w1"), (w2, "w2")):
-            for g in range(PASSES):
-                load_weight(w, name, g, 2, 4)
+        pair = scratch("pair", 2 * PIECE_WORDS - LAP)
+        for g in range(PASSES):
+            load_weight(w1, "w1", g, 2, 4)
+        load_weight(w2, "w2", 0, 2, 4)
+        load_weight(w2, "w2", 1, 2, 4, pair[:, :PIECE_WORDS])
         w5_raw = keep.tile([P, PASSES, PACK * N], F32, name="w5_raw", align_bytes=64)
         nc.sync.dma_start(out=w5_raw[:], in_=w5.rearrange("(g p j) c -> p g (j c)", g=PASSES, j=PACK))
         load_weight(w4, "w4", 0, 0, 1)
@@ -207,92 +226,75 @@ def tile_picked_ytri_gated_p_kernel(
         x_codes = [keep.tile([P, S], U32, name="x_codes%d" % g, align_bytes=64) for g in range(PASSES)]
         nc.vector.tensor_copy(out=x_codes[0][:], in_=x_all[0][:].indirect(offs_t[:]))
         nc.vector.tensor_copy(out=x_scale[:], in_=x_all_scales[:].indirect(offs_t[:]))
+        for u in range(2):
+            round_columns("scalar", ("w3", 0, 0), u * P, (u + 1) * P)
+        multiply(("w3", 0, 0), 0)
         nc.vector.tensor_copy(out=x_codes[1][:], in_=x_all[1][:].indirect(offs_t[:]))
-
-        arena = scratch("arena", 6 * PIECE_WORDS + 5 * LAP)
-        chain = [arena[:, 5 * LAP + n * (PIECE_WORDS - LAP) :][:, :PIECE_WORDS] for n in range(6)]
-        slot = [arena[:, n * V : (n + 1) * V] for n in range(12)]
-
-        first = {}
-        for g, u, engine in ((0, 0, "scalar"), (0, 1, "scalar"), (1, 0, "vector"), (1, 1, "scalar")):
-            first[g, u] = scratch("first%d%d" % (g, u), TILE_WORDS)
-            round_on(engine, raw["w3", 0, g][:, :, u * P : (u + 1) * P], first[g, u])
-        for g in range(PASSES):
-            for u in range(2):
-                one_pass(u, quantize(first[g, u].bitcast(BF16), "w3_first%d%d" % (g, u)), 0, g)
-        round_on("vector", raw["w3", 2, 0][:], chain[0])
+        for t, engine in enumerate(("vector", "scalar")):
+            round_columns(engine, ("w3", t, 1), 0, P)
+            multiply_tile(("w3", t, 1), 0, t)
+        round_columns("vector", ("w3", 2, 0), 0, 2 * P)
         copy_e(0, 0)
+        multiply_whole(("w3", 2, 0), 2)
+        round_shared(("w3", 2, 1))
         copy_e(1, 1)
-        multiply(("w3", 2, 0), chain[0], 2)
-        fetch(0, 0, slot[0])
-        fetch(0, 1, slot[1])
-        round_tile("gpsimd", ("w3", 2, 1), 0, chain[1])
-        round_tile("scalar", ("w3", 2, 1), 1, chain[1])
-        multiply(("w3", 2, 1), chain[1], 2)
-        fetch(1, 0, slot[2])
-        fetch(1, 1, slot[3])
-        round_tile("gpsimd", ("w1", 0, 0), 0, chain[2])
-        round_tile("scalar", ("w1", 0, 0), 1, chain[2])
+        fetch(0, 0, scratch("picked00", V))
+        multiply(("w3", 2, 1), 2)
+        fetch(0, 1, behind(("w3", 2, 1), 0))
+        fetch(1, 0, behind(("w3", 2, 1), 1))
+        round_columns("scalar", ("w1", 0, 0), 0, 2 * P)
+        multiply(("w1", 0, 0), 4)
+        fetch(1, 1, behind(("w1", 0, 0), 0))
         copy_e(2, 2)
+        round_shared(("w1", 0, 1))
         copy_e(3, 3)
-        multiply(("w1", 0, 0), chain[2], 4)
-        fetch(2, 0, slot[4])
-        fetch(2, 1, slot[5])
-        round_tile("gpsimd", ("w1", 0, 1), 0, chain[3])
-        round_tile("scalar", ("w1", 0, 1), 1, chain[3])
-        multiply(("w1", 0, 1), chain[3], 4)
-        fetch(3, 0, slot[6])
-        late = {key: scratch("%s_%d%d_stage" % key, PIECE_WORDS) for key in (("w2", 0, 0), ("w1", 2, 1), ("w2", 2, 0), ("w2", 2, 1))}
-        round_on("scalar", raw["w2", 0, 0][:], late["w2", 0, 0])
-        round_tile("gpsimd", ("w2", 0, 1), 0, chain[4])
-        round_tile("vector", ("w2", 0, 1), 1, chain[4])
-        multiply(("w2", 0, 0), late["w2", 0, 0], 6)
-        multiply(("w2", 0, 1), chain[4], 6)
+        fetch(2, 0, behind(("w1", 0, 0), 1))
+        multiply(("w1", 0, 1), 4)
+        fetch(2, 1, behind(("w1", 0, 1), 0))
+        round_columns("scalar", ("w2", 0, 0), 0, 2 * P)
+        round_columns("vector", ("w2", 0, 1), 0, 2 * P)
+        multiply_whole(("w2", 0, 0), 6)
+        multiply(("w2", 0, 1), 6)
         for t in range(2):
             make_gate(t, 4 + t, scratch("gate%d" % t, S))
-        fetch(3, 1, slot[8])
-        round_on("gpsimd", raw["w1", 2, 0][:], chain[5])
+        for d in range(2):
+            fetch(3, d, behind(("w2", 0, 1), d))
         make_a(0, 6)
         make_a(1, 7)
-        multiply(("w1", 2, 0), chain[5], 0)
-        fetch_times(0, 0, slot[11])
-        for key, bank, t, d in ((("w1", 2, 1), 0, 0, 1), (("w2", 2, 0), 2, 1, 0), (("w2", 2, 1), 2, 1, 1)):
-            round_on("scalar", raw[key][:], late[key])
-            multiply(key, late[key], bank)
-            fetch_times(t, d, late[key][:, :V])
+        for key, bank, t, d in ((("w1", 2, 0), 0, 0, 0), (("w1", 2, 1), 0, 0, 1), (("w2", 2, 0), 2, 1, 0), (("w2", 2, 1), 2, 1, 1)):
+            round_columns("scalar", key, 0, 2 * P)
+            multiply(key, bank)
+            fetch_times(t, d, behind(key, 0))
         last_raw = raw["w2", 2, 1][:].rearrange("p j c -> p (j c)")
         for t in range(2, 4):
             make_gate(t, t - 2, last_raw[:, (t - 2) * S : (t - 1) * S])
-        w5_stage = scratch("w5_stage", PIECE_WORDS)
-        for g in range(PASSES):
-            round_on(
-                "scalar",
-                w5_raw[:, g, :].rearrange("p (j c) -> p j c", j=PACK),
-                w5_stage[:, g * TILE_WORDS : (g + 1) * TILE_WORDS],
-            )
+        w5_stage = pair[:, PIECE_WORDS - LAP :]
+        nc.scalar.copy(
+            out=w5_stage.bitcast(BF16).rearrange("p (g c i j) -> p g c j i", g=PASSES, i=4, j=PACK),
+            in_=w5_raw[:].rearrange("p g (j c i) -> p g c j i", j=PACK, i=4),
+        )
         make_a(2, 2)
         make_a(3, 3)
         for b in range(2):
-            turn((0, 1), b, 5 + b)
-        fetch_times(2, 0, gate[3][:, :V])
-        w5_planes = quantize(w5_stage.bitcast(BF16), "w5")
+            turn((0, 1), b, b)
+        fetch_times(2, 0, scratch("term20", V))
         for g in range(PASSES):
-            one_pass(4, w5_planes, g, g)
-        w4_stage = scratch("w4_stage", TILE_WORDS)
-        round_on("scalar", raw["w4", 0, 0][:], w4_stage)
+            values = w5_stage[:, g * TILE_WORDS : (g + 1) * TILE_WORDS].bitcast(BF16)
+            one_pass(4, quantize(values, "w5_%d" % g), 0, g)
+        round_columns("scalar", ("w4", 0, 0), 0, P)
         fetch_times(2, 1, w5_stage[:, :V])
         for d in range(2):
             fetch_times_half(3, d, 0, w5_stage[:, V + d * P : V + (d + 1) * P])
         for d in range(2):
             fetch_times_half(3, d, 1, picked[2, 1][:, d * P : (d + 1) * P])
         for b in range(2):
-            turn((2,), b, (7, 0)[b])
+            turn((2,), b, 5 + b)
         gg = keep.tile([P, S], F32, name="gg")
         nc.scalar.activation(out=gg[:], in_=banks[4][:], func=SIGMOID)
         for b in range(2):
-            turn((3,), b, (1, 2)[b])
-        w4_planes = quantize(w4_stage.bitcast(BF16), "w4")
+            turn((3,), b, (7, 2)[b])
+        w4_planes = quantize(stage["w4", 0, 0].bitcast(BF16), "w4")
         picked_g = keep.tile([P, V], F32, name="picked_g")
         nc.vector.tensor_copy(out=picked_g[:], in_=gg[:].indirect(own_t[:]))
-        finish(0, 3, 6)
-        finish(1, 5, 7)
+        finish(0, 3, 1)
+        finish(1, 0, 5)

@@ -22,7 +22,6 @@ K_PASS = P * PACK
 PASSES = K // K_PASS
 TILE_WORDS = P * PACK // 2
 PIECE_WORDS = 2 * TILE_WORDS
-LAP = 16
 
 
 def tile_picked_ytri_gated_p_kernel(
@@ -41,14 +40,15 @@ def tile_picked_ytri_gated_p_kernel(
 
         raw, stage = {}, {}
 
-        def load_weight(w, name, g, t0, t1, place=None):
+        def load_weight(w, name, g, t0, t1):
             tile = keep.tile([P, PACK, (t1 - t0) * P], F32, name="%s_raw%d%d" % (name, t0, g), align_bytes=64)
             rows = w[g * K_PASS : (g + 1) * K_PASS, :].rearrange("(p j) c -> p j c", j=PACK)
             nc.sync.dma_start(out=tile[:], in_=rows[:, :, t0 * P : t1 * P])
-            raw[name, t0, g] = tile
-            if place is None:
-                place = scratch("%s_stage%d%d" % (name, t0, g), (t1 - t0) * TILE_WORDS)
-            stage[name, t0, g] = place
+            for t in range(t0, t1):
+                raw[name, g, t] = (tile, t0 * P)
+            for h in range(t0 // 2, (t1 + 1) // 2):
+                if (name, g, h) not in stage:
+                    stage[name, g, h] = scratch("%s_stage%d%d" % (name, g, h), min(2, w.shape[1] // P) * TILE_WORDS)
 
         def load_words(g):
             tile = keep.tile([P, T], U32, name="x_all_words%d" % g, align_bytes=64)
@@ -68,12 +68,16 @@ def tile_picked_ytri_gated_p_kernel(
                 nc.scalar.copy(out=dst, in_=src)
 
         def round_columns(engine, key, c0, c1):
-            round_on(engine, raw[key][:, :, c0:c1], stage[key][:, 2 * c0 : 2 * c1])
+            tile, first = raw[key + (c0 // P,)]
+            h = c0 // (2 * P)
+            place = stage[key + (h,)][:, 2 * c0 - h * PIECE_WORDS : 2 * c1 - h * PIECE_WORDS]
+            round_on(engine, tile[:, :, c0 - first : c1 - first], place)
 
-        def round_shared(key):
-            round_columns("vector", key, 0, P // 2)
-            round_columns("vector", key, 3 * P // 2, 2 * P)
-            round_columns("scalar", key, P // 2, 3 * P // 2)
+        def round_shared(key, t0):
+            c0 = t0 * P
+            round_columns("vector", key, c0, c0 + P // 2)
+            round_columns("vector", key, c0 + 3 * P // 2, c0 + 2 * P)
+            round_columns("scalar", key, c0 + P // 2, c0 + 3 * P // 2)
 
         def quantize(values, name):
             width = values.shape[1] // PACK
@@ -94,21 +98,14 @@ def tile_picked_ytri_gated_p_kernel(
                 stop=(g == PASSES - 1),
             )
 
-        def multiply(key, first_bank):
-            for u in range(2):
-                multiply_tile(key, u, first_bank + u)
+        def multiply(key, t0, t1, first_bank):
+            values = stage[key + (t0 // 2,)][:, t0 % 2 * TILE_WORDS : ((t1 - 1) % 2 + 1) * TILE_WORDS].bitcast(BF16)
+            planes = quantize(values, "%s_%d" % key + "_%d" % t0)
+            for t in range(t0, t1):
+                one_pass(first_bank + t, planes, t - t0, key[1])
 
-        def multiply_whole(key, first_bank):
-            planes = quantize(stage[key].bitcast(BF16), "%s_%d%d" % key)
-            for u in range(2):
-                one_pass(first_bank + u, planes, u, key[2])
-
-        def multiply_tile(key, u, bank):
-            values = stage[key][:, u * TILE_WORDS : (u + 1) * TILE_WORDS].bitcast(BF16)
-            one_pass(bank, quantize(values, "%s_%d%d" % key + "_%d" % u), 0, key[2])
-
-        def behind(key, u):
-            return stage[key][:, u * V : (u + 1) * V]
+        def behind(key, t):
+            return stage[key + (t // 2,)][:, t % 2 * V : (t % 2 + 1) * V]
 
         ee, gate, a, picked, terms = {}, {}, {}, {}, {}
 
@@ -203,20 +200,19 @@ def tile_picked_ytri_gated_p_kernel(
         identity = keep.tile([P, P], F32, name="identity")
         make_identity(nc, identity[:])
 
-        for t in range(2):
-            load_weight(w3, "w3", 1, t, t + 1)
+        load_weight(w3, "w3", 1, 0, 2)
         load_weight(w3, "w3", 0, 2, 4)
         nxt_t = [load_list(nxt2, "nxt2_t"), load_list(nxt1, "nxt1_t")][::-1]
         load_weight(w3, "w3", 1, 2, 4)
-        for w, name in ((w1, "w1"), (w2, "w2")):
-            for g in range(PASSES):
-                load_weight(w, name, g, 0, 2)
+        for g in range(PASSES):
+            load_weight(w1, "w1", g, 0, 2)
+        for g in range(PASSES):
+            load_weight(w2, "w2", g, 0, 2)
         pos_t = [load_list(pos1, "pos1_t"), load_list(pos2, "pos2_t")]
-        pair = scratch("pair", 2 * PIECE_WORDS - LAP)
         for g in range(PASSES):
             load_weight(w1, "w1", g, 2, 4)
-        load_weight(w2, "w2", 0, 2, 4)
-        load_weight(w2, "w2", 1, 2, 4, pair[:, :PIECE_WORDS])
+        for g in range(PASSES):
+            load_weight(w2, "w2", g, 2, 4)
         w5_raw = keep.tile([P, PASSES, PACK * N], F32, name="w5_raw", align_bytes=64)
         nc.sync.dma_start(out=w5_raw[:], in_=w5.rearrange("(g p j) c -> p g (j c)", g=PASSES, j=PACK))
         load_weight(w4, "w4", 0, 0, 1)
@@ -226,49 +222,66 @@ def tile_picked_ytri_gated_p_kernel(
         x_codes = [keep.tile([P, S], U32, name="x_codes%d" % g, align_bytes=64) for g in range(PASSES)]
         nc.vector.tensor_copy(out=x_codes[0][:], in_=x_all[0][:].indirect(offs_t[:]))
         nc.vector.tensor_copy(out=x_scale[:], in_=x_all_scales[:].indirect(offs_t[:]))
-        for u in range(2):
-            round_columns("scalar", ("w3", 0, 0), u * P, (u + 1) * P)
-        multiply(("w3", 0, 0), 0)
+        for t in range(2):
+            round_columns("scalar", ("w3", 0), t * P, (t + 1) * P)
+            multiply(("w3", 0), t, t + 1, 0)
         nc.vector.tensor_copy(out=x_codes[1][:], in_=x_all[1][:].indirect(offs_t[:]))
         for t, engine in enumerate(("vector", "scalar")):
-            round_columns(engine, ("w3", t, 1), 0, P)
-            multiply_tile(("w3", t, 1), 0, t)
-        round_columns("vector", ("w3", 2, 0), 0, 2 * P)
+            round_columns(engine, ("w3", 1), t * P, (t + 1) * P)
+            multiply(("w3", 1), t, t + 1, 0)
+        for t in range(2, 4):
+            round_columns("vector", ("w3", 0), t * P, (t + 1) * P)
         copy_e(0, 0)
-        multiply_whole(("w3", 2, 0), 2)
-        round_shared(("w3", 2, 1))
+        for t in range(2, 4):
+            multiply(("w3", 0), t, t + 1, 0)
+        round_shared(("w3", 1), 2)
         copy_e(1, 1)
         fetch(0, 0, scratch("picked00", V))
-        multiply(("w3", 2, 1), 2)
-        fetch(0, 1, behind(("w3", 2, 1), 0))
-        fetch(1, 0, behind(("w3", 2, 1), 1))
-        round_columns("scalar", ("w1", 0, 0), 0, 2 * P)
-        multiply(("w1", 0, 0), 4)
-        fetch(1, 1, behind(("w1", 0, 0), 0))
+        for t in range(2, 4):
+            multiply(("w3", 1), t, t + 1, 0)
+        fetch(0, 1, behind(("w3", 1), 2))
+        fetch(1, 0, behind(("w3", 1), 3))
+        round_columns("scalar", ("w1", 0), 0, 2 * P)
+        for t in range(2):
+            multiply(("w1", 0), t, t + 1, 4)
+        fetch(1, 1, behind(("w1", 0), 0))
         copy_e(2, 2)
-        round_shared(("w1", 0, 1))
+        round_shared(("w1", 1), 0)
         copy_e(3, 3)
-        fetch(2, 0, behind(("w1", 0, 0), 1))
-        multiply(("w1", 0, 1), 4)
-        fetch(2, 1, behind(("w1", 0, 1), 0))
-        round_columns("scalar", ("w2", 0, 0), 0, 2 * P)
-        round_columns("vector", ("w2", 0, 1), 0, 2 * P)
-        multiply_whole(("w2", 0, 0), 6)
-        multiply(("w2", 0, 1), 6)
+        fetch(2, 0, behind(("w1", 0), 1))
+        for t in range(2):
+            multiply(("w1", 1), t, t + 1, 4)
+        fetch(2, 1, behind(("w1", 1), 0))
+        round_columns("scalar", ("w2", 0), 0, 2 * P)
+        round_columns("vector", ("w2", 1), 0, 2 * P)
+        multiply(("w2", 0), 0, 2, 0)
+        for t in range(2):
+            multiply(("w2", 1), t, t + 1, 0)
         for t in range(2):
             make_gate(t, 4 + t, scratch("gate%d" % t, S))
         for d in range(2):
-            fetch(3, d, behind(("w2", 0, 1), d))
-        make_a(0, 6)
-        make_a(1, 7)
-        for key, bank, t, d in ((("w1", 2, 0), 0, 0, 0), (("w1", 2, 1), 0, 0, 1), (("w2", 2, 0), 2, 1, 0), (("w2", 2, 1), 2, 1, 1)):
-            round_columns("scalar", key, 0, 2 * P)
-            multiply(key, bank)
-            fetch_times(t, d, behind(key, 0))
-        last_raw = raw["w2", 2, 1][:].rearrange("p j c -> p (j c)")
+            fetch(3, d, behind(("w2", 1), d))
+        make_a(0, 0)
+        make_a(1, 1)
+        round_columns("scalar", ("w1", 0), 2 * P, 4 * P)
         for t in range(2, 4):
-            make_gate(t, t - 2, last_raw[:, (t - 2) * S : (t - 1) * S])
-        w5_stage = pair[:, PIECE_WORDS - LAP :]
+            multiply(("w1", 0), t, t + 1, 4)
+        fetch_times(0, 0, behind(("w1", 0), 2))
+        round_shared(("w1", 1), 2)
+        for t in range(2, 4):
+            multiply(("w1", 1), t, t + 1, 4)
+        fetch_times(0, 1, behind(("w1", 1), 2))
+        round_columns("scalar", ("w2", 0), 2 * P, 4 * P)
+        for t in range(2, 4):
+            multiply(("w2", 0), t, t + 1, 0)
+        fetch_times(1, 0, behind(("w2", 0), 2))
+        round_shared(("w2", 1), 2)
+        for t in range(2, 4):
+            multiply(("w2", 1), t, t + 1, 0)
+        fetch_times(1, 1, behind(("w2", 1), 2))
+        for t in range(2, 4):
+            make_gate(t, 4 + t, raw["w2", 0, 2][0][:].rearrange("p j c -> p (j c)")[:, (t - 2) * S : (t - 1) * S])
+        w5_stage = scratch("w5_stage", PIECE_WORDS)
         nc.scalar.copy(
             out=w5_stage.bitcast(BF16).rearrange("p (g c i j) -> p g c j i", g=PASSES, i=4, j=PACK),
             in_=w5_raw[:].rearrange("p g (j c i) -> p g c j i", j=PACK, i=4),
@@ -276,25 +289,24 @@ def tile_picked_ytri_gated_p_kernel(
         make_a(2, 2)
         make_a(3, 3)
         for b in range(2):
-            turn((0, 1), b, b)
-        fetch_times(2, 0, scratch("term20", V))
+            turn((0, 1), b, 6 + b)
         for g in range(PASSES):
             values = w5_stage[:, g * TILE_WORDS : (g + 1) * TILE_WORDS].bitcast(BF16)
             one_pass(4, quantize(values, "w5_%d" % g), 0, g)
-        round_columns("scalar", ("w4", 0, 0), 0, P)
-        fetch_times(2, 1, w5_stage[:, :V])
+        round_columns("scalar", ("w4", 0), 0, P)
         for d in range(2):
-            fetch_times_half(3, d, 0, w5_stage[:, V + d * P : V + (d + 1) * P])
-        for d in range(2):
-            fetch_times_half(3, d, 1, picked[2, 1][:, d * P : (d + 1) * P])
+            fetch_times(2, d, w5_stage[:, d * V : (d + 1) * V])
         for b in range(2):
-            turn((2,), b, 5 + b)
+            for d in range(2):
+                fetch_times_half(3, d, b, picked[2, b][:, d * P : (d + 1) * P])
+        for b in range(2):
+            turn((2,), b, b)
         gg = keep.tile([P, S], F32, name="gg")
         nc.scalar.activation(out=gg[:], in_=banks[4][:], func=SIGMOID)
         for b in range(2):
-            turn((3,), b, (7, 2)[b])
+            turn((3,), b, (5, 2)[b])
         w4_planes = quantize(stage["w4", 0, 0].bitcast(BF16), "w4")
         picked_g = keep.tile([P, V], F32, name="picked_g")
         nc.vector.tensor_copy(out=picked_g[:], in_=gg[:].indirect(own_t[:]))
-        finish(0, 3, 1)
-        finish(1, 0, 5)
+        finish(0, 3, 6)
+        finish(1, 7, 0)

@@ -73,12 +73,6 @@ def tile_picked_ytri_gated_p_kernel(
             place = stage[key + (h,)][:, 2 * c0 - h * PIECE_WORDS : 2 * c1 - h * PIECE_WORDS]
             round_on(engine, tile[:, :, c0 - first : c1 - first], place)
 
-        def round_shared(key, t0):
-            c0 = t0 * P
-            round_columns("vector", key, c0, c0 + P // 2)
-            round_columns("vector", key, c0 + 3 * P // 2, c0 + 2 * P)
-            round_columns("scalar", key, c0 + P // 2, c0 + 3 * P // 2)
-
         def quantize(values, name):
             width = values.shape[1] // PACK
             codes = keep.tile([P, width], U32, name=name + "_codes", align_bytes=64)
@@ -104,8 +98,8 @@ def tile_picked_ytri_gated_p_kernel(
             for t in range(t0, t1):
                 one_pass(first_bank + t, planes, t - t0, key[1])
 
-        def behind(key, t):
-            return stage[key + (t // 2,)][:, t % 2 * V : (t % 2 + 1) * V]
+        def after(key, t0, row):
+            return raw[key + (t0,)][0][:, row, :V]
 
         ee, gate, a, picked, terms = {}, {}, {}, {}, {}
 
@@ -229,58 +223,48 @@ def tile_picked_ytri_gated_p_kernel(
         for t, engine in enumerate(("vector", "scalar")):
             round_columns(engine, ("w3", 1), t * P, (t + 1) * P)
             multiply(("w3", 1), t, t + 1, 0)
-        for t in range(2, 4):
-            round_columns("vector", ("w3", 0), t * P, (t + 1) * P)
+        round_columns("vector", ("w3", 0), 2 * P, 4 * P)
         copy_e(0, 0)
-        for t in range(2, 4):
-            multiply(("w3", 0), t, t + 1, 0)
-        round_shared(("w3", 1), 2)
         copy_e(1, 1)
         fetch(0, 0, scratch("picked00", V))
-        for t in range(2, 4):
-            multiply(("w3", 1), t, t + 1, 0)
-        fetch(0, 1, behind(("w3", 1), 2))
-        fetch(1, 0, behind(("w3", 1), 3))
+        multiply(("w3", 0), 2, 4, 0)
+        round_columns("scalar", ("w3", 1), 2 * P, 4 * P)
+        fetch(0, 1, scratch("picked01", V))
+        multiply(("w3", 1), 2, 4, 0)
+        fetch(1, 0, after(("w3", 1), 2, 0))
+        fetch(1, 1, after(("w3", 1), 2, 1))
         round_columns("scalar", ("w1", 0), 0, 2 * P)
-        for t in range(2):
-            multiply(("w1", 0), t, t + 1, 4)
-        fetch(1, 1, behind(("w1", 0), 0))
+        round_columns("vector", ("w1", 1), 0, 2 * P)
+        multiply(("w1", 0), 0, 2, 4)
+        multiply(("w1", 1), 0, 2, 4)
         copy_e(2, 2)
-        round_shared(("w1", 1), 0)
         copy_e(3, 3)
-        fetch(2, 0, behind(("w1", 0), 1))
-        for t in range(2):
-            multiply(("w1", 1), t, t + 1, 4)
-        fetch(2, 1, behind(("w1", 1), 0))
+        fetch(2, 0, scratch("picked20", V))
+        fetch(2, 1, scratch("picked21", V))
         round_columns("scalar", ("w2", 0), 0, 2 * P)
         round_columns("vector", ("w2", 1), 0, 2 * P)
         multiply(("w2", 0), 0, 2, 0)
-        for t in range(2):
-            multiply(("w2", 1), t, t + 1, 0)
-        for t in range(2):
-            make_gate(t, 4 + t, scratch("gate%d" % t, S))
-        for d in range(2):
-            fetch(3, d, behind(("w2", 1), d))
+        multiply(("w2", 1), 0, 2, 0)
+        make_gate(0, 4, raw[("w1", 0) + (0,)][0][:, 0 : 2, :].rearrange("p j c -> p (j c)"))
+        make_gate(1, 5, raw[("w1", 0) + (0,)][0][:, 2 : 4, :].rearrange("p j c -> p (j c)"))
+        fetch(3, 0, after(("w2", 0), 0, 0))
+        fetch(3, 1, after(("w2", 0), 0, 1))
         make_a(0, 0)
         make_a(1, 1)
         round_columns("scalar", ("w1", 0), 2 * P, 4 * P)
-        for t in range(2, 4):
-            multiply(("w1", 0), t, t + 1, 4)
-        fetch_times(0, 0, behind(("w1", 0), 2))
-        round_shared(("w1", 1), 2)
-        for t in range(2, 4):
-            multiply(("w1", 1), t, t + 1, 4)
-        fetch_times(0, 1, behind(("w1", 1), 2))
+        multiply(("w1", 0), 2, 4, 4)
+        fetch_times(0, 0, after(("w1", 0), 2, 0))
+        round_columns("scalar", ("w1", 1), 2 * P, 4 * P)
+        multiply(("w1", 1), 2, 4, 4)
+        fetch_times(0, 1, after(("w1", 1), 2, 0))
         round_columns("scalar", ("w2", 0), 2 * P, 4 * P)
-        for t in range(2, 4):
-            multiply(("w2", 0), t, t + 1, 0)
-        fetch_times(1, 0, behind(("w2", 0), 2))
-        round_shared(("w2", 1), 2)
-        for t in range(2, 4):
-            multiply(("w2", 1), t, t + 1, 0)
-        fetch_times(1, 1, behind(("w2", 1), 2))
-        for t in range(2, 4):
-            make_gate(t, 4 + t, raw["w2", 0, 2][0][:].rearrange("p j c -> p (j c)")[:, (t - 2) * S : (t - 1) * S])
+        multiply(("w2", 0), 2, 4, 0)
+        fetch_times(1, 0, after(("w2", 0), 2, 0))
+        round_columns("scalar", ("w2", 1), 2 * P, 4 * P)
+        multiply(("w2", 1), 2, 4, 0)
+        fetch_times(1, 1, after(("w2", 1), 2, 0))
+        make_gate(2, 6, raw[("w2", 0) + (2,)][0][:, 2 : 4, :].rearrange("p j c -> p (j c)"))
+        make_gate(3, 7, raw[("w2", 1) + (2,)][0][:, 2 : 4, :].rearrange("p j c -> p (j c)"))
         w5_stage = scratch("w5_stage", PIECE_WORDS)
         nc.scalar.copy(
             out=w5_stage.bitcast(BF16).rearrange("p (g c i j) -> p g c j i", g=PASSES, i=4, j=PACK),
@@ -290,15 +274,15 @@ def tile_picked_ytri_gated_p_kernel(
         make_a(3, 3)
         for b in range(2):
             turn((0, 1), b, 6 + b)
+        w5_planes = quantize(w5_stage.bitcast(BF16), "w5")
         for g in range(PASSES):
-            values = w5_stage[:, g * TILE_WORDS : (g + 1) * TILE_WORDS].bitcast(BF16)
-            one_pass(4, quantize(values, "w5_%d" % g), 0, g)
+            one_pass(4, w5_planes, g, g)
         round_columns("scalar", ("w4", 0), 0, P)
         for d in range(2):
-            fetch_times(2, d, w5_stage[:, d * V : (d + 1) * V])
+            fetch_times(2, d, w5_raw[:, 0, d * V : (d + 1) * V])
         for b in range(2):
             for d in range(2):
-                fetch_times_half(3, d, b, picked[2, b][:, d * P : (d + 1) * P])
+                fetch_times_half(3, d, b, w5_raw[:, 1, (2 * b + d) * P : (2 * b + d + 1) * P])
         for b in range(2):
             turn((2,), b, b)
         gg = keep.tile([P, S], F32, name="gg")

@@ -60,8 +60,9 @@ def tile_picked_ytri_gated_p_kernel(
 
         def round_on(engine, src, stage):
             grouped = stage.bitcast(BF16).rearrange("p (c j) -> p c j", j=PACK)
-            dst = grouped.rearrange("p (c i) j -> p c j i", i=4)
-            src = src.rearrange("p j (c i) -> p c j i", i=4)
+            run = 4 if engine == "vector" else 2
+            dst = grouped.rearrange("p (c i) j -> p c j i", i=run)
+            src = src.rearrange("p j (c i) -> p c j i", i=run)
             if engine == "vector":
                 nc.vector.tensor_copy(out=dst, in_=src)
             else:
@@ -267,8 +268,8 @@ def tile_picked_ytri_gated_p_kernel(
         make_gate(3, 7, raw[("w2", 1) + (2,)][0][:, 2 : 4, :].rearrange("p j c -> p (j c)"))
         w5_stage = scratch("w5_stage", PIECE_WORDS)
         nc.scalar.copy(
-            out=w5_stage.bitcast(BF16).rearrange("p (g c i j) -> p g c j i", g=PASSES, i=4, j=PACK),
-            in_=w5_raw[:].rearrange("p g (j c i) -> p g c j i", j=PACK, i=4),
+            out=w5_stage.bitcast(BF16).rearrange("p (g c i j) -> p g c j i", g=PASSES, i=2, j=PACK),
+            in_=w5_raw[:].rearrange("p g (j c i) -> p g c j i", j=PACK, i=2),
         )
         make_a(2, 2)
         make_a(3, 3)

@@ -195,9 +195,10 @@ def tile_picked_ytri_gated_p_kernel(
         identity = keep.tile([P, P], F32, name="identity")
         make_identity(nc, identity[:])
 
-        load_weight(w3, "w3", 1, 0, 2)
+        for t in range(2):
+            load_weight(w3, "w3", 1, t, t + 1)
         load_weight(w3, "w3", 0, 2, 4)
-        nxt_t = [load_list(nxt2, "nxt2_t"), load_list(nxt1, "nxt1_t")][::-1]
+        nxt_t = [load_list(nxt1, "nxt1_t"), load_list(nxt2, "nxt2_t")]
         load_weight(w3, "w3", 1, 2, 4)
         for g in range(PASSES):
             load_weight(w1, "w1", g, 0, 2)
@@ -221,7 +222,7 @@ def tile_picked_ytri_gated_p_kernel(
             round_columns("scalar", ("w3", 0), t * P, (t + 1) * P)
             multiply(("w3", 0), t, t + 1, 0)
         nc.vector.tensor_copy(out=x_codes[1][:], in_=x_all[1][:].indirect(offs_t[:]))
-        for t, engine in enumerate(("vector", "scalar")):
+        for t, engine in enumerate(("scalar", "vector")):
             round_columns(engine, ("w3", 1), t * P, (t + 1) * P)
             multiply(("w3", 1), t, t + 1, 0)
         round_columns("vector", ("w3", 0), 2 * P, 4 * P)
@@ -243,13 +244,14 @@ def tile_picked_ytri_gated_p_kernel(
         fetch(2, 0, scratch("picked20", V))
         fetch(2, 1, scratch("picked21", V))
         round_columns("scalar", ("w2", 0), 0, 2 * P)
-        round_columns("vector", ("w2", 1), 0, 2 * P)
+        round_columns("vector", ("w2", 1), 0, 1 * P)
+        round_columns("scalar", ("w2", 1), 1 * P, 2 * P)
         multiply(("w2", 0), 0, 2, 0)
         multiply(("w2", 1), 0, 2, 0)
-        make_gate(0, 4, raw[("w1", 0) + (0,)][0][:, 0 : 2, :].rearrange("p j c -> p (j c)"))
-        make_gate(1, 5, raw[("w1", 0) + (0,)][0][:, 2 : 4, :].rearrange("p j c -> p (j c)"))
-        fetch(3, 0, after(("w2", 0), 0, 0))
-        fetch(3, 1, after(("w2", 0), 0, 1))
+        make_gate(0, 4, raw[("w2", 0) + (0,)][0][:, 0 : 2, :].rearrange("p j c -> p (j c)"))
+        make_gate(1, 5, raw[("w2", 0) + (0,)][0][:, 2 : 4, :].rearrange("p j c -> p (j c)"))
+        fetch(3, 0, after(("w2", 1), 0, 0))
+        fetch(3, 1, after(("w2", 1), 0, 1))
         make_a(0, 0)
         make_a(1, 1)
         round_columns("scalar", ("w1", 0), 2 * P, 4 * P)

@@ -186,7 +186,7 @@ def tile_picked_ytri_gated_p_kernel(
                 out=x_all_scales[32 * q : 32 * q + 4 * PASSES, :].bitcast(I32),
                 in_=x_scales[:, 4 * q : 4 * q + 4, :].bitcast(I32),
             )
-        load_weight(w3, "w3", 0, 0, 2)
+        load_weight(w3, "w3", 0, 0, 1)
         x_all.append(load_words(1))
         warm = keep.tile([P, 1], F32, name="warm")
         nc.vector.memset(warm[:], 0.0)
@@ -195,8 +195,9 @@ def tile_picked_ytri_gated_p_kernel(
         identity = keep.tile([P, P], F32, name="identity")
         make_identity(nc, identity[:])
 
-        for t in range(2):
-            load_weight(w3, "w3", 1, t, t + 1)
+        load_weight(w3, "w3", 1, 0, 1)
+        for g in range(PASSES):
+            load_weight(w3, "w3", g, 1, 2)
         load_weight(w3, "w3", 0, 2, 4)
         nxt_t = [load_list(nxt1, "nxt1_t"), load_list(nxt2, "nxt2_t")]
         load_weight(w3, "w3", 1, 2, 4)
@@ -218,23 +219,26 @@ def tile_picked_ytri_gated_p_kernel(
         x_codes = [keep.tile([P, S], U32, name="x_codes%d" % g, align_bytes=64) for g in range(PASSES)]
         nc.vector.tensor_copy(out=x_codes[0][:], in_=x_all[0][:].indirect(offs_t[:]))
         nc.vector.tensor_copy(out=x_scale[:], in_=x_all_scales[:].indirect(offs_t[:]))
-        for t in range(2):
-            round_columns("scalar", ("w3", 0), t * P, (t + 1) * P)
-            multiply(("w3", 0), t, t + 1, 0)
+        round_columns("scalar", ("w3", 0), 0, P)
+        multiply(("w3", 0), 0, 1, 0)
         nc.vector.tensor_copy(out=x_codes[1][:], in_=x_all[1][:].indirect(offs_t[:]))
-        for t, engine in enumerate(("scalar", "vector")):
-            round_columns(engine, ("w3", 1), t * P, (t + 1) * P)
-            multiply(("w3", 1), t, t + 1, 0)
+        round_columns("scalar", ("w3", 1), 0, P)
+        multiply(("w3", 1), 0, 1, 0)
+        for g, engine in enumerate(("scalar", "vector")):
+            round_columns(engine, ("w3", g), P, 2 * P)
+        for g in range(PASSES):
+            multiply(("w3", g), 1, 2, 0)
         round_columns("vector", ("w3", 0), 2 * P, 4 * P)
         copy_e(0, 0)
         copy_e(1, 1)
         fetch(0, 0, scratch("picked00", V))
         multiply(("w3", 0), 2, 4, 0)
-        round_columns("scalar", ("w3", 1), 2 * P, 4 * P)
-        fetch(0, 1, scratch("picked01", V))
+        round_columns("vector", ("w3", 1), 2 * P, 3 * P)
+        round_columns("scalar", ("w3", 1), 3 * P, 4 * P)
         multiply(("w3", 1), 2, 4, 0)
-        fetch(1, 0, after(("w3", 1), 2, 0))
-        fetch(1, 1, after(("w3", 1), 2, 1))
+        fetch(0, 1, after(("w3", 1), 2, 0))
+        fetch(1, 0, after(("w3", 1), 2, 1))
+        fetch(1, 1, after(("w3", 1), 2, 2))
         round_columns("scalar", ("w1", 0), 0, 2 * P)
         round_columns("vector", ("w1", 1), 0, 2 * P)
         multiply(("w1", 0), 0, 2, 4)
@@ -244,13 +248,12 @@ def tile_picked_ytri_gated_p_kernel(
         fetch(2, 0, scratch("picked20", V))
         fetch(2, 1, scratch("picked21", V))
         round_columns("scalar", ("w2", 0), 0, 2 * P)
-        round_columns("vector", ("w2", 1), 0, 1 * P)
-        round_columns("scalar", ("w2", 1), 1 * P, 2 * P)
         multiply(("w2", 0), 0, 2, 0)
+        fetch(3, 0, after(("w2", 0), 0, 0))
+        round_columns("scalar", ("w2", 1), 0, 2 * P)
         multiply(("w2", 1), 0, 2, 0)
-        make_gate(0, 4, raw[("w2", 0) + (0,)][0][:, 0 : 2, :].rearrange("p j c -> p (j c)"))
-        make_gate(1, 5, raw[("w2", 0) + (0,)][0][:, 2 : 4, :].rearrange("p j c -> p (j c)"))
-        fetch(3, 0, after(("w2", 1), 0, 0))
+        make_gate(0, 4, raw[("w2", 0) + (0,)][0][:, 2 : 4, :].rearrange("p j c -> p (j c)"))
+        make_gate(1, 5, raw[("w2", 1) + (0,)][0][:, 2 : 4, :].rearrange("p j c -> p (j c)"))
         fetch(3, 1, after(("w2", 1), 0, 1))
         make_a(0, 0)
         make_a(1, 1)

@@ -60,6 +60,9 @@ def tile_picked_ytri_gated_p_kernel(
 
         def round_on(engine, src, stage):
             grouped = stage.bitcast(BF16).rearrange("p (c j) -> p c j", j=PACK)
+            if engine == "gpsimd":
+                nc.gpsimd.tensor_copy(out=grouped, in_=src.rearrange("p j c -> p c j"))
+                return
             run = 4 if engine == "vector" else 2
             dst = grouped.rearrange("p (c i) j -> p c j i", i=run)
             src = src.rearrange("p j (c i) -> p c j i", i=run)
@@ -257,8 +260,11 @@ def tile_picked_ytri_gated_p_kernel(
         fetch(3, 1, after(("w2", 1), 0, 1))
         make_a(0, 0)
         make_a(1, 1)
-        round_columns("scalar", ("w1", 0), 2 * P, 4 * P)
-        multiply(("w1", 0), 2, 4, 4)
+        place = ee[3][:, :TILE_WORDS]
+        round_on("gpsimd", raw["w1", 0, 2][0][:, :, :P], place)
+        round_columns("scalar", ("w1", 0), 3 * P, 4 * P)
+        multiply(("w1", 0), 3, 4, 4)
+        one_pass(6, quantize(place.bitcast(BF16), "w1_0_2"), 0, 0)
         fetch_times(0, 0, after(("w1", 0), 2, 0))
         round_columns("scalar", ("w1", 1), 2 * P, 4 * P)
         multiply(("w1", 1), 2, 4, 4)

@@ -243,7 +243,8 @@ def tile_picked_ytri_gated_p_kernel(
         fetch(1, 0, after(("w3", 1), 2, 1))
         fetch(1, 1, after(("w3", 1), 2, 2))
         round_columns("scalar", ("w1", 0), 0, 2 * P)
-        round_columns("vector", ("w1", 1), 0, 2 * P)
+        round_columns("vector", ("w1", 1), 0, P)
+        round_columns("scalar", ("w1", 1), P, 2 * P)
         multiply(("w1", 0), 0, 2, 4)
         multiply(("w1", 1), 0, 2, 4)
         copy_e(2, 2)
@@ -277,11 +278,13 @@ def tile_picked_ytri_gated_p_kernel(
         fetch_times(1, 1, after(("w2", 1), 2, 0))
         make_gate(2, 6, raw[("w2", 0) + (2,)][0][:, 2 : 4, :].rearrange("p j c -> p (j c)"))
         make_gate(3, 7, raw[("w2", 1) + (2,)][0][:, 2 : 4, :].rearrange("p j c -> p (j c)"))
-        w5_stage = scratch("w5_stage", PIECE_WORDS)
-        nc.scalar.copy(
-            out=w5_stage.bitcast(BF16).rearrange("p (g c i j) -> p g c j i", g=PASSES, i=2, j=PACK),
-            in_=w5_raw[:].rearrange("p g (j c i) -> p g c j i", j=PACK, i=2),
-        )
+        w5_stage = a[1][:]
+        for g, engine in enumerate(("gpsimd", "scalar")):
+            round_on(
+                engine,
+                w5_raw[:, g, :].rearrange("p (j c) -> p j c", j=PACK),
+                w5_stage[:, g * TILE_WORDS : (g + 1) * TILE_WORDS],
+            )
         make_a(2, 2)
         make_a(3, 3)
         for b in range(2):

@@ -1,7 +1,6 @@
 from contextlib import ExitStack
 
 import concourse.mybir as mybir
-from concourse.masks import make_identity
 
 K, T, S, V, H, N = 1024, 1024, 512, 256, 512, 128
 FLOPS = 2 * K * S * (3 * H + N) + 2 * H * N * V
@@ -14,14 +13,17 @@ U16 = mybir.dt.uint16
 U8 = mybir.dt.uint8
 FP8X4 = mybir.dt.float8_e4m3fn_x4
 MULT = mybir.AluOpType.mult
+ADD = mybir.AluOpType.add
 SIGMOID = mybir.ActivationFunctionType.Sigmoid
+COPY = mybir.ActivationFunctionType.Copy
 
 P = 128
 PACK = 4
 K_PASS = P * PACK
 PASSES = K // K_PASS
-TILE_WORDS = P * PACK // 2
-PIECE_WORDS = 2 * TILE_WORDS
+TILES = H // P
+TILE_COLS = P * PACK
+RUN = 4
 
 
 def tile_picked_ytri_gated_p_kernel(
@@ -38,44 +40,43 @@ def tile_picked_ytri_gated_p_kernel(
             nc.sync.dma_start(out=tile[:], in_=dram)
             return tile
 
-        raw, stage = {}, {}
-
-        def load_weight(w, name, g, t0, t1):
-            tile = keep.tile([P, PACK, (t1 - t0) * P], F32, name="%s_raw%d%d" % (name, t0, g), align_bytes=64)
-            rows = w[g * K_PASS : (g + 1) * K_PASS, :].rearrange("(p j) c -> p j c", j=PACK)
-            nc.sync.dma_start(out=tile[:], in_=rows[:, :, t0 * P : t1 * P])
-            for t in range(t0, t1):
-                raw[name, g, t] = (tile, t0 * P)
-            for h in range(t0 // 2, (t1 + 1) // 2):
-                if (name, g, h) not in stage:
-                    stage[name, g, h] = scratch("%s_stage%d%d" % (name, g, h), min(2, w.shape[1] // P) * TILE_WORDS)
-
         def load_words(g):
             tile = keep.tile([P, T], U32, name="x_all_words%d" % g, align_bytes=64)
             nc.sync.dma_start(out=tile[:].bitcast(I32), in_=x_words[g].rearrange("p n t -> p (n t)").bitcast(I32))
             return tile
 
-        def scratch(name, words):
-            return keep.tile([P, words], F32, name=name, align_bytes=64)[:]
+        raw, stage = {}, {}
 
-        def round_on(engine, src, stage):
-            grouped = stage.bitcast(BF16).rearrange("p (c j) -> p c j", j=PACK)
-            if engine == "gpsimd":
-                nc.gpsimd.tensor_copy(out=grouped, in_=src.rearrange("p j c -> p c j"))
-                return
-            run = 4 if engine == "vector" else 2
-            dst = grouped.rearrange("p (c i) j -> p c j i", i=run)
-            src = src.rearrange("p j (c i) -> p c j i", i=run)
+        def load_pass(w, name, g):
+            raw[name, g] = keep.tile([P, PACK * H], F32, name="%s_raw%d" % (name, g), align_bytes=64)
+            rows = w[g * K_PASS : (g + 1) * K_PASS, :].rearrange("(p j) c -> p (j c)", j=PACK)
+            nc.sync.dma_start(out=raw[name, g][:], in_=rows)
+            stage[name, g] = keep.tile([P, TILES * TILE_COLS], BF16, name="%s_stage%d" % (name, g), align_bytes=64)
+
+        def copy_on(engine, dst, src):
             if engine == "vector":
                 nc.vector.tensor_copy(out=dst, in_=src)
-            else:
+            elif engine == "scalar":
                 nc.scalar.copy(out=dst, in_=src)
+            else:
+                nc.gpsimd.tensor_copy(out=dst, in_=src)
 
-        def round_columns(engine, key, c0, c1):
-            tile, first = raw[key + (c0 // P,)]
-            h = c0 // (2 * P)
-            place = stage[key + (h,)][:, 2 * c0 - h * PIECE_WORDS : 2 * c1 - h * PIECE_WORDS]
-            round_on(engine, tile[:, :, c0 - first : c1 - first], place)
+        def round_tiles(engine, key, t0, t1):
+            src = raw[key][:].rearrange("p (j G t i) -> p t G j i", j=PACK, t=TILES, i=RUN)[:, t0:t1]
+            dst = stage[key][:, t0 * TILE_COLS : t1 * TILE_COLS].rearrange("p (t G i j) -> p t G j i", t=t1 - t0, i=RUN, j=PACK)
+            if t1 - t0 == 1:
+                src, dst = src[:, 0], dst[:, 0]
+            copy_on(engine, dst, src)
+
+        def round_plain(engine, src, dst):
+            if engine == "gpsimd":
+                copy_on(engine, dst.rearrange("p (c j) -> p c j", j=PACK), src.rearrange("p j c -> p c j"))
+            else:
+                copy_on(
+                    engine,
+                    dst.rearrange("p (c i j) -> p c j i", i=RUN, j=PACK),
+                    src.rearrange("p j (c i) -> p c j i", i=RUN),
+                )
 
         def quantize(values, name):
             width = values.shape[1] // PACK
@@ -97,88 +98,12 @@ def tile_picked_ytri_gated_p_kernel(
             )
 
         def multiply(key, t0, t1, first_bank):
-            values = stage[key + (t0 // 2,)][:, t0 % 2 * TILE_WORDS : ((t1 - 1) % 2 + 1) * TILE_WORDS].bitcast(BF16)
-            planes = quantize(values, "%s_%d" % key + "_%d" % t0)
+            planes = quantize(stage[key][:, t0 * TILE_COLS : t1 * TILE_COLS], "%s_%d" % key + "_%d" % t0)
             for t in range(t0, t1):
                 one_pass(first_bank + t, planes, t - t0, key[1])
 
-        def after(key, t0, row):
-            return raw[key + (t0,)][0][:, row, :V]
-
-        ee, gate, a, picked, terms = {}, {}, {}, {}, {}
-
-        def copy_e(t, bank):
-            ee[t] = keep.tile([P, S], F32, name="ee%d" % t)
-            nc.scalar.copy(out=ee[t][:], in_=banks[bank][:])
-
-        def make_gate(t, bank, place):
-            gate[t] = place
-            nc.scalar.activation(out=gate[t], in_=banks[bank][:], func=SIGMOID)
-
-        def make_a(t, bank):
-            a[t] = keep.tile([P, S], F32, name="a%d" % t)
-            nc.vector.tensor_tensor(out=a[t][:], in0=banks[bank][:], in1=gate[t], op=MULT)
-
-        def fetch(t, d, place):
-            picked[t, d] = place
-            nc.vector.tensor_copy(out=place, in_=ee[t][:].indirect(nxt_t[d][:]))
-
-        def fetch_times(t, d, place):
-            nc.vector.tensor_tensor(out=place, in0=a[t][:].indirect(pos_t[d][:]), in1=picked[t, d], op=MULT)
-            for b in range(2):
-                terms[t, d, b] = place[:, b * P : (b + 1) * P]
-
-        def fetch_times_half(t, d, b, place):
-            terms[t, d, b] = place
-            nc.vector.tensor_tensor(
-                out=place,
-                in0=a[t][:].indirect(pos_t[d][:, 8 * b : 8 * (b + 1)]),
-                in1=picked[t, d][:, b * P : (b + 1) * P],
-                op=MULT,
-            )
-
-        z_rows = [keep.tile([P, 2, P, 2], BF16, name="z_rows%d" % b) for b in range(2)]
-
-        def turn(tiles, b, bank):
-            for u, t in enumerate(tiles):
-                for d in range(2):
-                    nc.tensor.matmul(
-                        banks[bank][:, u * P : (u + 1) * P],
-                        terms[t, d, b],
-                        identity[:],
-                        start=(d == 0),
-                        stop=(d == 1),
-                        is_transpose=True,
-                    )
-            nc.scalar.copy(
-                out=z_rows[b][:, :, 32 * tiles[0] : 32 * (tiles[-1] + 1), :],
-                in_=banks[bank][:, : len(tiles) * P].rearrange("p (m e i) -> p e m i", e=2, i=2),
-            )
-
-        def finish(b, back_bank, rr_bank):
-            z_words = z_rows[b][:].rearrange("p e m i -> p (e m i)").bitcast(F32)
-            back = banks[back_bank][:, : 2 * P]
-            for e in range(2):
-                nc.tensor.transpose(back[:, e * P : (e + 1) * P], z_words[:, e * P : (e + 1) * P], identity[:])
-            z = keep.tile([P, P * PACK], BF16, name="z%d" % b, align_bytes=64)
-            nc.scalar.copy(
-                out=z[:].bitcast(F32).rearrange("p (v i e) -> p v e i", i=2, e=2),
-                in_=back.rearrange("p (e v i) -> p v e i", e=2, i=2),
-            )
-            z_codes, z_scales = quantize(z[:], "z%d" % b)
-            rr = banks[rr_bank][:, :P]
-            nc.tensor.matmul_mx(
-                out=rr,
-                lhsT=w4_planes[0][:].bitcast(FP8X4),
-                lhsT_scale=w4_planes[1][:],
-                rhs=z_codes[:].bitcast(FP8X4),
-                rhs_scale=z_scales[:],
-                start=True,
-                stop=True,
-            )
-            result = keep.tile([P, P], F32, name="result%d" % b)
-            nc.vector.tensor_tensor(out=result[:], in0=rr, in1=picked_g[:, b * P : (b + 1) * P], op=MULT)
-            nc.sync.dma_start(out=out[:, b * P : (b + 1) * P], in_=result[:])
+        def unit(tile, t, d):
+            return tile[:, (2 * t + d) * V : (2 * t + d + 1) * V]
 
         x_all_scales = keep.tile([P, T], U8, name="x_all_scales")
         nc.gpsimd.memset(x_all_scales[:].bitcast(I32), 0)
@@ -189,123 +114,145 @@ def tile_picked_ytri_gated_p_kernel(
                 out=x_all_scales[32 * q : 32 * q + 4 * PASSES, :].bitcast(I32),
                 in_=x_scales[:, 4 * q : 4 * q + 4, :].bitcast(I32),
             )
-        load_weight(w3, "w3", 0, 0, 1)
+        load_pass(w3, "w3", 0)
         x_all.append(load_words(1))
+        load_pass(w3, "w3", 1)
+        nxt_t = [load_list(nxt1, "nxt1_t"), load_list(nxt2, "nxt2_t")]
+        for g in range(PASSES):
+            load_pass(w1, "w1", g)
+        pos_t = [load_list(pos1, "pos1_t"), load_list(pos2, "pos2_t")]
+        for g in range(PASSES):
+            load_pass(w2, "w2", g)
+        w5_raw = keep.tile([P, PASSES, PACK * N], F32, name="w5_raw", align_bytes=64)
+        nc.sync.dma_start(out=w5_raw[:], in_=w5.rearrange("(g p j) c -> p g (j c)", g=PASSES, j=PACK))
+        w4_raw = keep.tile([P, TILES, N], F32, name="w4_raw", align_bytes=64)
+        w4_rows = w4.rearrange("(G t i) c -> t G i c", t=TILES, i=RUN)
+        for t in range(TILES):
+            nc.sync.dma_start(out=w4_raw[:, t, :], in_=w4_rows[t])
+        own_t = load_list(own, "own_t")
+
         warm = keep.tile([P, 1], F32, name="warm")
         nc.vector.memset(warm[:], 0.0)
         warm_out = keep.tile([P, 1], F32, name="warm_out")
         nc.scalar.activation(out=warm_out[:], in_=warm[:], func=SIGMOID)
-        identity = keep.tile([P, P], F32, name="identity")
-        make_identity(nc, identity[:])
-
-        load_weight(w3, "w3", 1, 0, 1)
-        for g in range(PASSES):
-            load_weight(w3, "w3", g, 1, 2)
-        load_weight(w3, "w3", 0, 2, 4)
-        nxt_t = [load_list(nxt1, "nxt1_t"), load_list(nxt2, "nxt2_t")]
-        load_weight(w3, "w3", 1, 2, 4)
-        for g in range(PASSES):
-            load_weight(w1, "w1", g, 0, 2)
-        for g in range(PASSES):
-            load_weight(w2, "w2", g, 0, 2)
-        pos_t = [load_list(pos1, "pos1_t"), load_list(pos2, "pos2_t")]
-        for g in range(PASSES):
-            load_weight(w1, "w1", g, 2, 4)
-        for g in range(PASSES):
-            load_weight(w2, "w2", g, 2, 4)
-        w5_raw = keep.tile([P, PASSES, PACK * N], F32, name="w5_raw", align_bytes=64)
-        nc.sync.dma_start(out=w5_raw[:], in_=w5.rearrange("(g p j) c -> p g (j c)", g=PASSES, j=PACK))
-        load_weight(w4, "w4", 0, 0, 1)
-        own_t = load_list(own, "own_t")
 
         x_scale = keep.tile([P, S], U8, name="x_scale", align_bytes=64)
         x_codes = [keep.tile([P, S], U32, name="x_codes%d" % g, align_bytes=64) for g in range(PASSES)]
         nc.vector.tensor_copy(out=x_codes[0][:], in_=x_all[0][:].indirect(offs_t[:]))
         nc.vector.tensor_copy(out=x_scale[:], in_=x_all_scales[:].indirect(offs_t[:]))
-        round_columns("scalar", ("w3", 0), 0, P)
-        multiply(("w3", 0), 0, 1, 0)
+        round_tiles("vector", ("w3", 0), 0, 2)
+        round_tiles("scalar", ("w3", 0), 2, 4)
+        multiply(("w3", 0), 0, 2, 0)
         nc.vector.tensor_copy(out=x_codes[1][:], in_=x_all[1][:].indirect(offs_t[:]))
-        round_columns("scalar", ("w3", 1), 0, P)
-        multiply(("w3", 1), 0, 1, 0)
-        for g, engine in enumerate(("scalar", "vector")):
-            round_columns(engine, ("w3", g), P, 2 * P)
-        for g in range(PASSES):
-            multiply(("w3", g), 1, 2, 0)
-        round_columns("vector", ("w3", 0), 2 * P, 4 * P)
-        copy_e(0, 0)
-        copy_e(1, 1)
-        fetch(0, 0, scratch("picked00", V))
         multiply(("w3", 0), 2, 4, 0)
-        round_columns("vector", ("w3", 1), 2 * P, 3 * P)
-        round_columns("scalar", ("w3", 1), 3 * P, 4 * P)
-        multiply(("w3", 1), 2, 4, 0)
-        fetch(0, 1, after(("w3", 1), 2, 0))
-        fetch(1, 0, after(("w3", 1), 2, 1))
-        fetch(1, 1, after(("w3", 1), 2, 2))
-        round_columns("scalar", ("w1", 0), 0, 2 * P)
-        round_columns("vector", ("w1", 1), 0, P)
-        round_columns("scalar", ("w1", 1), P, 2 * P)
-        multiply(("w1", 0), 0, 2, 4)
-        multiply(("w1", 1), 0, 2, 4)
-        copy_e(2, 2)
-        copy_e(3, 3)
-        fetch(2, 0, scratch("picked20", V))
-        fetch(2, 1, scratch("picked21", V))
-        round_columns("scalar", ("w2", 0), 0, 2 * P)
-        multiply(("w2", 0), 0, 2, 0)
-        fetch(3, 0, after(("w2", 0), 0, 0))
-        round_columns("scalar", ("w2", 1), 0, 2 * P)
-        multiply(("w2", 1), 0, 2, 0)
-        make_gate(0, 4, raw[("w2", 0) + (0,)][0][:, 2 : 4, :].rearrange("p j c -> p (j c)"))
-        make_gate(1, 5, raw[("w2", 1) + (0,)][0][:, 2 : 4, :].rearrange("p j c -> p (j c)"))
-        fetch(3, 1, after(("w2", 1), 0, 1))
-        make_a(0, 0)
-        make_a(1, 1)
-        place = ee[3][:, :TILE_WORDS]
-        round_on("gpsimd", raw["w1", 0, 2][0][:, :, :P], place)
-        round_columns("scalar", ("w1", 0), 3 * P, 4 * P)
-        multiply(("w1", 0), 3, 4, 4)
-        one_pass(6, quantize(place.bitcast(BF16), "w1_0_2"), 0, 0)
-        fetch_times(0, 0, after(("w1", 0), 2, 0))
-        round_columns("scalar", ("w1", 1), 2 * P, 4 * P)
-        multiply(("w1", 1), 2, 4, 4)
-        fetch_times(0, 1, after(("w1", 1), 2, 0))
-        round_columns("scalar", ("w2", 0), 2 * P, 4 * P)
-        multiply(("w2", 0), 2, 4, 0)
-        fetch_times(1, 0, after(("w2", 0), 2, 0))
-        round_columns("scalar", ("w2", 1), 2 * P, 4 * P)
-        multiply(("w2", 1), 2, 4, 0)
-        fetch_times(1, 1, after(("w2", 1), 2, 0))
-        make_gate(2, 6, raw[("w2", 0) + (2,)][0][:, 2 : 4, :].rearrange("p j c -> p (j c)"))
-        make_gate(3, 7, raw[("w2", 1) + (2,)][0][:, 2 : 4, :].rearrange("p j c -> p (j c)"))
-        w5_stage = a[1][:]
-        for g, engine in enumerate(("gpsimd", "scalar")):
-            round_on(
-                engine,
+        for t, engine in enumerate(("vector", "scalar", "vector", "scalar")):
+            round_tiles(engine, ("w3", 1), t, t + 1)
+        for t in range(TILES):
+            multiply(("w3", 1), t, t + 1, 0)
+        ee = [keep.tile([P, S], F32, name="ee%d" % t) for t in range(TILES)]
+        for t in range(TILES):
+            copy_on("scalar" if t else "vector", ee[t][:], banks[t][:])
+        picked_e = keep.tile([P, 2 * (TILES - 1) * V], F32, name="picked_e")
+        for t in range(TILES - 1):
+            for d in range(2):
+                nc.scalar.activation(out=unit(picked_e, t, d), in_=ee[t][:].indirect(nxt_t[d][:]), func=COPY)
+        picked_last = [raw["w1", d][:, :V] for d in range(2)]
+
+        for key, first_bank in ((("w1", 0), 4), (("w1", 1), 4), (("w2", 0), 0)):
+            for t0 in (0, 2):
+                round_tiles("vector", key, t0, t0 + 2)
+            for t0 in (0, 2):
+                multiply(key, t0, t0 + 2, first_bank)
+            if key[0] == "w1":
+                nc.vector.tensor_copy(out=picked_last[key[1]], in_=ee[TILES - 1][:].indirect(nxt_t[key[1]][:]))
+        gate = [keep.tile([P, S], F32, name="gate%d" % t) for t in range(TILES)]
+        for t in range(TILES):
+            nc.scalar.activation(out=gate[t][:], in_=banks[4 + t][:], func=SIGMOID)
+
+        last = ("w2", 1)
+        round_tiles("vector", last, 0, 1)
+        for t in range(TILES):
+            if t + 1 < TILES:
+                round_tiles("vector" if t + 2 < TILES else "scalar", last, t + 1, t + 2)
+            multiply(last, t, t + 1, 0)
+        w4_stage = stage[last][:, 3 * TILE_COLS :]
+        round_plain("gpsimd", w4_raw[:], w4_stage)
+        w5_stage = stage["w3", 0][:, : 2 * TILE_COLS]
+        for g in range(PASSES):
+            round_plain(
+                "scalar",
                 w5_raw[:, g, :].rearrange("p (j c) -> p j c", j=PACK),
-                w5_stage[:, g * TILE_WORDS : (g + 1) * TILE_WORDS],
+                w5_stage[:, g * TILE_COLS : (g + 1) * TILE_COLS],
             )
-        make_a(2, 2)
-        make_a(3, 3)
-        for b in range(2):
-            turn((0, 1), b, 6 + b)
-        w5_planes = quantize(w5_stage.bitcast(BF16), "w5")
+        a = [keep.tile([P, S], F32, name="a%d" % t) for t in range(TILES)]
+        for t in range(TILES):
+            nc.vector.tensor_tensor(out=a[t][:], in0=banks[t][:], in1=gate[t][:], op=MULT)
+        picked_a = keep.tile([P, 2 * (TILES - 1) * V], F32, name="picked_a")
+        for t in range(TILES - 1):
+            for d in range(2):
+                nc.scalar.activation(out=unit(picked_a, t, d), in_=a[t][:].indirect(pos_t[d][:]), func=COPY)
+        w5_planes = quantize(w5_stage, "w5")
         for g in range(PASSES):
             one_pass(4, w5_planes, g, g)
-        round_columns("scalar", ("w4", 0), 0, P)
-        for d in range(2):
-            fetch_times(2, d, w5_raw[:, 0, d * V : (d + 1) * V])
+
+        terms = [keep.tile([P, TILES, 2, P], F32, name="terms%d" % b) for b in range(2)]
         for b in range(2):
             for d in range(2):
-                fetch_times_half(3, d, b, w5_raw[:, 1, (2 * b + d) * P : (2 * b + d + 1) * P])
-        for b in range(2):
-            turn((2,), b, b)
+                nc.vector.tensor_tensor(
+                    out=terms[b][:, TILES - 1, d, :],
+                    in0=a[TILES - 1][:].indirect(pos_t[d][:, 8 * b : 8 * (b + 1)]),
+                    in1=picked_last[d][:, b * P : (b + 1) * P],
+                    op=MULT,
+                )
+
+        def multiply_terms(t0, t1, b):
+            def half(tile):
+                return tile[:, 2 * t0 * V : 2 * t1 * V].rearrange("p (u b v) -> p u b v", b=2, v=P)[:, :, b, :]
+
+            nc.vector.tensor_tensor(
+                out=terms[b][:, t0:t1].rearrange("p t d v -> p (t d) v"), in0=half(picked_a), in1=half(picked_e), op=MULT
+            )
+
+        z, z_planes = {}, {}
+
+        def add_terms(b):
+            z[b] = keep.tile([P, P * PACK], BF16, name="z%d" % b, align_bytes=64)
+            nc.vector.tensor_tensor(
+                out=z[b][:].rearrange("p (c i t) -> p c t i", i=2, t=TILES),
+                in0=terms[b][:, :, 0, :].rearrange("p t (c i) -> p c t i", i=2),
+                in1=terms[b][:, :, 1, :].rearrange("p t (c i) -> p c t i", i=2),
+                op=ADD,
+            )
+
+        def project(b):
+            z_codes, z_scales = quantize(z[b][:], "z%d" % b)
+            nc.tensor.matmul_mx(
+                out=banks[5 + b][:, :P],
+                lhsT=w4_planes[0][:].bitcast(FP8X4),
+                lhsT_scale=w4_planes[1][:],
+                rhs=z_codes[:].bitcast(FP8X4),
+                rhs_scale=z_scales[:],
+                start=True,
+                stop=True,
+            )
+
+        def finish(b):
+            result = keep.tile([P, P], F32, name="result%d" % b)
+            nc.vector.tensor_tensor(out=result[:], in0=banks[5 + b][:, :P], in1=picked_g[:, b * P : (b + 1) * P], op=MULT)
+            nc.sync.dma_start(out=out[:, b * P : (b + 1) * P], in_=result[:])
+
         gg = keep.tile([P, S], F32, name="gg")
         nc.scalar.activation(out=gg[:], in_=banks[4][:], func=SIGMOID)
-        for b in range(2):
-            turn((3,), b, (5, 2)[b])
-        w4_planes = quantize(stage["w4", 0, 0].bitcast(BF16), "w4")
         picked_g = keep.tile([P, V], F32, name="picked_g")
-        nc.vector.tensor_copy(out=picked_g[:], in_=gg[:].indirect(own_t[:]))
-        finish(0, 3, 6)
-        finish(1, 7, 0)
+        nc.scalar.activation(out=picked_g[:], in_=gg[:].indirect(own_t[:]), func=COPY)
+        for b in range(2):
+            multiply_terms(0, 2, b)
+        multiply_terms(2, 3, 0)
+        w4_planes = quantize(w4_stage, "w4")
+        add_terms(0)
+        multiply_terms(2, 3, 1)
+        project(0)
+        add_terms(1)
+        finish(0)
+        project(1)
+        finish(1)

@@ -120,11 +120,11 @@ def tile_picked_ytri_gated_p_kernel(
         nxt_t = [load_list(nxt1, "nxt1_t"), load_list(nxt2, "nxt2_t")]
         for g in range(PASSES):
             load_pass(w1, "w1", g)
-        pos_t = [load_list(pos1, "pos1_t"), load_list(pos2, "pos2_t")]
         for g in range(PASSES):
             load_pass(w2, "w2", g)
         w5_raw = keep.tile([P, PASSES, PACK * N], F32, name="w5_raw", align_bytes=64)
         nc.sync.dma_start(out=w5_raw[:], in_=w5.rearrange("(g p j) c -> p g (j c)", g=PASSES, j=PACK))
+        pos_t = [load_list(pos1, "pos1_t"), load_list(pos2, "pos2_t")]
         w4_raw = keep.tile([P, TILES, N], F32, name="w4_raw", align_bytes=64)
         w4_rows = w4.rearrange("(G t i) c -> t G i c", t=TILES, i=RUN)
         for t in range(TILES):
@@ -173,17 +173,17 @@ def tile_picked_ytri_gated_p_kernel(
         round_tiles("vector", last, 0, 1)
         for t in range(TILES):
             if t + 1 < TILES:
-                round_tiles("vector" if t + 2 < TILES else "scalar", last, t + 1, t + 2)
+                round_tiles("vector", last, t + 1, t + 2)
             multiply(last, t, t + 1, 0)
-        w4_stage = stage[last][:, 3 * TILE_COLS :]
-        round_plain("gpsimd", w4_raw[:], w4_stage)
-        w5_stage = stage["w3", 0][:, : 2 * TILE_COLS]
-        for g in range(PASSES):
+        w5_stage = stage[last][:, TILE_COLS : 3 * TILE_COLS]
+        for g, engine in enumerate(("scalar", "gpsimd")):
             round_plain(
-                "scalar",
+                engine,
                 w5_raw[:, g, :].rearrange("p (j c) -> p j c", j=PACK),
                 w5_stage[:, g * TILE_COLS : (g + 1) * TILE_COLS],
             )
+        w4_stage = stage[last][:, 3 * TILE_COLS :]
+        round_plain("gpsimd", w4_raw[:], w4_stage)
         a = [keep.tile([P, S], F32, name="a%d" % t) for t in range(TILES)]
         for t in range(TILES):
             nc.vector.tensor_tensor(out=a[t][:], in0=banks[t][:], in1=gate[t][:], op=MULT)

@@ -152,19 +152,19 @@ def tile_picked_ytri_gated_p_kernel(
         ee = [keep.tile([P, S], F32, name="ee%d" % t) for t in range(TILES)]
         for t in range(TILES):
             copy_on("scalar" if t else "vector", ee[t][:], banks[t][:])
-        picked_e = keep.tile([P, 2 * (TILES - 1) * V], F32, name="picked_e")
-        for t in range(TILES - 1):
-            for d in range(2):
-                nc.scalar.activation(out=unit(picked_e, t, d), in_=ee[t][:].indirect(nxt_t[d][:]), func=COPY)
-        picked_last = [raw["w1", d][:, :V] for d in range(2)]
+        units = [(t, d) for t in range(TILES) for d in range(2)]
+        picked_e = keep.tile([P, (2 * TILES - 1) * V], F32, name="picked_e")
+        for t, d in units[:-1]:
+            nc.scalar.activation(out=unit(picked_e, t, d), in_=ee[t][:].indirect(nxt_t[d][:]), func=COPY)
+        picked_last = [unit(picked_e, TILES - 1, 0), raw["w1", 0][:, :V]]
 
         for key, first_bank in ((("w1", 0), 4), (("w1", 1), 4), (("w2", 0), 0)):
             for t0 in (0, 2):
                 round_tiles("vector", key, t0, t0 + 2)
             for t0 in (0, 2):
                 multiply(key, t0, t0 + 2, first_bank)
-            if key[0] == "w1":
-                nc.vector.tensor_copy(out=picked_last[key[1]], in_=ee[TILES - 1][:].indirect(nxt_t[key[1]][:]))
+            if key == ("w1", 0):
+                nc.vector.tensor_copy(out=picked_last[1], in_=ee[TILES - 1][:].indirect(nxt_t[1][:]))
         gate = [keep.tile([P, S], F32, name="gate%d" % t) for t in range(TILES)]
         for t in range(TILES):
             nc.scalar.activation(out=gate[t][:], in_=banks[4 + t][:], func=SIGMOID)
@@ -195,36 +195,29 @@ def tile_picked_ytri_gated_p_kernel(
         for g in range(PASSES):
             one_pass(4, w5_planes, g, g)
 
-        terms = [keep.tile([P, TILES, 2, P], F32, name="terms%d" % b) for b in range(2)]
+        terms = keep.tile([P, 2 * TILES * V], F32, name="terms")
+        for d in range(2):
+            nc.vector.tensor_tensor(
+                out=unit(terms, TILES - 1, d),
+                in0=a[TILES - 1][:].indirect(pos_t[d][:]),
+                in1=picked_last[d],
+                op=MULT,
+            )
+        gg = keep.tile([P, S], F32, name="gg")
+        nc.scalar.activation(out=gg[:], in_=banks[4][:], func=SIGMOID)
+        picked_g = keep.tile([P, V], F32, name="picked_g")
+        nc.scalar.activation(out=picked_g[:], in_=gg[:].indirect(own_t[:]), func=COPY)
+        for u0, u1 in ((0, 4), (4, 5), (5, 6)):
+            cols = slice(u0 * V, u1 * V)
+            nc.vector.tensor_tensor(out=terms[:, cols], in0=picked_a[:, cols], in1=picked_e[:, cols], op=MULT)
+        w4_planes = quantize(w4_stage, "w4")
+        walk = terms[:].rearrange("p (t d b c i) -> p d b c t i", t=TILES, d=2, b=2, i=2)
+        z = [keep.tile([P, P * PACK], BF16, name="z%d" % b, align_bytes=64) for b in range(2)]
         for b in range(2):
-            for d in range(2):
-                nc.vector.tensor_tensor(
-                    out=terms[b][:, TILES - 1, d, :],
-                    in0=a[TILES - 1][:].indirect(pos_t[d][:, 8 * b : 8 * (b + 1)]),
-                    in1=picked_last[d][:, b * P : (b + 1) * P],
-                    op=MULT,
-                )
-
-        def multiply_terms(t0, t1, b):
-            def half(tile):
-                return tile[:, 2 * t0 * V : 2 * t1 * V].rearrange("p (u b v) -> p u b v", b=2, v=P)[:, :, b, :]
-
             nc.vector.tensor_tensor(
-                out=terms[b][:, t0:t1].rearrange("p t d v -> p (t d) v"), in0=half(picked_a), in1=half(picked_e), op=MULT
+                out=z[b][:].rearrange("p (c i t) -> p c t i", i=2, t=TILES), in0=walk[:, 0, b], in1=walk[:, 1, b], op=ADD
             )
-
-        z, z_planes = {}, {}
-
-        def add_terms(b):
-            z[b] = keep.tile([P, P * PACK], BF16, name="z%d" % b, align_bytes=64)
-            nc.vector.tensor_tensor(
-                out=z[b][:].rearrange("p (c i t) -> p c t i", i=2, t=TILES),
-                in0=terms[b][:, :, 0, :].rearrange("p t (c i) -> p c t i", i=2),
-                in1=terms[b][:, :, 1, :].rearrange("p t (c i) -> p c t i", i=2),
-                op=ADD,
-            )
-
-        def project(b):
+        for b in range(2):
             z_codes, z_scales = quantize(z[b][:], "z%d" % b)
             nc.tensor.matmul_mx(
                 out=banks[5 + b][:, :P],
@@ -235,24 +228,7 @@ def tile_picked_ytri_gated_p_kernel(
                 start=True,
                 stop=True,
             )
-
-        def finish(b):
+        for b in range(2):
             result = keep.tile([P, P], F32, name="result%d" % b)
             nc.vector.tensor_tensor(out=result[:], in0=banks[5 + b][:, :P], in1=picked_g[:, b * P : (b + 1) * P], op=MULT)
             nc.sync.dma_start(out=out[:, b * P : (b + 1) * P], in_=result[:])
-
-        gg = keep.tile([P, S], F32, name="gg")
-        nc.scalar.activation(out=gg[:], in_=banks[4][:], func=SIGMOID)
-        picked_g = keep.tile([P, V], F32, name="picked_g")
-        nc.scalar.activation(out=picked_g[:], in_=gg[:].indirect(own_t[:]), func=COPY)
-        for b in range(2):
-            multiply_terms(0, 2, b)
-        multiply_terms(2, 3, 0)
-        w4_planes = quantize(w4_stage, "w4")
-        add_terms(0)
-        multiply_terms(2, 3, 1)
-        project(0)
-        add_terms(1)
-        finish(0)
-        project(1)
-        finish(1)

@@ -153,18 +153,18 @@ def tile_picked_ytri_gated_p_kernel(
         for t in range(TILES):
             copy_on("scalar" if t else "vector", ee[t][:], banks[t][:])
         units = [(t, d) for t in range(TILES) for d in range(2)]
-        picked_e = keep.tile([P, (2 * TILES - 1) * V], F32, name="picked_e")
-        for t, d in units[:-1]:
+        picked_e = keep.tile([P, (2 * TILES - 2) * V], F32, name="picked_e")
+        for t, d in units[:-2]:
             nc.scalar.activation(out=unit(picked_e, t, d), in_=ee[t][:].indirect(nxt_t[d][:]), func=COPY)
-        picked_last = [unit(picked_e, TILES - 1, 0), raw["w1", 0][:, :V]]
+        picked_last = [raw["w1", d][:, :V] for d in range(2)]
 
         for key, first_bank in ((("w1", 0), 4), (("w1", 1), 4), (("w2", 0), 0)):
             for t0 in (0, 2):
                 round_tiles("vector", key, t0, t0 + 2)
             for t0 in (0, 2):
                 multiply(key, t0, t0 + 2, first_bank)
-            if key == ("w1", 0):
-                nc.vector.tensor_copy(out=picked_last[1], in_=ee[TILES - 1][:].indirect(nxt_t[1][:]))
+            if key[0] == "w1":
+                nc.vector.tensor_copy(out=picked_last[key[1]], in_=ee[TILES - 1][:].indirect(nxt_t[key[1]][:]))
         gate = [keep.tile([P, S], F32, name="gate%d" % t) for t in range(TILES)]
         for t in range(TILES):
             nc.scalar.activation(out=gate[t][:], in_=banks[4 + t][:], func=SIGMOID)
@@ -175,10 +175,10 @@ def tile_picked_ytri_gated_p_kernel(
             if t + 1 < TILES:
                 round_tiles("vector", last, t + 1, t + 2)
             multiply(last, t, t + 1, 0)
-        w5_stage = stage[last][:, TILE_COLS : 3 * TILE_COLS]
-        for g, engine in enumerate(("scalar", "gpsimd")):
+        w5_stage = stage["w3", 0][:, : 2 * TILE_COLS]
+        for g in range(PASSES):
             round_plain(
-                engine,
+                "scalar",
                 w5_raw[:, g, :].rearrange("p (j c) -> p j c", j=PACK),
                 w5_stage[:, g * TILE_COLS : (g + 1) * TILE_COLS],
             )

@@ -120,11 +120,11 @@ def tile_picked_ytri_gated_p_kernel(
         nxt_t = [load_list(nxt1, "nxt1_t"), load_list(nxt2, "nxt2_t")]
         for g in range(PASSES):
             load_pass(w1, "w1", g)
+        pos_t = [load_list(pos1, "pos1_t"), load_list(pos2, "pos2_t")]
         for g in range(PASSES):
             load_pass(w2, "w2", g)
         w5_raw = keep.tile([P, PASSES, PACK * N], F32, name="w5_raw", align_bytes=64)
         nc.sync.dma_start(out=w5_raw[:], in_=w5.rearrange("(g p j) c -> p g (j c)", g=PASSES, j=PACK))
-        pos_t = [load_list(pos1, "pos1_t"), load_list(pos2, "pos2_t")]
         w4_raw = keep.tile([P, TILES, N], F32, name="w4_raw", align_bytes=64)
         w4_rows = w4.rearrange("(G t i) c -> t G i c", t=TILES, i=RUN)
         for t in range(TILES):

@@ -140,11 +140,13 @@ def tile_picked_ytri_gated_p_kernel(
         x_codes = [keep.tile([P, S], U32, name="x_codes%d" % g, align_bytes=64) for g in range(PASSES)]
         nc.vector.tensor_copy(out=x_codes[0][:], in_=x_all[0][:].indirect(offs_t[:]))
         nc.vector.tensor_copy(out=x_scale[:], in_=x_all_scales[:].indirect(offs_t[:]))
-        round_tiles("vector", ("w3", 0), 0, 2)
-        round_tiles("scalar", ("w3", 0), 2, 4)
-        multiply(("w3", 0), 0, 2, 0)
+        round_tiles("scalar", ("w3", 0), 0, 1)
+        round_tiles("vector", ("w3", 0), 3, 4)
+        round_tiles("scalar", ("w3", 0), 1, 3)
+        multiply(("w3", 0), 0, 1, 0)
+        multiply(("w3", 0), 3, 4, 0)
         nc.vector.tensor_copy(out=x_codes[1][:], in_=x_all[1][:].indirect(offs_t[:]))
-        multiply(("w3", 0), 2, 4, 0)
+        multiply(("w3", 0), 1, 3, 0)
         for t, engine in enumerate(("vector", "scalar", "vector", "scalar")):
             round_tiles(engine, ("w3", 1), t, t + 1)
         for t in range(TILES):
@@ -153,18 +155,18 @@ def tile_picked_ytri_gated_p_kernel(
         for t in range(TILES):
             copy_on("scalar" if t else "vector", ee[t][:], banks[t][:])
         units = [(t, d) for t in range(TILES) for d in range(2)]
-        picked_e = keep.tile([P, (2 * TILES - 2) * V], F32, name="picked_e")
-        for t, d in units[:-2]:
+        picked_e = keep.tile([P, (2 * TILES - 1) * V], F32, name="picked_e")
+        for t, d in units[:-1]:
             nc.scalar.activation(out=unit(picked_e, t, d), in_=ee[t][:].indirect(nxt_t[d][:]), func=COPY)
-        picked_last = [raw["w1", d][:, :V] for d in range(2)]
+        picked_last = [unit(picked_e, TILES - 1, 0), raw["w1", 0][:, :V]]
 
         for key, first_bank in ((("w1", 0), 4), (("w1", 1), 4), (("w2", 0), 0)):
             for t0 in (0, 2):
                 round_tiles("vector", key, t0, t0 + 2)
             for t0 in (0, 2):
                 multiply(key, t0, t0 + 2, first_bank)
-            if key[0] == "w1":
-                nc.vector.tensor_copy(out=picked_last[key[1]], in_=ee[TILES - 1][:].indirect(nxt_t[key[1]][:]))
+            if key == ("w1", 0):
+                nc.vector.tensor_copy(out=picked_last[1], in_=ee[TILES - 1][:].indirect(nxt_t[1][:]))
         gate = [keep.tile([P, S], F32, name="gate%d" % t) for t in range(TILES)]
         for t in range(TILES):
             nc.scalar.activation(out=gate[t][:], in_=banks[4 + t][:], func=SIGMOID)
@@ -207,7 +209,7 @@ def tile_picked_ytri_gated_p_kernel(
         nc.scalar.activation(out=gg[:], in_=banks[4][:], func=SIGMOID)
         picked_g = keep.tile([P, V], F32, name="picked_g")
         nc.scalar.activation(out=picked_g[:], in_=gg[:].indirect(own_t[:]), func=COPY)
-        for u0, u1 in ((0, 4), (4, 5), (5, 6)):
+        for u0, u1 in ((0, 2), (2, 4), (4, 5), (5, 6)):
             cols = slice(u0 * V, u1 * V)
             nc.vector.tensor_tensor(out=terms[:, cols], in0=picked_a[:, cols], in1=picked_e[:, cols], op=MULT)
         w4_planes = quantize(w4_stage, "w4")

@@ -123,8 +123,9 @@ def tile_picked_ytri_gated_p_kernel(
         pos_t = [load_list(pos1, "pos1_t"), load_list(pos2, "pos2_t")]
         for g in range(PASSES):
             load_pass(w2, "w2", g)
-        w5_raw = keep.tile([P, PASSES, PACK * N], F32, name="w5_raw", align_bytes=64)
-        nc.sync.dma_start(out=w5_raw[:], in_=w5.rearrange("(g p j) c -> p g (j c)", g=PASSES, j=PACK))
+        w5_raw = [keep.tile([P, PACK * N], F32, name="w5_raw%d" % g, align_bytes=64) for g in range(PASSES)]
+        for g in range(PASSES):
+            nc.sync.dma_start(out=w5_raw[g][:], in_=w5.rearrange("(g p j) c -> g p (j c)", g=PASSES, j=PACK)[g])
         w4_raw = keep.tile([P, TILES, N], F32, name="w4_raw", align_bytes=64)
         w4_rows = w4.rearrange("(G t i) c -> t G i c", t=TILES, i=RUN)
         for t in range(TILES):
@@ -156,62 +157,62 @@ def tile_picked_ytri_gated_p_kernel(
             copy_on("scalar" if t else "vector", ee[t][:], banks[t][:])
         units = [(t, d) for t in range(TILES) for d in range(2)]
         picked_e = keep.tile([P, (2 * TILES - 1) * V], F32, name="picked_e")
-        for t, d in units[:-1]:
-            nc.scalar.activation(out=unit(picked_e, t, d), in_=ee[t][:].indirect(nxt_t[d][:]), func=COPY)
-        picked_last = [unit(picked_e, TILES - 1, 0), raw["w1", 0][:, :V]]
+        early = [(("w1", 0), 4), (("w1", 1), 4), (("w2", 0), 0)]
+        by_vector = dict(zip([key for key, first_bank in early], units[6:]))
+        picked = {u: unit(picked_e, *u) for u in units[:6]}
+        for t, d in picked:
+            nc.scalar.activation(out=picked[t, d], in_=ee[t][:].indirect(nxt_t[d][:]), func=COPY)
 
-        for key, first_bank in ((("w1", 0), 4), (("w1", 1), 4), (("w2", 0), 0)):
+        for key, first_bank in early:
             for t0 in (0, 2):
                 round_tiles("vector", key, t0, t0 + 2)
             for t0 in (0, 2):
                 multiply(key, t0, t0 + 2, first_bank)
-            if key == ("w1", 0):
-                nc.vector.tensor_copy(out=picked_last[1], in_=ee[TILES - 1][:].indirect(nxt_t[1][:]))
-        gate = [keep.tile([P, S], F32, name="gate%d" % t) for t in range(TILES)]
-        for t in range(TILES):
-            nc.scalar.activation(out=gate[t][:], in_=banks[4 + t][:], func=SIGMOID)
-
+            if key in by_vector:
+                t, d = by_vector[key]
+                picked[t, d] = raw[key][:, :V]
+                nc.vector.tensor_copy(out=picked[t, d], in_=ee[t][:].indirect(nxt_t[d][:]))
         last = ("w2", 1)
+        gate = [keep.tile([P, S], F32, name="gate%d" % t)[:] for t in range(TILES - 1)] + [raw[last][:, :S]]
+        for t in range(TILES - 1):
+            nc.scalar.activation(out=gate[t], in_=banks[4 + t][:], func=SIGMOID)
+
         round_tiles("vector", last, 0, 1)
         for t in range(TILES):
             if t + 1 < TILES:
-                round_tiles("vector", last, t + 1, t + 2)
+                round_tiles("vector" if t + 2 < TILES else "scalar", last, t + 1, t + 2)
             multiply(last, t, t + 1, 0)
+        nc.scalar.activation(out=gate[TILES - 1], in_=banks[4 + TILES - 1][:], func=SIGMOID)
         w5_stage = stage["w3", 0][:, : 2 * TILE_COLS]
         for g in range(PASSES):
             round_plain(
                 "scalar",
-                w5_raw[:, g, :].rearrange("p (j c) -> p j c", j=PACK),
+                w5_raw[g][:].rearrange("p (j c) -> p j c", j=PACK),
                 w5_stage[:, g * TILE_COLS : (g + 1) * TILE_COLS],
             )
         w4_stage = stage[last][:, 3 * TILE_COLS :]
         round_plain("gpsimd", w4_raw[:], w4_stage)
         a = [keep.tile([P, S], F32, name="a%d" % t) for t in range(TILES)]
         for t in range(TILES):
-            nc.vector.tensor_tensor(out=a[t][:], in0=banks[t][:], in1=gate[t][:], op=MULT)
-        picked_a = keep.tile([P, 2 * (TILES - 1) * V], F32, name="picked_a")
-        for t in range(TILES - 1):
-            for d in range(2):
-                nc.scalar.activation(out=unit(picked_a, t, d), in_=a[t][:].indirect(pos_t[d][:]), func=COPY)
+            nc.vector.tensor_tensor(out=a[t][:], in0=banks[t][:], in1=gate[t], op=MULT)
+        picked_a = keep.tile([P, 6 * V], F32, name="picked_a")
+        for t, d in units[:6]:
+            nc.scalar.activation(out=unit(picked_a, t, d), in_=a[t][:].indirect(pos_t[d][:]), func=COPY)
         w5_planes = quantize(w5_stage, "w5")
         for g in range(PASSES):
             one_pass(4, w5_planes, g, g)
 
         terms = keep.tile([P, 2 * TILES * V], F32, name="terms")
-        for d in range(2):
-            nc.vector.tensor_tensor(
-                out=unit(terms, TILES - 1, d),
-                in0=a[TILES - 1][:].indirect(pos_t[d][:]),
-                in1=picked_last[d],
-                op=MULT,
-            )
+        for t, d in units[6:]:
+            nc.vector.tensor_tensor(out=unit(terms, t, d), in0=a[t][:].indirect(pos_t[d][:]), in1=picked[t, d], op=MULT)
         gg = keep.tile([P, S], F32, name="gg")
         nc.scalar.activation(out=gg[:], in_=banks[4][:], func=SIGMOID)
         picked_g = keep.tile([P, V], F32, name="picked_g")
         nc.scalar.activation(out=picked_g[:], in_=gg[:].indirect(own_t[:]), func=COPY)
         for u0, u1 in ((0, 2), (2, 4), (4, 5), (5, 6)):
             cols = slice(u0 * V, u1 * V)
-            nc.vector.tensor_tensor(out=terms[:, cols], in0=picked_a[:, cols], in1=picked_e[:, cols], op=MULT)
+            other = picked_e[:, cols] if u1 - u0 > 1 else picked[units[u0]]
+            nc.vector.tensor_tensor(out=terms[:, cols], in0=picked_a[:, cols], in1=other, op=MULT)
         w4_planes = quantize(w4_stage, "w4")
         walk = terms[:].rearrange("p (t d b c i) -> p d b c t i", t=TILES, d=2, b=2, i=2)
         z = [keep.tile([P, P * PACK], BF16, name="z%d" % b, align_bytes=64) for b in range(2)]

@@ -196,8 +196,14 @@ def tile_picked_ytri_gated_p_kernel(
         for t in range(TILES):
             nc.vector.tensor_tensor(out=a[t][:], in0=banks[t][:], in1=gate[t], op=MULT)
         picked_a = keep.tile([P, 6 * V], F32, name="picked_a")
-        for t, d in units[:6]:
+        for t, d in units[:5]:
             nc.scalar.activation(out=unit(picked_a, t, d), in_=a[t][:].indirect(pos_t[d][:]), func=COPY)
+        for b in range(2):
+            nc.scalar.activation(
+                out=unit(picked_a, 2, 1)[:, b * P : (b + 1) * P],
+                in_=a[2][:].indirect(pos_t[1][:, 8 * b : 8 * (b + 1)]),
+                func=COPY,
+            )
         w5_planes = quantize(w5_stage, "w5")
         for g in range(PASSES):
             one_pass(4, w5_planes, g, g)
@@ -209,10 +215,9 @@ def tile_picked_ytri_gated_p_kernel(
         nc.scalar.activation(out=gg[:], in_=banks[4][:], func=SIGMOID)
         picked_g = keep.tile([P, V], F32, name="picked_g")
         nc.scalar.activation(out=picked_g[:], in_=gg[:].indirect(own_t[:]), func=COPY)
-        for u0, u1 in ((0, 2), (2, 4), (4, 5), (5, 6)):
-            cols = slice(u0 * V, u1 * V)
-            other = picked_e[:, cols] if u1 - u0 > 1 else picked[units[u0]]
-            nc.vector.tensor_tensor(out=terms[:, cols], in0=picked_a[:, cols], in1=other, op=MULT)
+        for c0, c1 in ((0, 4), (4, 8), (8, 10), (10, 11), (11, 12)):
+            cols = slice(c0 * P, c1 * P)
+            nc.vector.tensor_tensor(out=terms[:, cols], in0=picked_a[:, cols], in1=picked_e[:, cols], op=MULT)
         w4_planes = quantize(w4_stage, "w4")
         walk = terms[:].rearrange("p (t d b c i) -> p d b c t i", t=TILES, d=2, b=2, i=2)
         z = [keep.tile([P, P * PACK], BF16, name="z%d" % b, align_bytes=64) for b in range(2)]

@@ -69,14 +69,12 @@ def tile_picked_ytri_gated_p_kernel(
             copy_on(engine, dst, src)
 
         def round_plain(engine, src, dst):
-            if engine == "gpsimd":
-                copy_on(engine, dst.rearrange("p (c j) -> p c j", j=PACK), src.rearrange("p j c -> p c j"))
-            else:
-                copy_on(
-                    engine,
-                    dst.rearrange("p (c i j) -> p c j i", i=RUN, j=PACK),
-                    src.rearrange("p j (c i) -> p c j i", i=RUN),
-                )
+            run = 2 if engine == "gpsimd" else RUN
+            copy_on(
+                engine,
+                dst.rearrange("p (c i j) -> p c j i", i=run, j=PACK),
+                src.rearrange("p j (c i) -> p c j i", i=run),
+            )
 
         def quantize(values, name):
             width = values.shape[1] // PACK

from contextlib import ExitStack

import concourse.mybir as mybir

K, T, S, V, H, N = 1024, 1024, 512, 256, 512, 128
FLOPS = 2 * K * S * (3 * H + N) + 2 * H * N * V

F32 = mybir.dt.float32
BF16 = mybir.dt.bfloat16
I32 = mybir.dt.int32
U32 = mybir.dt.uint32
U16 = mybir.dt.uint16
U8 = mybir.dt.uint8
FP8X4 = mybir.dt.float8_e4m3fn_x4
MULT = mybir.AluOpType.mult
ADD = mybir.AluOpType.add
SIGMOID = mybir.ActivationFunctionType.Sigmoid
COPY = mybir.ActivationFunctionType.Copy

P = 128
PACK = 4
K_PASS = P * PACK
PASSES = K // K_PASS
TILES = H // P
TILE_COLS = P * PACK
RUN = 4


def tile_picked_ytri_gated_p_kernel(
    tc, x_words, x_scales, w1, w2, w3, w4, w5, offs, pos1, pos2, nxt1, nxt2, own, out
):
    nc = tc.nc
    with ExitStack() as ctx:
        keep = ctx.enter_context(tc.tile_pool(name="keep", bufs=1))
        psum = ctx.enter_context(tc.psum_pool(name="psum", bufs=1))
        banks = [psum.tile([P, S], F32, name="bank%d" % i) for i in range(8)]

        def load_list(dram, name):
            tile = keep.tile(list(dram.shape), U16, name=name)
            nc.sync.dma_start(out=tile[:], in_=dram)
            return tile

        def load_words(g):
            tile = keep.tile([P, T], U32, name="x_all_words%d" % g, align_bytes=64)
            nc.sync.dma_start(out=tile[:].bitcast(I32), in_=x_words[g].rearrange("p n t -> p (n t)").bitcast(I32))
            return tile

        raw, stage = {}, {}

        def load_pass(w, name, g):
            raw[name, g] = keep.tile([P, PACK * H], F32, name="%s_raw%d" % (name, g), align_bytes=64)
            rows = w[g * K_PASS : (g + 1) * K_PASS, :].rearrange("(p j) c -> p (j c)", j=PACK)
            nc.sync.dma_start(out=raw[name, g][:], in_=rows)
            stage[name, g] = keep.tile([P, TILES * TILE_COLS], BF16, name="%s_stage%d" % (name, g), align_bytes=64)

        def copy_on(engine, dst, src):
            if engine == "vector":
                nc.vector.tensor_copy(out=dst, in_=src)
            elif engine == "scalar":
                nc.scalar.copy(out=dst, in_=src)
            else:
                nc.gpsimd.tensor_copy(out=dst, in_=src)

        def round_tiles(engine, key, t0, t1):
            src = raw[key][:].rearrange("p (j G t i) -> p t G j i", j=PACK, t=TILES, i=RUN)[:, t0:t1]
            dst = stage[key][:, t0 * TILE_COLS : t1 * TILE_COLS].rearrange("p (t G i j) -> p t G j i", t=t1 - t0, i=RUN, j=PACK)
            if t1 - t0 == 1:
                src, dst = src[:, 0], dst[:, 0]
            copy_on(engine, dst, src)

        def round_plain(engine, src, dst):
            run = 2 if engine == "gpsimd" else RUN
            copy_on(
                engine,
                dst.rearrange("p (c i j) -> p c j i", i=run, j=PACK),
                src.rearrange("p j (c i) -> p c j i", i=run),
            )

        def quantize(values, name):
            width = values.shape[1] // PACK
            codes = keep.tile([P, width], U32, name=name + "_codes", align_bytes=64)
            scales = keep.tile([P, width], U8, name=name + "_scales", align_bytes=64)
            nc.vector.quantize_mx(out=codes[:].bitcast(FP8X4), scales=scales[:], in_=values)
            return codes, scales

        def one_pass(bank, planes, u, g):
            codes, scales = planes
            nc.tensor.matmul_mx(
                out=banks[bank][:],
                lhsT=codes[:, u * P : (u + 1) * P].bitcast(FP8X4),
                lhsT_scale=scales[:, u * P : (u + 1) * P],
                rhs=x_codes[g][:].bitcast(FP8X4),
                rhs_scale=x_scale[4 * g :, :],
                start=(g == 0),
                stop=(g == PASSES - 1),
            )

        def multiply(key, t0, t1, first_bank):
            planes = quantize(stage[key][:, t0 * TILE_COLS : t1 * TILE_COLS], "%s_%d" % key + "_%d" % t0)
            for t in range(t0, t1):
                one_pass(first_bank + t, planes, t - t0, key[1])

        def unit(tile, t, d):
            return tile[:, (2 * t + d) * V : (2 * t + d + 1) * V]

        x_all_scales = keep.tile([P, T], U8, name="x_all_scales")
        nc.gpsimd.memset(x_all_scales[:].bitcast(I32), 0)
        x_all = [load_words(0)]
        offs_t = load_list(offs, "offs_t")
        for q in range(4):
            nc.sync.dma_start(
                out=x_all_scales[32 * q : 32 * q + 4 * PASSES, :].bitcast(I32),
                in_=x_scales[:, 4 * q : 4 * q + 4, :].bitcast(I32),
            )
        load_pass(w3, "w3", 0)
        x_all.append(load_words(1))
        load_pass(w3, "w3", 1)
        nxt_t = [load_list(nxt1, "nxt1_t"), load_list(nxt2, "nxt2_t")]
        for g in range(PASSES):
            load_pass(w1, "w1", g)
        pos_t = [load_list(pos1, "pos1_t"), load_list(pos2, "pos2_t")]
        for g in range(PASSES):
            load_pass(w2, "w2", g)
        w5_raw = [keep.tile([P, PACK * N], F32, name="w5_raw%d" % g, align_bytes=64) for g in range(PASSES)]
        for g in range(PASSES):
            nc.sync.dma_start(out=w5_raw[g][:], in_=w5.rearrange("(g p j) c -> g p (j c)", g=PASSES, j=PACK)[g])
        w4_raw = keep.tile([P, TILES, N], F32, name="w4_raw", align_bytes=64)
        w4_rows = w4.rearrange("(G t i) c -> t G i c", t=TILES, i=RUN)
        for t in range(TILES):
            nc.sync.dma_start(out=w4_raw[:, t, :], in_=w4_rows[t])
        own_t = load_list(own, "own_t")

        warm = keep.tile([P, 1], F32, name="warm")
        nc.vector.memset(warm[:], 0.0)
        warm_out = keep.tile([P, 1], F32, name="warm_out")
        nc.scalar.activation(out=warm_out[:], in_=warm[:], func=SIGMOID)

        x_scale = keep.tile([P, S], U8, name="x_scale", align_bytes=64)
        x_codes = [keep.tile([P, S], U32, name="x_codes%d" % g, align_bytes=64) for g in range(PASSES)]
        nc.vector.tensor_copy(out=x_codes[0][:], in_=x_all[0][:].indirect(offs_t[:]))
        nc.vector.tensor_copy(out=x_scale[:], in_=x_all_scales[:].indirect(offs_t[:]))
        round_tiles("scalar", ("w3", 0), 0, 1)
        round_tiles("vector", ("w3", 0), 3, 4)
        round_tiles("scalar", ("w3", 0), 1, 3)
        multiply(("w3", 0), 0, 1, 0)
        multiply(("w3", 0), 3, 4, 0)
        nc.vector.tensor_copy(out=x_codes[1][:], in_=x_all[1][:].indirect(offs_t[:]))
        multiply(("w3", 0), 1, 3, 0)
        for t, engine in enumerate(("vector", "scalar", "vector", "scalar")):
            round_tiles(engine, ("w3", 1), t, t + 1)
        for t in range(TILES):
            multiply(("w3", 1), t, t + 1, 0)
        ee = [keep.tile([P, S], F32, name="ee%d" % t) for t in range(TILES)]
        for t in range(TILES):
            copy_on("scalar" if t else "vector", ee[t][:], banks[t][:])
        units = [(t, d) for t in range(TILES) for d in range(2)]
        picked_e = keep.tile([P, (2 * TILES - 1) * V], F32, name="picked_e")
        early = [(("w1", 0), 4), (("w1", 1), 4), (("w2", 0), 0)]
        by_vector = dict(zip([key for key, first_bank in early], units[6:]))
        picked = {u: unit(picked_e, *u) for u in units[:6]}
        for t, d in picked:
            nc.scalar.activation(out=picked[t, d], in_=ee[t][:].indirect(nxt_t[d][:]), func=COPY)

        for key, first_bank in early:
            for t0 in (0, 2):
                round_tiles("vector", key, t0, t0 + 2)
            for t0 in (0, 2):
                multiply(key, t0, t0 + 2, first_bank)
            if key in by_vector:
                t, d = by_vector[key]
                picked[t, d] = raw[key][:, :V]
                nc.vector.tensor_copy(out=picked[t, d], in_=ee[t][:].indirect(nxt_t[d][:]))
        last = ("w2", 1)
        gate = [keep.tile([P, S], F32, name="gate%d" % t)[:] for t in range(TILES - 1)] + [raw[last][:, :S]]
        for t in range(TILES - 1):
            nc.scalar.activation(out=gate[t], in_=banks[4 + t][:], func=SIGMOID)

        round_tiles("vector", last, 0, 1)
        for t in range(TILES):
            if t + 1 < TILES:
                round_tiles("vector" if t + 2 < TILES else "scalar", last, t + 1, t + 2)
            multiply(last, t, t + 1, 0)
        nc.scalar.activation(out=gate[TILES - 1], in_=banks[4 + TILES - 1][:], func=SIGMOID)
        w5_stage = stage["w3", 0][:, : 2 * TILE_COLS]
        for g in range(PASSES):
            round_plain(
                "scalar",
                w5_raw[g][:].rearrange("p (j c) -> p j c", j=PACK),
                w5_stage[:, g * TILE_COLS : (g + 1) * TILE_COLS],
            )
        w4_stage = stage[last][:, 3 * TILE_COLS :]
        round_plain("gpsimd", w4_raw[:], w4_stage)
        a = [keep.tile([P, S], F32, name="a%d" % t) for t in range(TILES)]
        for t in range(TILES):
            nc.vector.tensor_tensor(out=a[t][:], in0=banks[t][:], in1=gate[t], op=MULT)
        picked_a = keep.tile([P, 6 * V], F32, name="picked_a")
        for t, d in units[:5]:
            nc.scalar.activation(out=unit(picked_a, t, d), in_=a[t][:].indirect(pos_t[d][:]), func=COPY)
        for b in range(2):
            nc.scalar.activation(
                out=unit(picked_a, 2, 1)[:, b * P : (b + 1) * P],
                in_=a[2][:].indirect(pos_t[1][:, 8 * b : 8 * (b + 1)]),
                func=COPY,
            )
        w5_planes = quantize(w5_stage, "w5")
        for g in range(PASSES):
            one_pass(4, w5_planes, g, g)

        terms = keep.tile([P, 2 * TILES * V], F32, name="terms")
        for t, d in units[6:]:
            nc.vector.tensor_tensor(out=unit(terms, t, d), in0=a[t][:].indirect(pos_t[d][:]), in1=picked[t, d], op=MULT)
        gg = keep.tile([P, S], F32, name="gg")
        nc.scalar.activation(out=gg[:], in_=banks[4][:], func=SIGMOID)
        picked_g = keep.tile([P, V], F32, name="picked_g")
        nc.scalar.activation(out=picked_g[:], in_=gg[:].indirect(own_t[:]), func=COPY)
        for c0, c1 in ((0, 4), (4, 8), (8, 10), (10, 11), (11, 12)):
            cols = slice(c0 * P, c1 * P)
            nc.vector.tensor_tensor(out=terms[:, cols], in0=picked_a[:, cols], in1=picked_e[:, cols], op=MULT)
        w4_planes = quantize(w4_stage, "w4")
        walk = terms[:].rearrange("p (t d b c i) -> p d b c t i", t=TILES, d=2, b=2, i=2)
        z = [keep.tile([P, P * PACK], BF16, name="z%d" % b, align_bytes=64) for b in range(2)]
        for b in range(2):
            nc.vector.tensor_tensor(
                out=z[b][:].rearrange("p (c i t) -> p c t i", i=2, t=TILES), in0=walk[:, 0, b], in1=walk[:, 1, b], op=ADD
            )
        for b in range(2):
            z_codes, z_scales = quantize(z[b][:], "z%d" % b)
            nc.tensor.matmul_mx(
                out=banks[5 + b][:, :P],
                lhsT=w4_planes[0][:].bitcast(FP8X4),
                lhsT_scale=w4_planes[1][:],
                rhs=z_codes[:].bitcast(FP8X4),
                rhs_scale=z_scales[:],
                start=True,
                stop=True,
            )
        for b in range(2):
            result = keep.tile([P, P], F32, name="result%d" % b)
            nc.vector.tensor_tensor(out=result[:], in0=banks[5 + b][:, :P], in1=picked_g[:, b * P : (b + 1) * P], op=MULT)
            nc.sync.dma_start(out=out[:, b * P : (b + 1) * P], in_=result[:])
